import numpy as np
import ml_dtypes


def mxq(x, axis, fmt="e4m3"):
    dtype, down = {"e4m3": (ml_dtypes.float8_e4m3fn, 7), "e5m2": (ml_dtypes.float8_e5m2, 14)}[fmt]
    v = np.moveaxis(np.asarray(x, np.float32).astype(ml_dtypes.bfloat16).astype(np.float64), axis, -1)
    blocks = v.reshape(v.shape[:-1] + (-1, 32))
    amax = np.abs(blocks).max(-1, keepdims=True)
    byte = np.maximum(np.where(amax > 0, np.frexp(amax)[1] - 1 + 127, 0) - down, 1)
    scale = np.exp2(byte - 127.0)
    codes = (blocks / scale).astype(np.float32).astype(dtype).astype(np.float64)
    return np.moveaxis((codes * scale).reshape(v.shape), -1, axis)


WIDE = False


def mx_kscale(k):
    if not WIDE:
        return np.ones(k)
    levels = np.array([30, -30])
    if k % 512:
        return np.exp2(np.random.permutation(np.resize(levels, k // 32))).repeat(32)
    a = np.empty((k // 512, 16))
    for p in range(k // 512):
        a[p, :8] = np.random.permutation(np.resize(levels, 8))
        for g in range(8):
            far = levels[np.abs(levels - a[p, g]) >= 10]
            a[p, g + 8] = far[np.random.randint(len(far))]
    return np.exp2(a.ravel()).repeat(32)


def f64(x):
    return np.asarray(x).astype(np.float64)


def striped(idx):
    return np.tile(idx.reshape(-1, 16).T, (8, 1)).astype(np.uint16)


def unstriped(offs):
    return offs[:16].T.reshape(-1).astype(np.int64)


E2M1 = np.array([0.0, 0.5, 1.0, 1.5, 2.0, 3.0, 4.0, 6.0, -0.0, -0.5, -1.0, -1.5, -2.0, -3.0, -4.0, -6.0])


def pack_weight(w, fmt):
    k, n = w.shape
    w = f64(np.asarray(w, np.float32).astype(ml_dtypes.bfloat16)).reshape(k // 32, 32, n)
    amax = np.abs(w).max(1)
    if fmt == "e4m3":
        byte = np.frexp(amax)[1] - 1 + 127 - 7
    elif fmt == "e5m2":
        byte = np.frexp(amax)[1] - 1 + 127 - 14
    else:
        mant, ex = np.frexp(amax / 6.0)
        byte = np.where(mant > 0.5, ex, ex - 1) + 127
    byte = np.clip(np.where(amax > 0, byte, 1), 1, 254)
    scaled = (w * np.exp2(127.0 - byte)[:, None, :]).reshape(k, n).astype(np.float32)
    by_word = np.ascontiguousarray(scaled.reshape(k // 512, 128, 4, n).transpose(0, 1, 3, 2))
    if fmt == "e4m3":
        words = by_word.astype(ml_dtypes.float8_e4m3fn).view(np.uint8)
    elif fmt == "e5m2":
        words = by_word.astype(ml_dtypes.float8_e5m2).view(np.uint8)
    else:
        c = by_word.astype(ml_dtypes.float4_e2m1fn).view(np.uint8) & 0xF
        words = (c[..., 0::2] | (c[..., 1::2] << 4)).reshape(k // 512, 128, 2 * n)
    return np.ascontiguousarray(words), np.ascontiguousarray(byte.astype(np.uint8).reshape(k // 512, 16, n))


def unpack_weight(words, scales, fmt):
    g, _, n = scales.shape
    words = np.ascontiguousarray(words).reshape(g, 128, n, -1)
    if fmt == "e4m3":
        vals = words.view(ml_dtypes.float8_e4m3fn).astype(np.float64)
    elif fmt == "e5m2":
        vals = words.view(ml_dtypes.float8_e5m2).astype(np.float64)
    else:
        nib = np.empty((g, 128, n, 4), np.uint8)
        nib[..., 0::2] = words & 0xF
        nib[..., 1::2] = words >> 4
        vals = E2M1[nib]
    vals = vals * np.repeat(np.exp2(scales.astype(np.float64) - 127.0), 8, axis=1)[..., None]
    return vals.transpose(0, 1, 3, 2).reshape(g * 512, n)


def d_silu(v):
    s = 1.0 / (1.0 + np.exp(-np.maximum(v, -700.0)))
    return s * (1.0 + v * (1.0 - s))


K, T, E, C, H, N = 256, 1024, 4, 512, 512, 512


def by_expert(wq, xq):
    return np.concatenate([wq[e].T @ xq[:, e * C:(e + 1) * C] for e in range(E)], axis=1)


def setup_inputs():
    n = np.random.standard_normal
    v = mx_kscale(N)
    u = mx_kscale(H)
    first = np.random.permutation(np.repeat(np.arange(E), T // E))
    second = (first + 1 + np.random.permutation(np.repeat(np.arange(E - 1), -(-T // (E - 1)))[:T])) % E
    while np.bincount(second, minlength=E).max() != T // E:
        load = np.bincount(second, minlength=E); hi, lo = int(load.argmax()), int(load.argmin())
        t = np.flatnonzero((second == hi) & (first != lo))[0]; second[t] = lo
    slot_token = np.empty(E * C, np.int64); pos = np.empty((2, T), np.int64); fill = np.zeros(E, np.int64)
    place = np.stack([np.random.permutation(C) for _ in range(E)])
    for r, deal in enumerate((first, second)):
        for t in np.random.permutation(T):
            e = deal[t]; j = e * C + place[e, fill[e]]; fill[e] += 1; slot_token[j] = t; pos[r, t] = j
    g = np.random.uniform(0.2, 0.8, T)
    dy = pack_weight(n((N, T)) * v[:, None], "e5m2")
    w2t = [pack_weight(m, "e2m1") for m in n((E, N, H)) / np.sqrt(N) / v[None, :, None] * u]
    w1t = pack_weight(n((H, K)) / np.sqrt(H) / u[:, None], "e2m1")
    return {
        "dy_words": dy[0],
        "dy_scales": dy[1],
        "w2t_words": np.stack([m[0] for m in w2t]),
        "w2t_scales": np.stack([m[1] for m in w2t]),
        "w1t_words": w1t[0],
        "w1t_scales": w1t[1],
        "a": (n((H, T))).astype(np.float32),
        "gate": np.stack([np.tile(g, (128, 1)), np.tile(1.0 - g, (128, 1))]).astype(np.float32),
        "offs": striped(slot_token),
        "pos1": striped(pos[0]),
        "pos2": striped(pos[1]),
    }


def reference(dy_words, dy_scales, w2t_words, w2t_scales, w1t_words, w1t_scales, a, gate, offs, pos1, pos2):
    w2t = np.stack([unpack_weight(w2t_words[e], w2t_scales[e], "e2m1") for e in range(E)])
    w1t = unpack_weight(w1t_words, w1t_scales, "e2m1")
    idx = unstriped(offs)
    gq = unpack_weight(dy_words, dy_scales, "e5m2")[:, idx]
    y = by_expert(w2t, gq)
    dh = sum(f64(gate[r, :1]) * y[:, unstriped(p)] for r, p in enumerate((pos1, pos2)))
    return w1t.T @ mxq(dh * d_silu(f64(a)), 0, "e5m2")

@@ -1,0 +1,202 @@
+from contextlib import ExitStack
+
+import concourse.mybir as mybir
+from concourse.masks import make_identity
+
+K, T, E, C, H, N = 256, 1024, 4, 512, 512, 512
+FLOPS = 2 * N * H * E * C + 2 * H * K * T
+
+F32 = mybir.dt.float32
+BF16 = mybir.dt.bfloat16
+I32 = mybir.dt.int32
+U32 = mybir.dt.uint32
+U16 = mybir.dt.uint16
+U8 = mybir.dt.uint8
+E5M2 = mybir.dt.float8_e5m2_x4
+E2M1 = mybir.dt.float4_e2m1fn_x4
+ACT = mybir.ActivationFunctionType
+ALU = mybir.AluOpType
+
+P = 128
+PACK = 4
+CHUNK = 256
+HALF = 512
+PER_COL = 16
+
+
+def tile_moe_sub_silu_kernel(
+    tc, dy_words, dy_scales, w2t_words, w2t_scales, w1t_words, w1t_scales, a, gate, offs, pos1, pos2, out
+):
+    nc = tc.nc
+    chunks = T // CHUNK
+    tiles_per_chunk = CHUNK // P
+
+    with ExitStack() as ctx:
+        keep = ctx.enter_context(tc.tile_pool(name="keep", bufs=1))
+        wide = ctx.enter_context(tc.psum_pool(name="wide", bufs=4))
+        narrow = ctx.enter_context(tc.psum_pool(name="narrow", bufs=4))
+
+        slot_tokens = keep.tile([P, E * C // PER_COL], U16, name="slot_tokens")
+        token_slots = [keep.tile([P, T // PER_COL], U16, name=f"token_slots{s}") for s in range(2)]
+        dy_w = keep.tile([P, T], I32, name="dy_w", align_bytes=64)
+        dy_s = keep.tile([P, T], U8, name="dy_s", align_bytes=64)
+        w2_w = [keep.tile([P, 1, 2 * H], U8, name="w2_first", tag="first_then_a", align_bytes=64),
+                keep.tile([P, E - 1, 2 * H], U8, name="w2_rest", align_bytes=64)]
+        w2_s = keep.tile([P, E, H], U8, name="w2_s", align_bytes=64)
+        w1_w = keep.tile([P, 2 * K], U8, name="w1_w", align_bytes=64)
+        w1_s = keep.tile([P, K], U8, name="w1_s", align_bytes=64)
+        gate_rows = keep.tile([P, 2, P], F32, name="gate_rows")
+        neg_gate = keep.tile([P, 2, T // P], F32, name="neg_gate")
+        ident = keep.tile([P, P], F32, name="ident")
+        warm = keep.tile([P, 1], F32, name="warm")
+
+        nc.vector.memset(w2_s[:].bitcast(I32), 0)
+        nc.vector.memset(w1_s[:].bitcast(I32), 0)
+        nc.vector.memset(gate_rows[:], 0.0)
+        make_identity(nc, ident[:])
+        nc.scalar.activation(warm[:], ident[:, 0:1], ACT.Sigmoid)
+
+        nc.sync.dma_start(slot_tokens[:], offs)
+        nc.sync.dma_start(dy_w[:], dy_words[0].rearrange("p t d -> p (t d)").bitcast(I32))
+        for q in range(4):
+            rows = dy_scales[0, 4 * q : 4 * (q + 1), :].bitcast(I32)
+            queue = nc.sync if q == 0 else nc.scalar
+            queue.dma_start(dy_s[32 * q : 32 * (q + 1), :].bitcast(I32), rows.unsqueeze(0).to_broadcast([8, 4, T // 4]))
+        nc.sync.dma_start(w2_w[0][:].bitcast(I32), w2t_words[0:1, 0].rearrange("e p b -> p e b").bitcast(I32))
+        w2_rows = w2t_scales[:, 0].rearrange("e (q j) i -> j q e i", j=4)
+        for j in range(4):
+            nc.sync.dma_start(w2_s[j:P:32, :, :].bitcast(I32), w2_rows[j].bitcast(I32))
+        nc.sync.dma_start(w2_w[1][:].bitcast(I32), w2t_words[1:E, 0].rearrange("e p b -> p e b").bitcast(I32))
+        nc.sync.dma_start(token_slots[0][:], pos1)
+        nc.sync.dma_start(token_slots[1][:], pos2)
+        nc.sync.dma_start(gate_rows[0 : T // P, :, :], gate[:, 0, :].rearrange("s (c p) -> c s p", p=P))
+        nc.sync.dma_start(w1_w[:].bitcast(I32), w1t_words[0].bitcast(I32))
+        w1_rows = w1t_scales[0].rearrange("(q j) k -> j q k", j=4)
+        for j in range(4):
+            nc.sync.dma_start(w1_s[j:P:32, :].bitcast(I32), w1_rows[j].bitcast(I32))
+
+        y = [keep.tile([P, E * C], F32, name=f"y{r}") for r in range(H // P)]
+        for e in range(E):
+            entries = slot_tokens[:, e * C // PER_COL : (e + 1) * C // PER_COL]
+            g_w = keep.tile([P, C], U32, name=f"g_w{e}", align_bytes=64)
+            g_s = keep.tile([P, C], U8, name=f"g_s{e}", align_bytes=64)
+            nc.vector.tensor_copy(g_s[:], dy_s[:].indirect(entries))
+            nc.vector.tensor_copy(g_w[:], dy_w[:].bitcast(U32).indirect(entries))
+            words = w2_w[0][:, 0, :] if e == 0 else w2_w[1][:, e - 1, :]
+            for r in range(H // P):
+                bank = wide.tile([P, C], F32, name="bank")
+                nc.tensor.matmul_mx(
+                    bank[:],
+                    lhsT=words[:, 2 * P * r : 2 * P * (r + 1)].bitcast(E2M1),
+                    lhsT_scale=w2_s[:, e, P * r : P * (r + 1)],
+                    rhs=g_w[:].bitcast(E5M2),
+                    rhs_scale=g_s[:],
+                    start=True,
+                    stop=True,
+                )
+                if e == E - 1 and r == 0:
+                    nc.vector.tensor_copy(y[r][:, e * C : (e + 1) * C], bank[:])
+                else:
+                    nc.scalar.copy(y[r][:, e * C : (e + 1) * C], bank[:])
+
+        a_sb = keep.tile([P, PACK, T], F32, name="a_sb", tag="first_then_a", align_bytes=64)
+        nc.sync.dma_start(a_sb[:], a.rearrange("(p d) t -> p d t", d=PACK))
+
+        gate_t = narrow.tile([P, 2, P], F32, name="small")
+        for s in range(2):
+            nc.tensor.transpose(gate_t[:, s, :], gate_rows[:, s, :], ident[:])
+        nc.scalar.activation(neg_gate[:], gate_t[:, :, 0 : T // P], ACT.Copy, scale=-1.0)
+
+        sig = [keep.tile([P, CHUNK * PACK], F32, name=f"sig{c}") for c in range(chunks)]
+        sil = [keep.tile([P, CHUNK * PACK], F32, name=f"sil{c}") for c in range(chunks)]
+
+        def woven(func, dst, c, scale):
+            nc.scalar.activation(
+                dst[:].rearrange("p (g i d) -> p g d i", i=4, d=PACK),
+                a_sb[:, :, c * CHUNK : (c + 1) * CHUNK].rearrange("p d (g i) -> p g d i", i=4),
+                func,
+                scale=scale,
+            )
+
+        for c in range(chunks):
+            woven(ACT.Sigmoid, sig[c], c, 1.0)
+
+        z = {}
+        for c in range(chunks):
+            for s in range(2):
+                z[c, s] = keep.tile([P, H // P, CHUNK], F32, name=f"z{c}_{s}")
+            order = [(s, r) for s in range(2) for r in range(H // P)]
+            if c == 0:
+                order = sorted(order, key=lambda sr: sr[1])
+            for s, r in order:
+                entries = token_slots[s][:, c * CHUNK // PER_COL : (c + 1) * CHUNK // PER_COL]
+                nc.vector.tensor_copy(z[c, s][:, r, :], y[r][:].indirect(entries))
+
+        da = [keep.tile([P, HALF * PACK], BF16, name=f"da{h}", align_bytes=64) for h in range(T // HALF)]
+        da_w = [keep.tile([P, HALF], U32, name=f"da_w{h}", align_bytes=64) for h in range(T // HALF)]
+        da_s = [keep.tile([P, HALF], U8, name=f"da_s{h}", align_bytes=64) for h in range(T // HALF)]
+
+        gated = {}
+        for c in range(chunks):
+            woven(ACT.Silu, sil[c], c, -1.0)
+            for s in range(2):
+                for b in range(tiles_per_chunk):
+                    bank = wide.tile([P, H], F32, name="bank")
+                    for r in range(H // P):
+                        nc.tensor.transpose(bank[:, r * P : (r + 1) * P], z[c, s][:, r, b * P : (b + 1) * P], ident[:])
+                    tok = c * tiles_per_chunk + b
+                    gated[c, s, b] = keep.tile([P, PACK, P], F32, name=f"gated{c}_{s}_{b}")
+                    nc.scalar.activation(
+                        gated[c, s, b][:],
+                        bank[:].rearrange("t (p d) -> t d p", d=PACK),
+                        ACT.Copy,
+                        scale=neg_gate[:, s, tok : tok + 1],
+                    )
+
+        for c in range(chunks):
+            neg_ds = keep.tile([P, CHUNK * PACK], F32, name=f"neg_ds{c}")
+            nc.vector.scalar_tensor_tensor(neg_ds[:], sil[c][:], 1.0, sig[c][:], ALU.subtract, ALU.mult)
+            h, first = divmod(c * CHUNK, HALF)
+            for b in range(tiles_per_chunk):
+                neg_dh = narrow.tile([P, PACK, P], F32, name="small")
+                for d in range(PACK):
+                    for s in range(2):
+                        nc.tensor.matmul(
+                            neg_dh[:, d, :], lhsT=gated[c, s, b][:, d, :], rhs=ident[:],
+                            start=(s == 0), stop=(s == 1), is_transpose=True,
+                        )
+                lo = (first + b * P) * PACK
+                nc.vector.tensor_tensor(
+                    da[h][:, lo : lo + P * PACK].rearrange("p (t d) -> p t d", d=PACK),
+                    neg_dh[:].rearrange("p d t -> p t d"),
+                    neg_ds[:, b * P * PACK : (b + 1) * P * PACK].rearrange("p (t d) -> p t d", d=PACK),
+                    ALU.mult,
+                )
+            nc.vector.quantize_mx(
+                da_w[h][:, first : first + CHUNK].bitcast(E5M2),
+                da_s[h][:, first : first + CHUNK],
+                da[h][:, first * PACK : (first + CHUNK) * PACK],
+            )
+            if first + CHUNK == HALF:
+                for kb in range(K // P):
+                    sums = wide.tile([P, HALF], F32, name="bank")
+                    nc.tensor.matmul_mx(
+                        sums[:],
+                        lhsT=w1_w[:, 2 * P * kb : 2 * P * (kb + 1)].bitcast(E2M1),
+                        lhsT_scale=w1_s[:, P * kb : P * (kb + 1)],
+                        rhs=da_w[h][:].bitcast(E5M2),
+                        rhs_scale=da_s[h][:],
+                        start=True,
+                        stop=True,
+                    )
+                    res = keep.tile([P, HALF], F32, name=f"res{h}_{kb}")
+                    dst = out[kb * P : (kb + 1) * P, h * HALF : (h + 1) * HALF]
+                    if h == T // HALF - 1 and kb == 1:
+                        nc.vector.tensor_copy(res[:], sums[:])
+                        nc.sync.dma_start(dst, res[:])
+                    elif h == T // HALF - 1:
+                        nc.scalar.copy(res[:], sums[:])
+                        nc.scalar.dma_start(dst, res[:])
+                    else:
+                        nc.scalar.copy(res[:], sums[:])
+                        nc.sync.dma_start(dst, res[:])

@@ -33,8 +33,8 @@ def tile_moe_sub_silu_kernel(
 
     with ExitStack() as ctx:
         keep = ctx.enter_context(tc.tile_pool(name="keep", bufs=1))
-        wide = ctx.enter_context(tc.psum_pool(name="wide", bufs=4))
-        narrow = ctx.enter_context(tc.psum_pool(name="narrow", bufs=4))
+        wide = ctx.enter_context(tc.psum_pool(name="wide", bufs=3))
+        narrow = ctx.enter_context(tc.psum_pool(name="narrow", bufs=5))
 
         slot_tokens = keep.tile([P, E * C // PER_COL], U16, name="slot_tokens")
         token_slots = [keep.tile([P, T // PER_COL], U16, name=f"token_slots{s}") for s in range(2)]
@@ -56,18 +56,28 @@ def tile_moe_sub_silu_kernel(
         make_identity(nc, ident[:])
         nc.scalar.activation(warm[:], ident[:, 0:1], ACT.Sigmoid)
 
-        nc.sync.dma_start(slot_tokens[:], offs)
-        nc.sync.dma_start(dy_w[:], dy_words[0].rearrange("p t d -> p (t d)").bitcast(I32))
-        for q in range(4):
+        def load_dy_scales(queue, q):
             rows = dy_scales[0, 4 * q : 4 * (q + 1), :].bitcast(I32)
-            queue = nc.sync if q == 0 else nc.scalar
             queue.dma_start(dy_s[32 * q : 32 * (q + 1), :].bitcast(I32), rows.unsqueeze(0).to_broadcast([8, 4, T // 4]))
-        nc.sync.dma_start(w2_w[0][:].bitcast(I32), w2t_words[0:1, 0].rearrange("e p b -> p e b").bitcast(I32))
+
         w2_rows = w2t_scales[:, 0].rearrange("e (q j) i -> j q e i", j=4)
-        for j in range(4):
-            nc.sync.dma_start(w2_s[j:P:32, :, :].bitcast(I32), w2_rows[j].bitcast(I32))
-        nc.sync.dma_start(w2_w[1][:].bitcast(I32), w2t_words[1:E, 0].rearrange("e p b -> p e b").bitcast(I32))
+
+        def load_w2_scales(queue, j):
+            queue.dma_start(w2_s[j:P:32, :, :].bitcast(I32), w2_rows[j].bitcast(I32))
+
+        load_dy_scales(nc.sync, 0)
+        nc.sync.dma_start(dy_w[:], dy_words[0].rearrange("p t d -> p (t d)").bitcast(I32))
+        load_dy_scales(nc.sync, 1)
+        nc.sync.dma_start(slot_tokens[:], offs)
+        load_dy_scales(nc.scalar, 2)
+        load_dy_scales(nc.scalar, 3)
+        nc.scalar.dma_start(w2_w[0][:].bitcast(I32), w2t_words[0:1, 0].rearrange("e p b -> p e b").bitcast(I32))
+        load_w2_scales(nc.scalar, 0)
+        load_w2_scales(nc.sync, 1)
+        load_w2_scales(nc.scalar, 2)
         nc.sync.dma_start(token_slots[0][:], pos1)
+        load_w2_scales(nc.scalar, 3)
+        nc.sync.dma_start(w2_w[1][:].bitcast(I32), w2t_words[1:E, 0].rearrange("e p b -> p e b").bitcast(I32))
         nc.sync.dma_start(token_slots[1][:], pos2)
         nc.sync.dma_start(gate_rows[0 : T // P, :, :], gate[:, 0, :].rearrange("s (c p) -> c s p", p=P))
         nc.sync.dma_start(w1_w[:].bitcast(I32), w1t_words[0].bitcast(I32))
@@ -84,7 +94,7 @@ def tile_moe_sub_silu_kernel(
             nc.vector.tensor_copy(g_w[:], dy_w[:].bitcast(U32).indirect(entries))
             words = w2_w[0][:, 0, :] if e == 0 else w2_w[1][:, e - 1, :]
             for r in range(H // P):
-                bank = wide.tile([P, C], F32, name="bank")
+                bank = narrow.tile([P, C], F32, name="small")
                 nc.tensor.matmul_mx(
                     bank[:],
                     lhsT=words[:, 2 * P * r : 2 * P * (r + 1)].bitcast(E2M1),
@@ -94,7 +104,7 @@ def tile_moe_sub_silu_kernel(
                     start=True,
                     stop=True,
                 )
-                if e == E - 1 and r == 0:
+                if (e, r) in ((E - 2, H // P - 1), (E - 1, 0)):
                     nc.vector.tensor_copy(y[r][:, e * C : (e + 1) * C], bank[:])
                 else:
                     nc.scalar.copy(y[r][:, e * C : (e + 1) * C], bank[:])
@@ -122,23 +132,26 @@ def tile_moe_sub_silu_kernel(
             woven(ACT.Sigmoid, sig[c], c, 1.0)
 
         z = {}
-        for c in range(chunks):
-            for s in range(2):
-                z[c, s] = keep.tile([P, H // P, CHUNK], F32, name=f"z{c}_{s}")
+        for lo, hi in ((0, 2), (2, 3), (3, 4)):
+            width = (hi - lo) * CHUNK
+            picked = [keep.tile([P, H // P, width], F32, name=f"z{lo}_{s}") for s in range(2)]
             order = [(s, r) for s in range(2) for r in range(H // P)]
-            if c == 0:
+            if lo == 0:
                 order = sorted(order, key=lambda sr: sr[1])
             for s, r in order:
-                entries = token_slots[s][:, c * CHUNK // PER_COL : (c + 1) * CHUNK // PER_COL]
-                nc.vector.tensor_copy(z[c, s][:, r, :], y[r][:].indirect(entries))
+                entries = token_slots[s][:, lo * CHUNK // PER_COL : hi * CHUNK // PER_COL]
+                nc.vector.tensor_copy(picked[s][:, r, :], y[r][:].indirect(entries))
+            for c in range(lo, hi):
+                for s in range(2):
+                    z[c, s] = picked[s][:, :, (c - lo) * CHUNK : (c - lo + 1) * CHUNK]
 
-        da = [keep.tile([P, HALF * PACK], BF16, name=f"da{h}", align_bytes=64) for h in range(T // HALF)]
-        da_w = [keep.tile([P, HALF], U32, name=f"da_w{h}", align_bytes=64) for h in range(T // HALF)]
-        da_s = [keep.tile([P, HALF], U8, name=f"da_s{h}", align_bytes=64) for h in range(T // HALF)]
+        da = keep.tile([P, T * PACK], BF16, name="da", align_bytes=64)
+        da_w = keep.tile([P, T], U32, name="da_w", align_bytes=64)
+        da_s = keep.tile([P, T], U8, name="da_s", align_bytes=64)
 
         gated = {}
+        neg_dh = {}
         for c in range(chunks):
-            woven(ACT.Silu, sil[c], c, -1.0)
             for s in range(2):
                 for b in range(tiles_per_chunk):
                     bank = wide.tile([P, H], F32, name="bank")
@@ -147,56 +160,57 @@ def tile_moe_sub_silu_kernel(
                     tok = c * tiles_per_chunk + b
                     gated[c, s, b] = keep.tile([P, PACK, P], F32, name=f"gated{c}_{s}_{b}")
                     nc.scalar.activation(
-                        gated[c, s, b][:],
-                        bank[:].rearrange("t (p d) -> t d p", d=PACK),
+                        gated[c, s, b][:].rearrange("t d p -> t p d"),
+                        bank[:].rearrange("t (p d) -> t p d", d=PACK),
                         ACT.Copy,
                         scale=neg_gate[:, s, tok : tok + 1],
                     )
+            for b in range(tiles_per_chunk):
+                neg_dh[c, b] = narrow.tile([P, PACK, P], F32, name="small")
+                for d in range(PACK):
+                    for s in range(2):
+                        nc.tensor.matmul(
+                            neg_dh[c, b][:, d, :], lhsT=gated[c, s, b][:, d, :], rhs=ident[:],
+                            start=(s == 0), stop=(s == 1), is_transpose=True,
+                        )
+            woven(ACT.Silu, sil[c], c, -1.0)
 
         for c in range(chunks):
             neg_ds = keep.tile([P, CHUNK * PACK], F32, name=f"neg_ds{c}")
             nc.vector.scalar_tensor_tensor(neg_ds[:], sil[c][:], 1.0, sig[c][:], ALU.subtract, ALU.mult)
-            h, first = divmod(c * CHUNK, HALF)
             for b in range(tiles_per_chunk):
-                neg_dh = narrow.tile([P, PACK, P], F32, name="small")
-                for d in range(PACK):
-                    for s in range(2):
-                        nc.tensor.matmul(
-                            neg_dh[:, d, :], lhsT=gated[c, s, b][:, d, :], rhs=ident[:],
-                            start=(s == 0), stop=(s == 1), is_transpose=True,
-                        )
-                lo = (first + b * P) * PACK
+                lo = (c * CHUNK + b * P) * PACK
                 nc.vector.tensor_tensor(
-                    da[h][:, lo : lo + P * PACK].rearrange("p (t d) -> p t d", d=PACK),
-                    neg_dh[:].rearrange("p d t -> p t d"),
-                    neg_ds[:, b * P * PACK : (b + 1) * P * PACK].rearrange("p (t d) -> p t d", d=PACK),
+                    da[:, lo : lo + P * PACK].rearrange("p (g i d) -> p g d i", i=2, d=PACK),
+                    neg_dh[c, b][:].rearrange("p d (g i) -> p g d i", i=2),
+                    neg_ds[:, b * P * PACK : (b + 1) * P * PACK].rearrange("p (g i d) -> p g d i", i=2, d=PACK),
                     ALU.mult,
                 )
-            nc.vector.quantize_mx(
-                da_w[h][:, first : first + CHUNK].bitcast(E5M2),
-                da_s[h][:, first : first + CHUNK],
-                da[h][:, first * PACK : (first + CHUNK) * PACK],
-            )
-            if first + CHUNK == HALF:
-                for kb in range(K // P):
-                    sums = wide.tile([P, HALF], F32, name="bank")
-                    nc.tensor.matmul_mx(
-                        sums[:],
-                        lhsT=w1_w[:, 2 * P * kb : 2 * P * (kb + 1)].bitcast(E2M1),
-                        lhsT_scale=w1_s[:, P * kb : P * (kb + 1)],
-                        rhs=da_w[h][:].bitcast(E5M2),
-                        rhs_scale=da_s[h][:],
-                        start=True,
-                        stop=True,
-                    )
-                    res = keep.tile([P, HALF], F32, name=f"res{h}_{kb}")
-                    dst = out[kb * P : (kb + 1) * P, h * HALF : (h + 1) * HALF]
-                    if h == T // HALF - 1 and kb == 1:
-                        nc.vector.tensor_copy(res[:], sums[:])
-                        nc.sync.dma_start(dst, res[:])
-                    elif h == T // HALF - 1:
-                        nc.scalar.copy(res[:], sums[:])
-                        nc.scalar.dma_start(dst, res[:])
-                    else:
-                        nc.scalar.copy(res[:], sums[:])
-                        nc.sync.dma_start(dst, res[:])
+            if c == 0:
+                continue
+            end = (c + 1) * CHUNK
+            fresh = 0 if c == 1 else c * CHUNK
+            nc.vector.quantize_mx(da_w[:, fresh:end].bitcast(E5M2), da_s[:, fresh:end], da[:, fresh * PACK : end * PACK])
+            for kb in range(K // P):
+                sums = wide.tile([P, HALF], F32, name="bank")
+                nc.tensor.matmul_mx(
+                    sums[:],
+                    lhsT=w1_w[:, 2 * P * kb : 2 * P * (kb + 1)].bitcast(E2M1),
+                    lhsT_scale=w1_s[:, P * kb : P * (kb + 1)],
+                    rhs=da_w[:, end - HALF : end].bitcast(E5M2),
+                    rhs_scale=da_s[:, end - HALF : end],
+                    start=True,
+                    stop=True,
+                )
+                res = keep.tile([P, end - fresh], F32, name=f"res{c}_{kb}")
+                dst = out[kb * P : (kb + 1) * P, fresh:end]
+                new_sums = sums[:, fresh - (end - HALF) :]
+                if c == chunks - 1 and kb == 1:
+                    nc.vector.tensor_copy(res[:], new_sums)
+                    nc.sync.dma_start(dst, res[:])
+                elif c == chunks - 1:
+                    nc.scalar.copy(res[:], new_sums)
+                    nc.scalar.dma_start(dst, res[:])
+                else:
+                    nc.scalar.copy(res[:], new_sums)
+                    nc.sync.dma_start(dst, res[:])

@@ -19,51 +19,52 @@ ALU = mybir.AluOpType
 
 P = 128
 PACK = 4
+QUADRANT = 32
+SCALE_ROWS = 4
+PER_COL = 16
 CHUNK = 256
 HALF = 512
-PER_COL = 16
+BANKS = 8
+ROW_BLOCKS = H // P
+CHUNKS = T // CHUNK
+TILES = CHUNK // P
 
 
 def tile_moe_sub_silu_kernel(
     tc, dy_words, dy_scales, w2t_words, w2t_scales, w1t_words, w1t_scales, a, gate, offs, pos1, pos2, out
 ):
     nc = tc.nc
-    chunks = T // CHUNK
-    tiles_per_chunk = CHUNK // P
 
     with ExitStack() as ctx:
         keep = ctx.enter_context(tc.tile_pool(name="keep", bufs=1))
-        wide = ctx.enter_context(tc.psum_pool(name="wide", bufs=3))
-        narrow = ctx.enter_context(tc.psum_pool(name="narrow", bufs=5))
+        psum = ctx.enter_context(tc.psum_pool(name="psum", bufs=BANKS))
 
         slot_tokens = keep.tile([P, E * C // PER_COL], U16, name="slot_tokens")
         token_slots = [keep.tile([P, T // PER_COL], U16, name=f"token_slots{s}") for s in range(2)]
         dy_w = keep.tile([P, T], I32, name="dy_w", align_bytes=64)
         dy_s = keep.tile([P, T], U8, name="dy_s", align_bytes=64)
-        w2_w = [keep.tile([P, 1, 2 * H], U8, name="w2_first", tag="first_then_a", align_bytes=64),
-                keep.tile([P, E - 1, 2 * H], U8, name="w2_rest", align_bytes=64)]
+        w2_first = keep.tile([P, 1, 2 * H], U8, name="w2_first", align_bytes=64)
+        w2_rest = keep.tile([P, E - 1, 2 * H], U8, name="w2_rest", align_bytes=64)
         w2_s = keep.tile([P, E, H], U8, name="w2_s", align_bytes=64)
-        w1_w = keep.tile([P, 2 * K], U8, name="w1_w", align_bytes=64)
         w1_s = keep.tile([P, K], U8, name="w1_s", align_bytes=64)
-        gate_rows = keep.tile([P, 2, P], F32, name="gate_rows")
-        neg_gate = keep.tile([P, 2, T // P], F32, name="neg_gate")
+        gates = keep.tile([P, 2, T], F32, name="gates")
         ident = keep.tile([P, P], F32, name="ident")
-        warm = keep.tile([P, 1], F32, name="warm")
 
         nc.vector.memset(w2_s[:].bitcast(I32), 0)
         nc.vector.memset(w1_s[:].bitcast(I32), 0)
-        nc.vector.memset(gate_rows[:], 0.0)
         make_identity(nc, ident[:])
-        nc.scalar.activation(warm[:], ident[:, 0:1], ACT.Sigmoid)
 
         def load_dy_scales(queue, q):
-            rows = dy_scales[0, 4 * q : 4 * (q + 1), :].bitcast(I32)
-            queue.dma_start(dy_s[32 * q : 32 * (q + 1), :].bitcast(I32), rows.unsqueeze(0).to_broadcast([8, 4, T // 4]))
+            rows = dy_scales[0, SCALE_ROWS * q : SCALE_ROWS * (q + 1), :].bitcast(I32)
+            queue.dma_start(
+                dy_s[QUADRANT * q : QUADRANT * (q + 1), :].bitcast(I32),
+                rows.unsqueeze(0).to_broadcast([QUADRANT // SCALE_ROWS, SCALE_ROWS, T // 4]),
+            )
 
-        w2_rows = w2t_scales[:, 0].rearrange("e (q j) i -> j q e i", j=4)
+        w2_rows = w2t_scales[:, 0].rearrange("e (q j) i -> j q e i", j=SCALE_ROWS)
 
         def load_w2_scales(queue, j):
-            queue.dma_start(w2_s[j:P:32, :, :].bitcast(I32), w2_rows[j].bitcast(I32))
+            queue.dma_start(w2_s[j:P:QUADRANT, :, :].bitcast(I32), w2_rows[j].bitcast(I32))
 
         load_dy_scales(nc.sync, 0)
         nc.sync.dma_start(dy_w[:], dy_words[0].rearrange("p t d -> p (t d)").bitcast(I32))
@@ -71,32 +72,36 @@ def tile_moe_sub_silu_kernel(
         nc.sync.dma_start(slot_tokens[:], offs)
         load_dy_scales(nc.scalar, 2)
         load_dy_scales(nc.scalar, 3)
-        nc.scalar.dma_start(w2_w[0][:].bitcast(I32), w2t_words[0:1, 0].rearrange("e p b -> p e b").bitcast(I32))
+        nc.scalar.dma_start(w2_first[:].bitcast(I32), w2t_words[0:1, 0].rearrange("e p b -> p e b").bitcast(I32))
         load_w2_scales(nc.scalar, 0)
         load_w2_scales(nc.sync, 1)
         load_w2_scales(nc.scalar, 2)
         nc.sync.dma_start(token_slots[0][:], pos1)
         load_w2_scales(nc.scalar, 3)
-        nc.sync.dma_start(w2_w[1][:].bitcast(I32), w2t_words[1:E, 0].rearrange("e p b -> p e b").bitcast(I32))
+        nc.sync.dma_start(w2_rest[:].bitcast(I32), w2t_words[1:E, 0].rearrange("e p b -> p e b").bitcast(I32))
         nc.sync.dma_start(token_slots[1][:], pos2)
-        nc.sync.dma_start(gate_rows[0 : T // P, :, :], gate[:, 0, :].rearrange("s (c p) -> c s p", p=P))
+        nc.sync.dma_start(gates[:], gate.rearrange("s p t -> p s t"))
+        a_sb = keep.tile([P, ROW_BLOCKS, T], F32, name="a_sb")
+        nc.sync.dma_start(a_sb[:], a.rearrange("(r q) t -> q r t", q=P))
+        w1_w = keep.tile([P, 2 * K], U8, name="w1_w", align_bytes=64)
         nc.sync.dma_start(w1_w[:].bitcast(I32), w1t_words[0].bitcast(I32))
-        w1_rows = w1t_scales[0].rearrange("(q j) k -> j q k", j=4)
-        for j in range(4):
-            nc.sync.dma_start(w1_s[j:P:32, :].bitcast(I32), w1_rows[j].bitcast(I32))
+        w1_rows = w1t_scales[0].rearrange("(q j) k -> j q k", j=SCALE_ROWS)
+        for j in range(SCALE_ROWS):
+            nc.sync.dma_start(w1_s[j:P:QUADRANT, :].bitcast(I32), w1_rows[j].bitcast(I32))
 
-        y = [keep.tile([P, E * C], F32, name=f"y{r}") for r in range(H // P)]
+        y = [keep.tile([P, E * C], F32, name=f"y{r}") for r in range(ROW_BLOCKS)]
+        emptied_by_vector = ((E - 2, ROW_BLOCKS - 1), (E - 1, 0))
         for e in range(E):
             entries = slot_tokens[:, e * C // PER_COL : (e + 1) * C // PER_COL]
             g_w = keep.tile([P, C], U32, name=f"g_w{e}", align_bytes=64)
             g_s = keep.tile([P, C], U8, name=f"g_s{e}", align_bytes=64)
             nc.vector.tensor_copy(g_s[:], dy_s[:].indirect(entries))
             nc.vector.tensor_copy(g_w[:], dy_w[:].bitcast(U32).indirect(entries))
-            words = w2_w[0][:, 0, :] if e == 0 else w2_w[1][:, e - 1, :]
-            for r in range(H // P):
-                bank = narrow.tile([P, C], F32, name="small")
+            words = w2_first[:, 0, :] if e == 0 else w2_rest[:, e - 1, :]
+            for r in range(ROW_BLOCKS):
+                y_sums = psum.tile([P, C], F32, name="bank")
                 nc.tensor.matmul_mx(
-                    bank[:],
+                    y_sums[:],
                     lhsT=words[:, 2 * P * r : 2 * P * (r + 1)].bitcast(E2M1),
                     lhsT_scale=w2_s[:, e, P * r : P * (r + 1)],
                     rhs=g_w[:].bitcast(E5M2),
@@ -104,113 +109,94 @@ def tile_moe_sub_silu_kernel(
                     start=True,
                     stop=True,
                 )
-                if (e, r) in ((E - 2, H // P - 1), (E - 1, 0)):
-                    nc.vector.tensor_copy(y[r][:, e * C : (e + 1) * C], bank[:])
+                if (e, r) in emptied_by_vector:
+                    nc.vector.tensor_copy(y[r][:, e * C : (e + 1) * C], y_sums[:])
                 else:
-                    nc.scalar.copy(y[r][:, e * C : (e + 1) * C], bank[:])
+                    nc.scalar.copy(y[r][:, e * C : (e + 1) * C], y_sums[:])
 
-        a_sb = keep.tile([P, PACK, T], F32, name="a_sb", tag="first_then_a", align_bytes=64)
-        nc.sync.dma_start(a_sb[:], a.rearrange("(p d) t -> p d t", d=PACK))
+        sig = [keep.tile([P, TILES, H], F32, name=f"sig{c}") for c in range(CHUNKS)]
+        a_t = [keep.tile([P, TILES, H], F32, name=f"a_t{c}") for c in range(CHUNKS)]
+        sil = [keep.tile([P, TILES, H], F32, name=f"sil{c}") for c in range(CHUNKS)]
+        for c in range(CHUNKS):
+            for b in range(TILES):
+                first = c * CHUNK + b * P
+                a_turned = psum.tile([P, H], F32, name="bank")
+                for r in range(ROW_BLOCKS):
+                    nc.tensor.transpose(a_turned[:, r * P : (r + 1) * P], a_sb[:, r, first : first + P], ident[:])
+                nc.scalar.activation(sig[c][:, b, :], a_turned[:], ACT.Sigmoid)
+                nc.scalar.copy(a_t[c][:, b, :], a_turned[:])
+        for c in range(CHUNKS):
+            nc.scalar.activation(sil[c][:], a_t[c][:], ACT.Silu, scale=-1.0)
 
-        gate_t = narrow.tile([P, 2, P], F32, name="small")
-        for s in range(2):
-            nc.tensor.transpose(gate_t[:, s, :], gate_rows[:, s, :], ident[:])
-        nc.scalar.activation(neg_gate[:], gate_t[:, :, 0 : T // P], ACT.Copy, scale=-1.0)
-
-        sig = [keep.tile([P, CHUNK * PACK], F32, name=f"sig{c}") for c in range(chunks)]
-        sil = [keep.tile([P, CHUNK * PACK], F32, name=f"sil{c}") for c in range(chunks)]
-
-        def woven(func, dst, c, scale):
-            nc.scalar.activation(
-                dst[:].rearrange("p (g i d) -> p g d i", i=4, d=PACK),
-                a_sb[:, :, c * CHUNK : (c + 1) * CHUNK].rearrange("p d (g i) -> p g d i", i=4),
-                func,
-                scale=scale,
-            )
-
-        for c in range(chunks):
-            woven(ACT.Sigmoid, sig[c], c, 1.0)
-
-        z = {}
-        for lo, hi in ((0, 2), (2, 3), (3, 4)):
-            width = (hi - lo) * CHUNK
-            picked = [keep.tile([P, H // P, width], F32, name=f"z{lo}_{s}") for s in range(2)]
-            order = [(s, r) for s in range(2) for r in range(H // P)]
-            if lo == 0:
-                order = sorted(order, key=lambda sr: sr[1])
-            for s, r in order:
-                entries = token_slots[s][:, lo * CHUNK // PER_COL : hi * CHUNK // PER_COL]
-                nc.vector.tensor_copy(picked[s][:, r, :], y[r][:].indirect(entries))
-            for c in range(lo, hi):
+        dh_t = {}
+        for c in range(CHUNKS):
+            tokens = slice(c * CHUNK, (c + 1) * CHUNK)
+            gated = [keep.tile([P, ROW_BLOCKS, CHUNK], F32, name=f"gated{c}_{s}") for s in range(2)]
+            for b in range(TILES):
+                dh_t[c, b] = psum.tile([P, H], F32, name="bank")
+            for r in range(ROW_BLOCKS):
                 for s in range(2):
-                    z[c, s] = picked[s][:, :, (c - lo) * CHUNK : (c - lo + 1) * CHUNK]
-
-        da = keep.tile([P, T * PACK], BF16, name="da", align_bytes=64)
-        da_w = keep.tile([P, T], U32, name="da_w", align_bytes=64)
-        da_s = keep.tile([P, T], U8, name="da_s", align_bytes=64)
-
-        gated = {}
-        neg_dh = {}
-        for c in range(chunks):
-            for s in range(2):
-                for b in range(tiles_per_chunk):
-                    bank = wide.tile([P, H], F32, name="bank")
-                    for r in range(H // P):
-                        nc.tensor.transpose(bank[:, r * P : (r + 1) * P], z[c, s][:, r, b * P : (b + 1) * P], ident[:])
-                    tok = c * tiles_per_chunk + b
-                    gated[c, s, b] = keep.tile([P, PACK, P], F32, name=f"gated{c}_{s}_{b}")
-                    nc.scalar.activation(
-                        gated[c, s, b][:].rearrange("t d p -> t p d"),
-                        bank[:].rearrange("t (p d) -> t p d", d=PACK),
-                        ACT.Copy,
-                        scale=neg_gate[:, s, tok : tok + 1],
-                    )
-            for b in range(tiles_per_chunk):
-                neg_dh[c, b] = narrow.tile([P, PACK, P], F32, name="small")
-                for d in range(PACK):
+                    entries = token_slots[s][:, c * CHUNK // PER_COL : (c + 1) * CHUNK // PER_COL]
+                    nc.vector.tensor_tensor(gated[s][:, r, :], y[r][:].indirect(entries), gates[:, s, tokens], ALU.mult)
+                for b in range(TILES):
                     for s in range(2):
                         nc.tensor.matmul(
-                            neg_dh[c, b][:, d, :], lhsT=gated[c, s, b][:, d, :], rhs=ident[:],
-                            start=(s == 0), stop=(s == 1), is_transpose=True,
+                            dh_t[c, b][:, r * P : (r + 1) * P],
+                            lhsT=gated[s][:, r, b * P : (b + 1) * P],
+                            rhs=ident[:],
+                            start=(s == 0),
+                            stop=(s == 1),
+                            is_transpose=True,
                         )
-            woven(ACT.Silu, sil[c], c, -1.0)
 
-        for c in range(chunks):
-            neg_ds = keep.tile([P, CHUNK * PACK], F32, name=f"neg_ds{c}")
-            nc.vector.scalar_tensor_tensor(neg_ds[:], sil[c][:], 1.0, sig[c][:], ALU.subtract, ALU.mult)
-            for b in range(tiles_per_chunk):
-                lo = (c * CHUNK + b * P) * PACK
-                nc.vector.tensor_tensor(
-                    da[:, lo : lo + P * PACK].rearrange("p (g i d) -> p g d i", i=2, d=PACK),
-                    neg_dh[c, b][:].rearrange("p d (g i) -> p g d i", i=2),
-                    neg_ds[:, b * P * PACK : (b + 1) * P * PACK].rearrange("p (g i d) -> p g d i", i=2, d=PACK),
-                    ALU.mult,
-                )
-            if c == 0:
-                continue
+        da_w = keep.tile([P, T], U32, name="da_w", align_bytes=64)
+        da_s = keep.tile([P, T], U8, name="da_s", align_bytes=64)
+        for c in range(CHUNKS):
+            last = c == CHUNKS - 1
             end = (c + 1) * CHUNK
-            fresh = 0 if c == 1 else c * CHUNK
-            nc.vector.quantize_mx(da_w[:, fresh:end].bitcast(E5M2), da_s[:, fresh:end], da[:, fresh * PACK : end * PACK])
-            for kb in range(K // P):
-                sums = wide.tile([P, HALF], F32, name="bank")
-                nc.tensor.matmul_mx(
-                    sums[:],
-                    lhsT=w1_w[:, 2 * P * kb : 2 * P * (kb + 1)].bitcast(E2M1),
-                    lhsT_scale=w1_s[:, P * kb : P * (kb + 1)],
-                    rhs=da_w[:, end - HALF : end].bitcast(E5M2),
-                    rhs_scale=da_s[:, end - HALF : end],
-                    start=True,
-                    stop=True,
+            in_first_half = end <= HALF
+            fresh = 0 if in_first_half else c * CHUNK
+            if fresh == c * CHUNK:
+                da = keep.tile([P, (HALF if in_first_half else CHUNK) * PACK], BF16, name=f"da{c}", align_bytes=64)
+            neg_ds = keep.tile([P, TILES, H], F32, name=f"neg_ds{c}")
+            nc.vector.scalar_tensor_tensor(neg_ds[:], sil[c][:], 1.0, sig[c][:], ALU.subtract, ALU.mult)
+            per_bank = 1 if last else TILES
+            for b0 in range(0, TILES, per_bank):
+                turned = psum.tile([P, per_bank, 2, P], F32, name="bank")
+                for b in range(b0, b0 + per_bank):
+                    da_t = keep.tile([P, H], BF16, name=f"da_t{c}_{b}")
+                    nc.vector.scalar_tensor_tensor(da_t[:], dh_t[c, b][:], -1.0, neg_ds[:, b, :], ALU.mult, ALU.mult)
+                    pairs = da_t[:].bitcast(F32)
+                    for u in range(2):
+                        nc.tensor.transpose(turned[:, b - b0, u, :], pairs[:, u : H // 2 : 2], ident[:])
+                first_word = (c * CHUNK + b0 * P - fresh) * 2
+                da_pairs = da[:].bitcast(F32)[:, first_word : first_word + 2 * P * per_bank]
+                nc.scalar.copy(
+                    da_pairs.rearrange("p (b t u) -> p b t u", t=P, u=2),
+                    turned[:].rearrange("p b u t -> p b t u"),
                 )
-                res = keep.tile([P, end - fresh], F32, name=f"res{c}_{kb}")
-                dst = out[kb * P : (kb + 1) * P, fresh:end]
-                new_sums = sums[:, fresh - (end - HALF) :]
-                if c == chunks - 1 and kb == 1:
-                    nc.vector.tensor_copy(res[:], new_sums)
-                    nc.sync.dma_start(dst, res[:])
-                elif c == chunks - 1:
-                    nc.scalar.copy(res[:], new_sums)
-                    nc.scalar.dma_start(dst, res[:])
-                else:
-                    nc.scalar.copy(res[:], new_sums)
-                    nc.sync.dma_start(dst, res[:])
+            if end >= HALF:
+                nc.vector.quantize_mx(da_w[:, fresh:end].bitcast(E5M2), da_s[:, fresh:end], da[:])
+            if end % HALF == 0:
+                for kb in range(K // P):
+                    sums = psum.tile([P, HALF], F32, name="bank")
+                    nc.tensor.matmul_mx(
+                        sums[:],
+                        lhsT=w1_w[:, 2 * P * kb : 2 * P * (kb + 1)].bitcast(E2M1),
+                        lhsT_scale=w1_s[:, P * kb : P * (kb + 1)],
+                        rhs=da_w[:, end - HALF : end].bitcast(E5M2),
+                        rhs_scale=da_s[:, end - HALF : end],
+                        start=True,
+                        stop=True,
+                    )
+                    res = keep.tile([P, HALF], F32, name=f"res{c}_{kb}")
+                    dst = out[kb * P : (kb + 1) * P, end - HALF : end]
+                    if last and kb == 1:
+                        nc.vector.tensor_copy(res[:], sums[:])
+                        nc.sync.dma_start(dst, res[:])
+                    elif last:
+                        nc.scalar.copy(res[:], sums[:])
+                        nc.scalar.dma_start(dst, res[:])
+                    else:
+                        nc.scalar.copy(res[:], sums[:])
+                        nc.sync.dma_start(dst, res[:])

@@ -37,7 +37,11 @@ def tile_moe_sub_silu_kernel(
 
     with ExitStack() as ctx:
         keep = ctx.enter_context(tc.tile_pool(name="keep", bufs=1))
-        psum = ctx.enter_context(tc.psum_pool(name="psum", bufs=BANKS))
+        ring = ctx.enter_context(tc.tile_pool(name="ring", bufs=4))
+        psum = ctx.enter_context(tc.psum_pool(name="psum", bufs=1))
+
+        def bank(place, shape):
+            return psum.tile(shape, F32, name=f"bank{place % BANKS}")
 
         slot_tokens = keep.tile([P, E * C // PER_COL], U16, name="slot_tokens")
         token_slots = [keep.tile([P, T // PER_COL], U16, name=f"token_slots{s}") for s in range(2)]
@@ -47,7 +51,9 @@ def tile_moe_sub_silu_kernel(
         w2_rest = keep.tile([P, E - 1, 2 * H], U8, name="w2_rest", align_bytes=64)
         w2_s = keep.tile([P, E, H], U8, name="w2_s", align_bytes=64)
         w1_s = keep.tile([P, K], U8, name="w1_s", align_bytes=64)
-        gates = keep.tile([P, 2, T], F32, name="gates")
+        w1_w = keep.tile([P, 2 * K], U8, name="w1_w", align_bytes=64)
+        gates = [keep.tile([P, T], F32, name=f"gates{s}") for s in range(2)]
+        a_sb = [keep.tile([P, ROW_BLOCKS, CHUNK], F32, name=f"a_sb{c}") for c in range(CHUNKS)]
         ident = keep.tile([P, P], F32, name="ident")
 
         nc.vector.memset(w2_s[:].bitcast(I32), 0)
@@ -62,50 +68,81 @@ def tile_moe_sub_silu_kernel(
             )
 
         w2_rows = w2t_scales[:, 0].rearrange("e (q j) i -> j q e i", j=SCALE_ROWS)
+        w1_rows = w1t_scales[0].rearrange("(q j) k -> j q k", j=SCALE_ROWS)
+        a_rows = a.rearrange("(r q) t -> q r t", q=P)
 
-        def load_w2_scales(queue, j):
-            queue.dma_start(w2_s[j:P:QUADRANT, :, :].bitcast(I32), w2_rows[j].bitcast(I32))
+        def load_a(c):
+            nc.sync.dma_start(a_sb[c][:], a_rows[:, :, c * CHUNK : (c + 1) * CHUNK])
 
-        load_dy_scales(nc.sync, 0)
-        nc.sync.dma_start(dy_w[:], dy_words[0].rearrange("p t d -> p (t d)").bitcast(I32))
-        load_dy_scales(nc.sync, 1)
         nc.sync.dma_start(slot_tokens[:], offs)
+        load_dy_scales(nc.sync, 0)
+        load_dy_scales(nc.sync, 1)
         load_dy_scales(nc.scalar, 2)
         load_dy_scales(nc.scalar, 3)
-        nc.scalar.dma_start(w2_first[:].bitcast(I32), w2t_words[0:1, 0].rearrange("e p b -> p e b").bitcast(I32))
-        load_w2_scales(nc.scalar, 0)
-        load_w2_scales(nc.sync, 1)
-        load_w2_scales(nc.scalar, 2)
-        nc.sync.dma_start(token_slots[0][:], pos1)
-        load_w2_scales(nc.scalar, 3)
+        load_a(2)
+        nc.sync.dma_start(dy_w[:], dy_words[0].rearrange("p t d -> p (t d)").bitcast(I32))
+        nc.sync.dma_start(w2_first[:].bitcast(I32), w2t_words[0:1, 0].rearrange("e p b -> p e b").bitcast(I32))
+        for j in range(SCALE_ROWS):
+            nc.sync.dma_start(w2_s[j:P:QUADRANT, :, :].bitcast(I32), w2_rows[j].bitcast(I32))
+        load_a(3)
         nc.sync.dma_start(w2_rest[:].bitcast(I32), w2t_words[1:E, 0].rearrange("e p b -> p e b").bitcast(I32))
-        nc.sync.dma_start(token_slots[1][:], pos2)
-        nc.sync.dma_start(gates[:], gate.rearrange("s p t -> p s t"))
-        a_sb = keep.tile([P, ROW_BLOCKS, T], F32, name="a_sb")
-        nc.sync.dma_start(a_sb[:], a.rearrange("(r q) t -> q r t", q=P))
-        w1_w = keep.tile([P, 2 * K], U8, name="w1_w", align_bytes=64)
+        load_a(0)
+        load_a(1)
+        for s, lst in enumerate((pos1, pos2)):
+            nc.sync.dma_start(token_slots[s][:], lst)
+        for s in range(2):
+            nc.sync.dma_start(gates[s][:], gate[s])
         nc.sync.dma_start(w1_w[:].bitcast(I32), w1t_words[0].bitcast(I32))
-        w1_rows = w1t_scales[0].rearrange("(q j) k -> j q k", j=SCALE_ROWS)
         for j in range(SCALE_ROWS):
             nc.sync.dma_start(w1_s[j:P:QUADRANT, :].bitcast(I32), w1_rows[j].bitcast(I32))
 
+        def block_columns(tile, r):
+            return tile[:].rearrange("t (u r q d) -> t r q u d", u=2, r=ROW_BLOCKS, d=2)[:, r]
+
+        def turn_a(c, b, a_turned):
+            for r in range(ROW_BLOCKS):
+                nc.tensor.transpose(block_columns(a_turned, r), a_sb[c][:, r, b * P : (b + 1) * P], ident[:])
+            return a_turned
+
+        sig = [keep.tile([P, TILES, H], F32, name=f"sig{c}") for c in range(CHUNKS)]
+        held = {}
+
+        def sigmoid(c, first_bank):
+            for b in range(TILES):
+                held[c, b] = turn_a(c, b, bank(first_bank + b, [P, H]))
+                nc.scalar.activation(sig[c][:, b, :], held[c, b][:], ACT.Sigmoid)
+
+        sigmoid(2, 0)
+
         y = [keep.tile([P, E * C], F32, name=f"y{r}") for r in range(ROW_BLOCKS)]
-        emptied_by_vector = ((E - 2, ROW_BLOCKS - 1), (E - 1, 0))
+        emptied_by_vector = ((3, 0), (3, 1), (3, 2), (3, 3))
+        g_s = {}
+        g_w = [keep.tile([P, C], U32, name=f"g_w{e}", align_bytes=64) for e in range(E)]
+
+        def expert_entries(e):
+            return slot_tokens[:, e * C // PER_COL : (e + 1) * C // PER_COL]
+
+        def gather_bytes(e):
+            g_s[e] = keep.tile([P, C], U8, name=f"g_s{e % 2}", align_bytes=64)
+            nc.vector.tensor_copy(g_s[e][:], dy_s[:].indirect(expert_entries(e)))
+
+        def gather_words(e):
+            nc.vector.tensor_copy(g_w[e][:], dy_w[:].bitcast(U32).indirect(expert_entries(e)))
+
         for e in range(E):
-            entries = slot_tokens[:, e * C // PER_COL : (e + 1) * C // PER_COL]
-            g_w = keep.tile([P, C], U32, name=f"g_w{e}", align_bytes=64)
-            g_s = keep.tile([P, C], U8, name=f"g_s{e}", align_bytes=64)
-            nc.vector.tensor_copy(g_s[:], dy_s[:].indirect(entries))
-            nc.vector.tensor_copy(g_w[:], dy_w[:].bitcast(U32).indirect(entries))
+            gather_bytes(e)
+            gather_words(e)
+            if e == 1:
+                sigmoid(3, 6)
             words = w2_first[:, 0, :] if e == 0 else w2_rest[:, e - 1, :]
             for r in range(ROW_BLOCKS):
-                y_sums = psum.tile([P, C], F32, name="bank")
+                y_sums = bank((2, 0, 4, 0)[e] + r, [P, C])
                 nc.tensor.matmul_mx(
                     y_sums[:],
                     lhsT=words[:, 2 * P * r : 2 * P * (r + 1)].bitcast(E2M1),
                     lhsT_scale=w2_s[:, e, P * r : P * (r + 1)],
-                    rhs=g_w[:].bitcast(E5M2),
-                    rhs_scale=g_s[:],
+                    rhs=g_w[e][:].bitcast(E5M2),
+                    rhs_scale=g_s[e][:],
                     start=True,
                     stop=True,
                 )
@@ -114,89 +151,115 @@ def tile_moe_sub_silu_kernel(
                 else:
                     nc.scalar.copy(y[r][:, e * C : (e + 1) * C], y_sums[:])
 
-        sig = [keep.tile([P, TILES, H], F32, name=f"sig{c}") for c in range(CHUNKS)]
-        a_t = [keep.tile([P, TILES, H], F32, name=f"a_t{c}") for c in range(CHUNKS)]
-        sil = [keep.tile([P, TILES, H], F32, name=f"sil{c}") for c in range(CHUNKS)]
-        for c in range(CHUNKS):
-            for b in range(TILES):
-                first = c * CHUNK + b * P
-                a_turned = psum.tile([P, H], F32, name="bank")
-                for r in range(ROW_BLOCKS):
-                    nc.tensor.transpose(a_turned[:, r * P : (r + 1) * P], a_sb[:, r, first : first + P], ident[:])
-                nc.scalar.activation(sig[c][:, b, :], a_turned[:], ACT.Sigmoid)
-                nc.scalar.copy(a_t[c][:, b, :], a_turned[:])
-        for c in range(CHUNKS):
-            nc.scalar.activation(sil[c][:], a_t[c][:], ACT.Silu, scale=-1.0)
-
-        dh_t = {}
-        for c in range(CHUNKS):
-            tokens = slice(c * CHUNK, (c + 1) * CHUNK)
-            gated = [keep.tile([P, ROW_BLOCKS, CHUNK], F32, name=f"gated{c}_{s}") for s in range(2)]
-            for b in range(TILES):
-                dh_t[c, b] = psum.tile([P, H], F32, name="bank")
-            for r in range(ROW_BLOCKS):
-                for s in range(2):
-                    entries = token_slots[s][:, c * CHUNK // PER_COL : (c + 1) * CHUNK // PER_COL]
-                    nc.vector.tensor_tensor(gated[s][:, r, :], y[r][:].indirect(entries), gates[:, s, tokens], ALU.mult)
-                for b in range(TILES):
-                    for s in range(2):
-                        nc.tensor.matmul(
-                            dh_t[c, b][:, r * P : (r + 1) * P],
-                            lhsT=gated[s][:, r, b * P : (b + 1) * P],
-                            rhs=ident[:],
-                            start=(s == 0),
-                            stop=(s == 1),
-                            is_transpose=True,
-                        )
-
         da_w = keep.tile([P, T], U32, name="da_w", align_bytes=64)
         da_s = keep.tile([P, T], U8, name="da_s", align_bytes=64)
-        for c in range(CHUNKS):
-            last = c == CHUNKS - 1
-            end = (c + 1) * CHUNK
-            in_first_half = end <= HALF
-            fresh = 0 if in_first_half else c * CHUNK
-            if fresh == c * CHUNK:
-                da = keep.tile([P, (HALF if in_first_half else CHUNK) * PACK], BF16, name=f"da{c}", align_bytes=64)
-            neg_ds = keep.tile([P, TILES, H], F32, name=f"neg_ds{c}")
-            nc.vector.scalar_tensor_tensor(neg_ds[:], sil[c][:], 1.0, sig[c][:], ALU.subtract, ALU.mult)
-            per_bank = 1 if last else TILES
-            for b0 in range(0, TILES, per_bank):
-                turned = psum.tile([P, per_bank, 2, P], F32, name="bank")
-                for b in range(b0, b0 + per_bank):
-                    da_t = keep.tile([P, H], BF16, name=f"da_t{c}_{b}")
-                    nc.vector.scalar_tensor_tensor(da_t[:], dh_t[c, b][:], -1.0, neg_ds[:, b, :], ALU.mult, ALU.mult)
-                    pairs = da_t[:].bitcast(F32)
-                    for u in range(2):
-                        nc.tensor.transpose(turned[:, b - b0, u, :], pairs[:, u : H // 2 : 2], ident[:])
-                first_word = (c * CHUNK + b0 * P - fresh) * 2
-                da_pairs = da[:].bitcast(F32)[:, first_word : first_word + 2 * P * per_bank]
-                nc.scalar.copy(
-                    da_pairs.rearrange("p (b t u) -> p b t u", t=P, u=2),
-                    turned[:].rearrange("p b u t -> p b t u"),
-                )
-            if end >= HALF:
-                nc.vector.quantize_mx(da_w[:, fresh:end].bitcast(E5M2), da_s[:, fresh:end], da[:])
-            if end % HALF == 0:
-                for kb in range(K // P):
-                    sums = psum.tile([P, HALF], F32, name="bank")
-                    nc.tensor.matmul_mx(
-                        sums[:],
-                        lhsT=w1_w[:, 2 * P * kb : 2 * P * (kb + 1)].bitcast(E2M1),
-                        lhsT_scale=w1_s[:, P * kb : P * (kb + 1)],
-                        rhs=da_w[:, end - HALF : end].bitcast(E5M2),
-                        rhs_scale=da_s[:, end - HALF : end],
-                        start=True,
-                        stop=True,
+        out_rows = out.rearrange("(kb p) t -> p kb t", p=P)
+        gated = {}
+        neg_ds = {}
+        dh_t = {}
+        da = {}
+
+        on_scalar = ((1, 0), (1, 1), (2, 1), (3, 1))
+
+        def gather(c, s):
+            tokens = slice(c * CHUNK, (c + 1) * CHUNK)
+            entries = token_slots[s][:, c * CHUNK // PER_COL : (c + 1) * CHUNK // PER_COL]
+            gated[c, s] = keep.tile([P, ROW_BLOCKS, CHUNK], F32, name=f"gated{c}_{s}")
+            for r in range(ROW_BLOCKS):
+                if (c, s) in on_scalar:
+                    nc.scalar.activation(gated[c, s][:, r, :], y[r][:].indirect(entries), ACT.Copy)
+                else:
+                    nc.vector.tensor_tensor(gated[c, s][:, r, :], y[r][:].indirect(entries), gates[s][:, tokens], ALU.mult)
+
+        def apply_gate(c, s):
+            tokens = slice(c * CHUNK, (c + 1) * CHUNK)
+            wide = gates[s][:, tokens].unsqueeze(1).to_broadcast([P, ROW_BLOCKS, CHUNK])
+            nc.vector.tensor_tensor(gated[c, s][:], gated[c, s][:], wide, ALU.mult)
+
+        sil = {}
+
+        def silu(c):
+            sil[c] = keep.tile([P, TILES, H], F32, name=f"sil{c}")
+            for b in range(TILES):
+                turned_a = held[c, b] if c < 2 else turn_a(c, b, bank((c - 2) * TILES + b, [P, H]))
+                nc.scalar.activation(sil[c][:, b, :], turned_a[:], ACT.Silu, scale=-1.0)
+
+        def slope(c):
+            neg_ds[c] = sil[c]
+            nc.vector.scalar_tensor_tensor(neg_ds[c][:], sil[c][:], 1.0, sig[c][:], ALU.subtract, ALU.mult)
+
+        def turn_sum(c, s):
+            for b in range(TILES):
+                if s == 0:
+                    dh_t[c, b] = bank((4, 2, 6, 0)[c] + b, [P, H])
+                for r in range(ROW_BLOCKS):
+                    nc.tensor.matmul(
+                        block_columns(dh_t[c, b], r),
+                        lhsT=gated[c, s][:, r, b * P : (b + 1) * P],
+                        rhs=ident[:],
+                        start=(s == 0 and r == 0),
+                        stop=(s == 1 and r == ROW_BLOCKS - 1),
+                        is_transpose=True,
                     )
-                    res = keep.tile([P, HALF], F32, name=f"res{c}_{kb}")
-                    dst = out[kb * P : (kb + 1) * P, end - HALF : end]
-                    if last and kb == 1:
-                        nc.vector.tensor_copy(res[:], sums[:])
-                        nc.sync.dma_start(dst, res[:])
-                    elif last:
-                        nc.scalar.copy(res[:], sums[:])
-                        nc.scalar.dma_start(dst, res[:])
-                    else:
-                        nc.scalar.copy(res[:], sums[:])
-                        nc.sync.dma_start(dst, res[:])
+
+        def turn_back(c):
+            da[c] = ring.tile([P, CHUNK * PACK], BF16, name="da", align_bytes=64)
+            turned = bank((4, 4, 2, 6)[c], [P, TILES, 2, P])
+            for b in range(TILES):
+                da_t = ring.tile([P, H], BF16, name="da_t")
+                nc.vector.scalar_tensor_tensor(da_t[:], dh_t[c, b][:], -1.0, neg_ds[c][:, b, :], ALU.mult, ALU.mult)
+                pairs = da_t[:].bitcast(F32)
+                for u in range(2):
+                    nc.tensor.transpose(turned[:, b, u, :], pairs[:, u * P : (u + 1) * P], ident[:])
+            nc.scalar.copy(
+                da[c][:].bitcast(F32).rearrange("p (b t u) -> p b t u", t=P, u=2),
+                turned[:].rearrange("p b u t -> p b t u"),
+            )
+
+        def finish(c):
+            tokens = slice(c * CHUNK, (c + 1) * CHUNK)
+            nc.vector.quantize_mx(da_w[:, tokens].bitcast(E5M2), da_s[:, tokens], da[c][:])
+            sums = bank((5, 5, 3, 7)[c], [P, K // P, CHUNK])
+            for kb in range(K // P):
+                nc.tensor.matmul_mx(
+                    sums[:, kb, :],
+                    lhsT=w1_w[:, 2 * P * kb : 2 * P * (kb + 1)].bitcast(E2M1),
+                    lhsT_scale=w1_s[:, P * kb : P * (kb + 1)],
+                    rhs=da_w[:, tokens].bitcast(E5M2),
+                    rhs_scale=da_s[:, tokens],
+                    start=True,
+                    stop=True,
+                )
+            res = keep.tile([P, K // P, CHUNK], F32, name=f"res{c}")
+            nc.scalar.copy(res[:], sums[:])
+            nc.sync.dma_start(out_rows[:, :, tokens], res[:])
+
+        sigmoid(0, 4)
+        sigmoid(1, 6)
+        for c in range(CHUNKS):
+            silu(c)
+        for c, s in ((0, 0), (0, 1), (2, 0), (3, 0)):
+            gather(c, s)
+            turn_sum(c, s)
+        for c, s in on_scalar:
+            gather(c, s)
+        slope(0)
+        slope(1)
+        turn_back(0)
+        apply_gate(1, 0)
+        turn_sum(1, 0)
+        slope(2)
+        apply_gate(1, 1)
+        turn_sum(1, 1)
+        finish(0)
+        slope(3)
+        apply_gate(2, 1)
+        turn_sum(2, 1)
+        turn_back(1)
+        apply_gate(3, 1)
+        turn_sum(3, 1)
+        turn_back(2)
+        finish(1)
+        turn_back(3)
+        finish(2)
+        finish(3)

@@ -22,12 +22,9 @@ PACK = 4
 QUADRANT = 32
 SCALE_ROWS = 4
 PER_COL = 16
-CHUNK = 256
-HALF = 512
 BANKS = 8
 ROW_BLOCKS = H // P
-CHUNKS = T // CHUNK
-TILES = CHUNK // P
+TOKEN_TILES = T // P
 
 
 def tile_moe_sub_silu_kernel(
@@ -37,7 +34,6 @@ def tile_moe_sub_silu_kernel(
 
     with ExitStack() as ctx:
         keep = ctx.enter_context(tc.tile_pool(name="keep", bufs=1))
-        ring = ctx.enter_context(tc.tile_pool(name="ring", bufs=4))
         psum = ctx.enter_context(tc.psum_pool(name="psum", bufs=1))
 
         def bank(place, shape):
@@ -53,7 +49,7 @@ def tile_moe_sub_silu_kernel(
         w1_s = keep.tile([P, K], U8, name="w1_s", align_bytes=64)
         w1_w = keep.tile([P, 2 * K], U8, name="w1_w", align_bytes=64)
         gates = [keep.tile([P, T], F32, name=f"gates{s}") for s in range(2)]
-        a_sb = [keep.tile([P, ROW_BLOCKS, CHUNK], F32, name=f"a_sb{c}") for c in range(CHUNKS)]
+        a_sb = [keep.tile([P, ROW_BLOCKS, 2 * P], F32, name=f"a_sb{c}") for c in range(TOKEN_TILES // 2)]
         ident = keep.tile([P, P], F32, name="ident")
 
         nc.vector.memset(w2_s[:].bitcast(I32), 0)
@@ -71,23 +67,32 @@ def tile_moe_sub_silu_kernel(
         w1_rows = w1t_scales[0].rearrange("(q j) k -> j q k", j=SCALE_ROWS)
         a_rows = a.rearrange("(r q) t -> q r t", q=P)
 
-        def load_a(c):
-            nc.sync.dma_start(a_sb[c][:], a_rows[:, :, c * CHUNK : (c + 1) * CHUNK])
+        def load_a(pair):
+            nc.sync.dma_start(a_sb[pair][:], a_rows[:, :, pair * 2 * P : (pair + 1) * 2 * P])
+
+        def load_dy_words():
+            nc.sync.dma_start(dy_w[:], dy_words[0].rearrange("p t d -> p (t d)").bitcast(I32))
+
+        def load_w2_first():
+            nc.sync.dma_start(w2_first[:].bitcast(I32), w2t_words[0:1, 0].rearrange("e p b -> p e b").bitcast(I32))
+            for j in range(SCALE_ROWS):
+                nc.sync.dma_start(w2_s[j:P:QUADRANT, :, :].bitcast(I32), w2_rows[j].bitcast(I32))
+
+        def load_w2_rest():
+            nc.sync.dma_start(w2_rest[:].bitcast(I32), w2t_words[1:E, 0].rearrange("e p b -> p e b").bitcast(I32))
 
         nc.sync.dma_start(slot_tokens[:], offs)
         load_dy_scales(nc.sync, 0)
         load_dy_scales(nc.sync, 1)
         load_dy_scales(nc.scalar, 2)
         load_dy_scales(nc.scalar, 3)
-        load_a(2)
-        nc.sync.dma_start(dy_w[:], dy_words[0].rearrange("p t d -> p (t d)").bitcast(I32))
-        nc.sync.dma_start(w2_first[:].bitcast(I32), w2t_words[0:1, 0].rearrange("e p b -> p e b").bitcast(I32))
-        for j in range(SCALE_ROWS):
-            nc.sync.dma_start(w2_s[j:P:QUADRANT, :, :].bitcast(I32), w2_rows[j].bitcast(I32))
-        load_a(3)
-        nc.sync.dma_start(w2_rest[:].bitcast(I32), w2t_words[1:E, 0].rearrange("e p b -> p e b").bitcast(I32))
-        load_a(0)
         load_a(1)
+        load_a(2)
+        load_dy_words()
+        load_a(3)
+        load_w2_first()
+        load_w2_rest()
+        load_a(0)
         for s, lst in enumerate((pos1, pos2)):
             nc.sync.dma_start(token_slots[s][:], lst)
         for s in range(2):
@@ -99,50 +104,42 @@ def tile_moe_sub_silu_kernel(
         def block_columns(tile, r):
             return tile[:].rearrange("t (u r q d) -> t r q u d", u=2, r=ROW_BLOCKS, d=2)[:, r]
 
-        def turn_a(c, b, a_turned):
+        def turn_a(b, place):
+            a_turned = bank(place, [P, H])
             for r in range(ROW_BLOCKS):
-                nc.tensor.transpose(block_columns(a_turned, r), a_sb[c][:, r, b * P : (b + 1) * P], ident[:])
+                nc.tensor.transpose(block_columns(a_turned, r), a_sb[b // 2][:, r, b % 2 * P : (b % 2 + 1) * P], ident[:])
             return a_turned
 
-        sig = [keep.tile([P, TILES, H], F32, name=f"sig{c}") for c in range(CHUNKS)]
-        held = {}
+        sig = keep.tile([P, TOKEN_TILES, H], F32, name="sig")
+        neg_ds = keep.tile([P, TOKEN_TILES, H], F32, name="neg_ds")
+        a_turned = {}
 
-        def sigmoid(c, first_bank):
-            for b in range(TILES):
-                held[c, b] = turn_a(c, b, bank(first_bank + b, [P, H]))
-                nc.scalar.activation(sig[c][:, b, :], held[c, b][:], ACT.Sigmoid)
+        def sigmoid(b, place):
+            a_turned[b] = turn_a(b, place)
+            nc.scalar.activation(sig[:, b, :], a_turned[b][:], ACT.Sigmoid)
 
-        sigmoid(2, 0)
+        EARLY = 6
+        LATE = TOKEN_TILES - EARLY
+        for b in range(LATE, TOKEN_TILES):
+            sigmoid(b, b - LATE)
 
         y = [keep.tile([P, E * C], F32, name=f"y{r}") for r in range(ROW_BLOCKS)]
-        emptied_by_vector = ((3, 0), (3, 1), (3, 2), (3, 3))
-        g_s = {}
-        g_w = [keep.tile([P, C], U32, name=f"g_w{e}", align_bytes=64) for e in range(E)]
-
-        def expert_entries(e):
-            return slot_tokens[:, e * C // PER_COL : (e + 1) * C // PER_COL]
-
-        def gather_bytes(e):
-            g_s[e] = keep.tile([P, C], U8, name=f"g_s{e % 2}", align_bytes=64)
-            nc.vector.tensor_copy(g_s[e][:], dy_s[:].indirect(expert_entries(e)))
-
-        def gather_words(e):
-            nc.vector.tensor_copy(g_w[e][:], dy_w[:].bitcast(U32).indirect(expert_entries(e)))
-
+        emptied_by_vector = ((2, 0), (2, 1), (2, 2), (3, 0), (3, 2))
         for e in range(E):
-            gather_bytes(e)
-            gather_words(e)
-            if e == 1:
-                sigmoid(3, 6)
+            entries = slot_tokens[:, e * C // PER_COL : (e + 1) * C // PER_COL]
+            g_s = keep.tile([P, C], U8, name=f"g_s{e % 3}", align_bytes=64)
+            g_w = keep.tile([P, C], U32, name=f"g_w{e}", align_bytes=64)
+            nc.vector.tensor_copy(g_s[:], dy_s[:].indirect(entries))
+            nc.vector.tensor_copy(g_w[:], dy_w[:].bitcast(U32).indirect(entries))
             words = w2_first[:, 0, :] if e == 0 else w2_rest[:, e - 1, :]
             for r in range(ROW_BLOCKS):
-                y_sums = bank((2, 0, 4, 0)[e] + r, [P, C])
+                y_sums = bank(((6, 7, 0, 1), (2, 3, 4, 5), (6, 7, 0, 1), (6, 2, 7, 3))[e][r], [P, C])
                 nc.tensor.matmul_mx(
                     y_sums[:],
                     lhsT=words[:, 2 * P * r : 2 * P * (r + 1)].bitcast(E2M1),
                     lhsT_scale=w2_s[:, e, P * r : P * (r + 1)],
-                    rhs=g_w[e][:].bitcast(E5M2),
-                    rhs_scale=g_s[e][:],
+                    rhs=g_w[:].bitcast(E5M2),
+                    rhs_scale=g_s[:],
                     start=True,
                     stop=True,
                 )
@@ -151,115 +148,126 @@ def tile_moe_sub_silu_kernel(
                 else:
                     nc.scalar.copy(y[r][:, e * C : (e + 1) * C], y_sums[:])
 
+        for b in range(LATE):
+            sigmoid(b, (4, 5, 0, 1, 6, 2, 7, 3)[b])
+        for b in range(TOKEN_TILES):
+            if b >= LATE:
+                a_turned[b] = turn_a(b, (4, 5, 0, 1, 6, 2, 7, 3)[b])
+            nc.scalar.activation(neg_ds[:, b, :], a_turned[b][:], ACT.Silu, scale=-1.0)
+
         da_w = keep.tile([P, T], U32, name="da_w", align_bytes=64)
         da_s = keep.tile([P, T], U8, name="da_s", align_bytes=64)
         out_rows = out.rearrange("(kb p) t -> p kb t", p=P)
+        chunks = (range(0, 2), range(2, 4), range(4, 6), range(6, 7), range(7, 8))
+        on_scalar = ((1, 0), (1, 1), (2, 0), (2, 1), (3, 1), (4, 1))
+        dh_bank = (4, 5, 6, 2, 7, 3, 0, 1)
+        back_bank = (4, 6, 7, 4, 0)
+        out_bank = (5, 2, 3, 5, 1)
         gated = {}
-        neg_ds = {}
         dh_t = {}
         da = {}
 
-        on_scalar = ((1, 0), (1, 1), (2, 1), (3, 1))
+        def tokens(c):
+            return slice(chunks[c].start * P, chunks[c].stop * P)
 
         def gather(c, s):
-            tokens = slice(c * CHUNK, (c + 1) * CHUNK)
-            entries = token_slots[s][:, c * CHUNK // PER_COL : (c + 1) * CHUNK // PER_COL]
-            gated[c, s] = keep.tile([P, ROW_BLOCKS, CHUNK], F32, name=f"gated{c}_{s}")
+            entries = token_slots[s][:, tokens(c).start // PER_COL : tokens(c).stop // PER_COL]
+            gated[c, s] = keep.tile([P, ROW_BLOCKS, len(chunks[c]) * P], F32, name=f"gated{c}_{s}")
             for r in range(ROW_BLOCKS):
                 if (c, s) in on_scalar:
                     nc.scalar.activation(gated[c, s][:, r, :], y[r][:].indirect(entries), ACT.Copy)
                 else:
-                    nc.vector.tensor_tensor(gated[c, s][:, r, :], y[r][:].indirect(entries), gates[s][:, tokens], ALU.mult)
+                    nc.vector.tensor_tensor(gated[c, s][:, r, :], y[r][:].indirect(entries), gates[s][:, tokens(c)], ALU.mult)
 
-        def apply_gate(c, s):
-            tokens = slice(c * CHUNK, (c + 1) * CHUNK)
-            wide = gates[s][:, tokens].unsqueeze(1).to_broadcast([P, ROW_BLOCKS, CHUNK])
-            nc.vector.tensor_tensor(gated[c, s][:], gated[c, s][:], wide, ALU.mult)
-
-        sil = {}
-
-        def silu(c):
-            sil[c] = keep.tile([P, TILES, H], F32, name=f"sil{c}")
-            for b in range(TILES):
-                turned_a = held[c, b] if c < 2 else turn_a(c, b, bank((c - 2) * TILES + b, [P, H]))
-                nc.scalar.activation(sil[c][:, b, :], turned_a[:], ACT.Silu, scale=-1.0)
-
-        def slope(c):
-            neg_ds[c] = sil[c]
-            nc.vector.scalar_tensor_tensor(neg_ds[c][:], sil[c][:], 1.0, sig[c][:], ALU.subtract, ALU.mult)
-
-        def turn_sum(c, s):
-            for b in range(TILES):
+        def turn(c, s):
+            if (c, s) in on_scalar:
+                wide = gates[s][:, tokens(c)].unsqueeze(1).to_broadcast([P, ROW_BLOCKS, len(chunks[c]) * P])
+                nc.vector.tensor_tensor(gated[c, s][:], gated[c, s][:], wide, ALU.mult)
+            for n, b in enumerate(chunks[c]):
                 if s == 0:
-                    dh_t[c, b] = bank((4, 2, 6, 0)[c] + b, [P, H])
+                    dh_t[b] = bank(dh_bank[b], [P, H])
                 for r in range(ROW_BLOCKS):
                     nc.tensor.matmul(
-                        block_columns(dh_t[c, b], r),
-                        lhsT=gated[c, s][:, r, b * P : (b + 1) * P],
+                        block_columns(dh_t[b], r),
+                        lhsT=gated[c, s][:, r, n * P : (n + 1) * P],
                         rhs=ident[:],
                         start=(s == 0 and r == 0),
                         stop=(s == 1 and r == ROW_BLOCKS - 1),
                         is_transpose=True,
                     )
 
+        def slope(first, stop):
+            nc.vector.scalar_tensor_tensor(
+                neg_ds[:, first:stop, :], neg_ds[:, first:stop, :], 1.0, sig[:, first:stop, :], ALU.subtract, ALU.mult
+            )
+
         def turn_back(c):
-            da[c] = ring.tile([P, CHUNK * PACK], BF16, name="da", align_bytes=64)
-            turned = bank((4, 4, 2, 6)[c], [P, TILES, 2, P])
-            for b in range(TILES):
-                da_t = ring.tile([P, H], BF16, name="da_t")
-                nc.vector.scalar_tensor_tensor(da_t[:], dh_t[c, b][:], -1.0, neg_ds[c][:, b, :], ALU.mult, ALU.mult)
+            width = len(chunks[c])
+            da[c] = keep.tile([P, width * P * PACK], BF16, name=f"da{c}", align_bytes=64)
+            turned = bank(back_bank[c], [P, width, 2, P])
+            for n, b in enumerate(chunks[c]):
+                da_t = keep.tile([P, H], BF16, name=f"da_t{b}")
+                nc.vector.scalar_tensor_tensor(da_t[:], dh_t[b][:], -1.0, neg_ds[:, b, :], ALU.mult, ALU.mult)
                 pairs = da_t[:].bitcast(F32)
                 for u in range(2):
-                    nc.tensor.transpose(turned[:, b, u, :], pairs[:, u * P : (u + 1) * P], ident[:])
+                    nc.tensor.transpose(turned[:, n, u, :], pairs[:, u * P : (u + 1) * P], ident[:])
             nc.scalar.copy(
                 da[c][:].bitcast(F32).rearrange("p (b t u) -> p b t u", t=P, u=2),
                 turned[:].rearrange("p b u t -> p b t u"),
             )
 
         def finish(c):
-            tokens = slice(c * CHUNK, (c + 1) * CHUNK)
-            nc.vector.quantize_mx(da_w[:, tokens].bitcast(E5M2), da_s[:, tokens], da[c][:])
-            sums = bank((5, 5, 3, 7)[c], [P, K // P, CHUNK])
+            width = len(chunks[c]) * P
+            nc.vector.quantize_mx(da_w[:, tokens(c)].bitcast(E5M2), da_s[:, tokens(c)], da[c][:])
+            sums = bank(out_bank[c], [P, K // P, width])
             for kb in range(K // P):
                 nc.tensor.matmul_mx(
                     sums[:, kb, :],
                     lhsT=w1_w[:, 2 * P * kb : 2 * P * (kb + 1)].bitcast(E2M1),
                     lhsT_scale=w1_s[:, P * kb : P * (kb + 1)],
-                    rhs=da_w[:, tokens].bitcast(E5M2),
-                    rhs_scale=da_s[:, tokens],
+                    rhs=da_w[:, tokens(c)].bitcast(E5M2),
+                    rhs_scale=da_s[:, tokens(c)],
                     start=True,
                     stop=True,
                 )
-            res = keep.tile([P, K // P, CHUNK], F32, name=f"res{c}")
-            nc.scalar.copy(res[:], sums[:])
-            nc.sync.dma_start(out_rows[:, :, tokens], res[:])
+            res = keep.tile([P, K // P, width], F32, name=f"res{c}")
+            if c in (4,):
+                nc.vector.tensor_copy(res[:], sums[:])
+            else:
+                nc.scalar.copy(res[:], sums[:])
+            nc.sync.dma_start(out_rows[:, :, tokens(c)], res[:])
 
-        sigmoid(0, 4)
-        sigmoid(1, 6)
-        for c in range(CHUNKS):
-            silu(c)
-        for c, s in ((0, 0), (0, 1), (2, 0), (3, 0)):
-            gather(c, s)
-            turn_sum(c, s)
-        for c, s in on_scalar:
-            gather(c, s)
-        slope(0)
-        slope(1)
+        gather(0, 0)
+        turn(0, 0)
+        gather(0, 1)
+        turn(0, 1)
+        gather(3, 0)
+        turn(3, 0)
+        gather(4, 0)
+        turn(4, 0)
+        gather(1, 0)
+        gather(1, 1)
+        gather(2, 0)
+        gather(2, 1)
+        slope(0, 2)
+        slope(2, 4)
         turn_back(0)
-        apply_gate(1, 0)
-        turn_sum(1, 0)
-        slope(2)
-        apply_gate(1, 1)
-        turn_sum(1, 1)
-        finish(0)
-        slope(3)
-        apply_gate(2, 1)
-        turn_sum(2, 1)
+        gather(3, 1)
+        gather(4, 1)
+        turn(1, 0)
+        slope(4, 6)
+        turn(1, 1)
+        slope(6, 8)
+        turn(2, 0)
         turn_back(1)
-        apply_gate(3, 1)
-        turn_sum(3, 1)
+        turn(2, 1)
+        finish(0)
+        turn(3, 1)
         turn_back(2)
+        turn(4, 1)
         finish(1)
         turn_back(3)
+        turn_back(4)
         finish(2)
         finish(3)
+        finish(4)

@@ -86,13 +86,13 @@ def tile_moe_sub_silu_kernel(
         load_dy_scales(nc.sync, 1)
         load_dy_scales(nc.scalar, 2)
         load_dy_scales(nc.scalar, 3)
+        load_a(3)
+        load_dy_words()
+        load_w2_first()
+        load_a(0)
+        load_w2_rest()
         load_a(1)
         load_a(2)
-        load_dy_words()
-        load_a(3)
-        load_w2_first()
-        load_w2_rest()
-        load_a(0)
         for s, lst in enumerate((pos1, pos2)):
             nc.sync.dma_start(token_slots[s][:], lst)
         for s in range(2):
@@ -118,22 +118,25 @@ def tile_moe_sub_silu_kernel(
             a_turned[b] = turn_a(b, place)
             nc.scalar.activation(sig[:, b, :], a_turned[b][:], ACT.Sigmoid)
 
-        EARLY = 6
-        LATE = TOKEN_TILES - EARLY
-        for b in range(LATE, TOKEN_TILES):
-            sigmoid(b, b - LATE)
+        late = (2, 3, 4, 5)
+        early = (6, 7, 0, 1)
+        sigmoid(6, 0)
+        sigmoid(7, 1)
 
         y = [keep.tile([P, E * C], F32, name=f"y{r}") for r in range(ROW_BLOCKS)]
         emptied_by_vector = ((2, 0), (2, 1), (2, 2), (3, 0), (3, 2))
         for e in range(E):
             entries = slot_tokens[:, e * C // PER_COL : (e + 1) * C // PER_COL]
-            g_s = keep.tile([P, C], U8, name=f"g_s{e % 3}", align_bytes=64)
+            g_s = keep.tile([P, C], U8, name=f"g_s{e % 2}", align_bytes=64)
             g_w = keep.tile([P, C], U32, name=f"g_w{e}", align_bytes=64)
             nc.vector.tensor_copy(g_s[:], dy_s[:].indirect(entries))
             nc.vector.tensor_copy(g_w[:], dy_w[:].bitcast(U32).indirect(entries))
+            if e == 1:
+                sigmoid(0, 6)
+                sigmoid(1, 7)
             words = w2_first[:, 0, :] if e == 0 else w2_rest[:, e - 1, :]
             for r in range(ROW_BLOCKS):
-                y_sums = bank(((6, 7, 0, 1), (2, 3, 4, 5), (6, 7, 0, 1), (6, 2, 7, 3))[e][r], [P, C])
+                y_sums = bank(((2, 3, 4, 5), (0, 1, 2, 3), (4, 5, 6, 7), (0, 4, 1, 5))[e][r], [P, C])
                 nc.tensor.matmul_mx(
                     y_sums[:],
                     lhsT=words[:, 2 * P * r : 2 * P * (r + 1)].bitcast(E2M1),
@@ -148,48 +151,57 @@ def tile_moe_sub_silu_kernel(
                 else:
                     nc.scalar.copy(y[r][:, e * C : (e + 1) * C], y_sums[:])
 
-        for b in range(LATE):
-            sigmoid(b, (4, 5, 0, 1, 6, 2, 7, 3)[b])
-        for b in range(TOKEN_TILES):
-            if b >= LATE:
-                a_turned[b] = turn_a(b, (4, 5, 0, 1, 6, 2, 7, 3)[b])
+        a_bank = dict(zip(late + early, (2, 3, 6, 7, 0, 4, 1, 5)))
+        for b in late:
+            sigmoid(b, a_bank[b])
+        for b in late + early:
+            if b in early:
+                a_turned[b] = turn_a(b, a_bank[b])
             nc.scalar.activation(neg_ds[:, b, :], a_turned[b][:], ACT.Silu, scale=-1.0)
 
         da_w = keep.tile([P, T], U32, name="da_w", align_bytes=64)
         da_s = keep.tile([P, T], U8, name="da_s", align_bytes=64)
         out_rows = out.rearrange("(kb p) t -> p kb t", p=P)
-        chunks = (range(0, 2), range(2, 4), range(4, 6), range(6, 7), range(7, 8))
-        on_scalar = ((1, 0), (1, 1), (2, 0), (2, 1), (3, 1), (4, 1))
-        dh_bank = (4, 5, 6, 2, 7, 3, 0, 1)
-        back_bank = (4, 6, 7, 4, 0)
-        out_bank = (5, 2, 3, 5, 1)
+        chunks = (range(2, 4), range(4, 6), range(6, 8), range(0, 1), range(1, 2))
+        dh_bank = (6, 7, 2, 3, 0, 4, 1, 5)
+        back_bank = (2, 0, 1, 2, 6)
+        out_bank = (3, 4, 5, 3, 7)
         gated = {}
+        block = {}
         dh_t = {}
         da = {}
 
         def tokens(c):
             return slice(chunks[c].start * P, chunks[c].stop * P)
 
-        def gather(c, s):
-            entries = token_slots[s][:, tokens(c).start // PER_COL : tokens(c).stop // PER_COL]
-            gated[c, s] = keep.tile([P, ROW_BLOCKS, len(chunks[c]) * P], F32, name=f"gated{c}_{s}")
-            for r in range(ROW_BLOCKS):
-                if (c, s) in on_scalar:
-                    nc.scalar.activation(gated[c, s][:, r, :], y[r][:].indirect(entries), ACT.Copy)
-                else:
-                    nc.vector.tensor_tensor(gated[c, s][:, r, :], y[r][:].indirect(entries), gates[s][:, tokens(c)], ALU.mult)
+        def new_gated(s, first, stop):
+            gated[s, first] = keep.tile([P, ROW_BLOCKS, (stop - first) * P], F32, name=f"gated{s}_{first}")
+            for b in range(first, stop):
+                block[s, b] = gated[s, first][:, :, (b - first) * P : (b - first + 1) * P]
+            return gated[s, first], token_slots[s][:, first * P // PER_COL : stop * P // PER_COL]
 
-        def turn(c, s):
-            if (c, s) in on_scalar:
-                wide = gates[s][:, tokens(c)].unsqueeze(1).to_broadcast([P, ROW_BLOCKS, len(chunks[c]) * P])
-                nc.vector.tensor_tensor(gated[c, s][:], gated[c, s][:], wide, ALU.mult)
-            for n, b in enumerate(chunks[c]):
+        def gather_gated(s, first, stop):
+            tile, entries = new_gated(s, first, stop)
+            for r in range(ROW_BLOCKS):
+                nc.vector.tensor_tensor(tile[:, r, :], y[r][:].indirect(entries), gates[s][:, first * P : stop * P], ALU.mult)
+
+        def gather_plain(s, first, stop):
+            tile, entries = new_gated(s, first, stop)
+            for r in range(ROW_BLOCKS):
+                nc.scalar.activation(tile[:, r, :], y[r][:].indirect(entries), ACT.Copy)
+
+        def apply_gate(s, first, stop):
+            wide = gates[s][:, first * P : stop * P].unsqueeze(1).to_broadcast([P, ROW_BLOCKS, (stop - first) * P])
+            nc.vector.tensor_tensor(gated[s, first][:], gated[s, first][:], wide, ALU.mult)
+
+        def turn(s, first, stop):
+            for b in range(first, stop):
                 if s == 0:
                     dh_t[b] = bank(dh_bank[b], [P, H])
                 for r in range(ROW_BLOCKS):
                     nc.tensor.matmul(
                         block_columns(dh_t[b], r),
-                        lhsT=gated[c, s][:, r, n * P : (n + 1) * P],
+                        lhsT=block[s, b][:, r, :],
                         rhs=ident[:],
                         start=(s == 0 and r == 0),
                         stop=(s == 1 and r == ROW_BLOCKS - 1),
@@ -237,34 +249,37 @@ def tile_moe_sub_silu_kernel(
                 nc.scalar.copy(res[:], sums[:])
             nc.sync.dma_start(out_rows[:, :, tokens(c)], res[:])
 
-        gather(0, 0)
-        turn(0, 0)
-        gather(0, 1)
-        turn(0, 1)
-        gather(3, 0)
-        turn(3, 0)
-        gather(4, 0)
-        turn(4, 0)
-        gather(1, 0)
-        gather(1, 1)
-        gather(2, 0)
-        gather(2, 1)
-        slope(0, 2)
-        slope(2, 4)
+        gather_gated(1, 2, 4)
+        gather_gated(0, 0, 5)
+        turn(0, 2, 4)
+        turn(1, 2, 4)
+        turn(0, 0, 2)
+        turn(0, 4, 5)
+        gather_plain(0, 5, 6)
+        gather_plain(1, 4, 6)
+        gather_plain(0, 6, 8)
+        gather_plain(1, 6, 8)
+        slope(2, 6)
         turn_back(0)
-        gather(3, 1)
-        gather(4, 1)
-        turn(1, 0)
-        slope(4, 6)
-        turn(1, 1)
+        gather_plain(1, 0, 1)
+        gather_plain(1, 1, 2)
+        apply_gate(0, 5, 6)
+        turn(0, 5, 6)
         slope(6, 8)
-        turn(2, 0)
+        apply_gate(1, 4, 6)
+        turn(1, 4, 6)
+        slope(0, 2)
+        apply_gate(0, 6, 8)
+        turn(0, 6, 8)
         turn_back(1)
-        turn(2, 1)
+        apply_gate(1, 6, 8)
+        turn(1, 6, 8)
         finish(0)
-        turn(3, 1)
+        apply_gate(1, 0, 1)
+        turn(1, 0, 1)
         turn_back(2)
-        turn(4, 1)
+        apply_gate(1, 1, 2)
+        turn(1, 1, 2)
         finish(1)
         turn_back(3)
         turn_back(4)

@@ -124,7 +124,7 @@ def tile_moe_sub_silu_kernel(
         sigmoid(7, 1)
 
         y = [keep.tile([P, E * C], F32, name=f"y{r}") for r in range(ROW_BLOCKS)]
-        emptied_by_vector = ((2, 0), (2, 1), (2, 2), (3, 0), (3, 2))
+        emptied_by_vector = ((3, 0), (3, 1), (3, 2), (3, 3))
         for e in range(E):
             entries = slot_tokens[:, e * C // PER_COL : (e + 1) * C // PER_COL]
             g_s = keep.tile([P, C], U8, name=f"g_s{e % 2}", align_bytes=64)
@@ -136,7 +136,7 @@ def tile_moe_sub_silu_kernel(
                 sigmoid(1, 7)
             words = w2_first[:, 0, :] if e == 0 else w2_rest[:, e - 1, :]
             for r in range(ROW_BLOCKS):
-                y_sums = bank(((2, 3, 4, 5), (0, 1, 2, 3), (4, 5, 6, 7), (0, 4, 1, 5))[e][r], [P, C])
+                y_sums = bank(((2, 3, 4, 5), (0, 1, 2, 3), (4, 5, 6, 7), (0, 1, 2, 3))[e][r], [P, C])
                 nc.tensor.matmul_mx(
                     y_sums[:],
                     lhsT=words[:, 2 * P * r : 2 * P * (r + 1)].bitcast(E2M1),
@@ -151,7 +151,7 @@ def tile_moe_sub_silu_kernel(
                 else:
                     nc.scalar.copy(y[r][:, e * C : (e + 1) * C], y_sums[:])
 
-        a_bank = dict(zip(late + early, (2, 3, 6, 7, 0, 4, 1, 5)))
+        a_bank = dict(zip(late + early, (4, 5, 6, 7, 0, 1, 2, 3)))
         for b in late:
             sigmoid(b, a_bank[b])
         for b in late + early:
@@ -163,9 +163,9 @@ def tile_moe_sub_silu_kernel(
         da_s = keep.tile([P, T], U8, name="da_s", align_bytes=64)
         out_rows = out.rearrange("(kb p) t -> p kb t", p=P)
         chunks = (range(2, 4), range(4, 6), range(6, 8), range(0, 1), range(1, 2))
-        dh_bank = (6, 7, 2, 3, 0, 4, 1, 5)
-        back_bank = (2, 0, 1, 2, 6)
-        out_bank = (3, 4, 5, 3, 7)
+        dh_bank = (6, 7, 4, 5, 0, 1, 2, 3)
+        back_bank = (4, 0, 2, 4, 6)
+        out_bank = (5, 1, 3, 5, 7)
         gated = {}
         block = {}
         dh_t = {}
@@ -250,12 +250,11 @@ def tile_moe_sub_silu_kernel(
             nc.sync.dma_start(out_rows[:, :, tokens(c)], res[:])
 
         gather_gated(1, 2, 4)
-        gather_gated(0, 0, 5)
+        gather_gated(0, 0, 6)
         turn(0, 2, 4)
         turn(1, 2, 4)
         turn(0, 0, 2)
-        turn(0, 4, 5)
-        gather_plain(0, 5, 6)
+        turn(0, 4, 6)
         gather_plain(1, 4, 6)
         gather_plain(0, 6, 8)
         gather_plain(1, 6, 8)
@@ -263,23 +262,21 @@ def tile_moe_sub_silu_kernel(
         turn_back(0)
         gather_plain(1, 0, 1)
         gather_plain(1, 1, 2)
-        apply_gate(0, 5, 6)
-        turn(0, 5, 6)
-        slope(6, 8)
         apply_gate(1, 4, 6)
         turn(1, 4, 6)
-        slope(0, 2)
+        slope(6, 8)
         apply_gate(0, 6, 8)
         turn(0, 6, 8)
+        slope(0, 2)
         turn_back(1)
         apply_gate(1, 6, 8)
         turn(1, 6, 8)
-        finish(0)
         apply_gate(1, 0, 1)
         turn(1, 0, 1)
-        turn_back(2)
+        finish(0)
         apply_gate(1, 1, 2)
         turn(1, 1, 2)
+        turn_back(2)
         finish(1)
         turn_back(3)
         turn_back(4)

@@ -124,7 +124,7 @@ def tile_moe_sub_silu_kernel(
         sigmoid(7, 1)
 
         y = [keep.tile([P, E * C], F32, name=f"y{r}") for r in range(ROW_BLOCKS)]
-        emptied_by_vector = ((3, 0), (3, 1), (3, 2), (3, 3))
+        emptied_by_vector = ((3, 1), (3, 2), (3, 3))
         for e in range(E):
             entries = slot_tokens[:, e * C // PER_COL : (e + 1) * C // PER_COL]
             g_s = keep.tile([P, C], U8, name=f"g_s{e % 2}", align_bytes=64)
@@ -174,37 +174,41 @@ def tile_moe_sub_silu_kernel(
         def tokens(c):
             return slice(chunks[c].start * P, chunks[c].stop * P)
 
-        def new_gated(s, first, stop):
-            gated[s, first] = keep.tile([P, ROW_BLOCKS, (stop - first) * P], F32, name=f"gated{s}_{first}")
+        def new_gated(s, first, stop, rows):
+            name = f"gated{s}_{first}_{rows.start}"
+            gated[s, first] = keep.tile([P, len(rows), (stop - first) * P], F32, name=name)
             for b in range(first, stop):
-                block[s, b] = gated[s, first][:, :, (b - first) * P : (b - first + 1) * P]
+                for n, r in enumerate(rows):
+                    block[s, b, r] = gated[s, first][:, n, (b - first) * P : (b - first + 1) * P]
             return gated[s, first], token_slots[s][:, first * P // PER_COL : stop * P // PER_COL]
 
-        def gather_gated(s, first, stop):
-            tile, entries = new_gated(s, first, stop)
-            for r in range(ROW_BLOCKS):
-                nc.vector.tensor_tensor(tile[:, r, :], y[r][:].indirect(entries), gates[s][:, first * P : stop * P], ALU.mult)
+        def gather_gated(s, first, stop, rows=range(ROW_BLOCKS)):
+            tile, entries = new_gated(s, first, stop, rows)
+            for n, r in enumerate(rows):
+                nc.vector.tensor_tensor(tile[:, n, :], y[r][:].indirect(entries), gates[s][:, first * P : stop * P], ALU.mult)
 
-        def gather_plain(s, first, stop):
-            tile, entries = new_gated(s, first, stop)
-            for r in range(ROW_BLOCKS):
-                nc.scalar.activation(tile[:, r, :], y[r][:].indirect(entries), ACT.Copy)
+        def gather_plain(s, first, stop, rows=range(ROW_BLOCKS)):
+            tile, entries = new_gated(s, first, stop, rows)
+            for n, r in enumerate(rows):
+                nc.scalar.activation(tile[:, n, :], y[r][:].indirect(entries), ACT.Copy)
 
         def apply_gate(s, first, stop):
-            wide = gates[s][:, first * P : stop * P].unsqueeze(1).to_broadcast([P, ROW_BLOCKS, (stop - first) * P])
-            nc.vector.tensor_tensor(gated[s, first][:], gated[s, first][:], wide, ALU.mult)
+            tile = gated[s, first]
+            wide = gates[s][:, first * P : stop * P].unsqueeze(1).to_broadcast(tile.shape)
+            nc.vector.tensor_tensor(tile[:], tile[:], wide, ALU.mult)
 
         def turn(s, first, stop):
             for b in range(first, stop):
-                if s == 0:
+                opens = b not in dh_t
+                if opens:
                     dh_t[b] = bank(dh_bank[b], [P, H])
                 for r in range(ROW_BLOCKS):
                     nc.tensor.matmul(
                         block_columns(dh_t[b], r),
-                        lhsT=block[s, b][:, r, :],
+                        lhsT=block[s, b, r],
                         rhs=ident[:],
-                        start=(s == 0 and r == 0),
-                        stop=(s == 1 and r == ROW_BLOCKS - 1),
+                        start=(opens and r == 0),
+                        stop=(not opens and r == ROW_BLOCKS - 1),
                         is_transpose=True,
                     )
 
@@ -250,9 +254,10 @@ def tile_moe_sub_silu_kernel(
             nc.sync.dma_start(out_rows[:, :, tokens(c)], res[:])
 
         gather_gated(1, 2, 4)
-        gather_gated(0, 0, 6)
-        turn(0, 2, 4)
+        gather_gated(0, 0, 4)
+        gather_gated(0, 4, 6)
         turn(1, 2, 4)
+        turn(0, 2, 4)
         turn(0, 0, 2)
         turn(0, 4, 6)
         gather_plain(1, 4, 6)

@@ -86,13 +86,13 @@ def tile_moe_sub_silu_kernel(
         load_dy_scales(nc.sync, 1)
         load_dy_scales(nc.scalar, 2)
         load_dy_scales(nc.scalar, 3)
-        load_a(3)
+        load_a(1)
         load_dy_words()
         load_w2_first()
-        load_a(0)
         load_w2_rest()
-        load_a(1)
         load_a(2)
+        load_a(3)
+        load_a(0)
         for s, lst in enumerate((pos1, pos2)):
             nc.sync.dma_start(token_slots[s][:], lst)
         for s in range(2):
@@ -110,33 +110,38 @@ def tile_moe_sub_silu_kernel(
                 nc.tensor.transpose(block_columns(a_turned, r), a_sb[b // 2][:, r, b % 2 * P : (b % 2 + 1) * P], ident[:])
             return a_turned
 
-        sig = keep.tile([P, TOKEN_TILES, H], F32, name="sig")
-        neg_ds = keep.tile([P, TOKEN_TILES, H], F32, name="neg_ds")
-        a_turned = {}
+        half_tanh = {}
+        neg_silu = {}
 
-        def sigmoid(b, place):
-            a_turned[b] = turn_a(b, place)
-            nc.scalar.activation(sig[:, b, :], a_turned[b][:], ACT.Sigmoid)
+        def activate(first, stop):
+            for b in range(first, stop):
+                a_turned = turn_a(b, (0, 1, 0, 1, 2, 3, 0, 1)[b])
+                half_tanh[b] = keep.tile([P, H], F32, name=f"half_tanh{b}")
+                neg_silu[b] = keep.tile([P, H], F32, name=f"neg_silu{b}")
+                nc.scalar.activation(neg_silu[b][:], a_turned[:], ACT.Silu, scale=-1.0)
+                nc.scalar.activation(half_tanh[b][:], a_turned[:], ACT.Tanh, scale=0.5)
 
-        late = (2, 3, 4, 5)
-        early = (6, 7, 0, 1)
-        sigmoid(6, 0)
-        sigmoid(7, 1)
+        activate(2, 4)
 
         y = [keep.tile([P, E * C], F32, name=f"y{r}") for r in range(ROW_BLOCKS)]
-        emptied_by_vector = ((3, 1), (3, 2), (3, 3))
+        emptied_by_vector = ((3, 0),)
+        sums_of = {}
+
+        def empty(e, r):
+            if (e, r) in emptied_by_vector:
+                nc.vector.tensor_copy(y[r][:, e * C : (e + 1) * C], sums_of[e, r][:])
+            else:
+                nc.scalar.copy(y[r][:, e * C : (e + 1) * C], sums_of[e, r][:])
+
         for e in range(E):
             entries = slot_tokens[:, e * C // PER_COL : (e + 1) * C // PER_COL]
             g_s = keep.tile([P, C], U8, name=f"g_s{e % 2}", align_bytes=64)
             g_w = keep.tile([P, C], U32, name=f"g_w{e}", align_bytes=64)
             nc.vector.tensor_copy(g_s[:], dy_s[:].indirect(entries))
             nc.vector.tensor_copy(g_w[:], dy_w[:].bitcast(U32).indirect(entries))
-            if e == 1:
-                sigmoid(0, 6)
-                sigmoid(1, 7)
             words = w2_first[:, 0, :] if e == 0 else w2_rest[:, e - 1, :]
             for r in range(ROW_BLOCKS):
-                y_sums = bank(((2, 3, 4, 5), (0, 1, 2, 3), (4, 5, 6, 7), (0, 1, 2, 3))[e][r], [P, C])
+                y_sums = bank(((2, 3, 4, 5), (6, 7, 0, 1), (2, 3, 4, 5), (6, 7, 0, 1))[e][r], [P, C])
                 nc.tensor.matmul_mx(
                     y_sums[:],
                     lhsT=words[:, 2 * P * r : 2 * P * (r + 1)].bitcast(E2M1),
@@ -146,26 +151,23 @@ def tile_moe_sub_silu_kernel(
                     start=True,
                     stop=True,
                 )
-                if (e, r) in emptied_by_vector:
-                    nc.vector.tensor_copy(y[r][:, e * C : (e + 1) * C], y_sums[:])
-                else:
-                    nc.scalar.copy(y[r][:, e * C : (e + 1) * C], y_sums[:])
-
-        a_bank = dict(zip(late + early, (4, 5, 6, 7, 0, 1, 2, 3)))
-        for b in late:
-            sigmoid(b, a_bank[b])
-        for b in late + early:
-            if b in early:
-                a_turned[b] = turn_a(b, a_bank[b])
-            nc.scalar.activation(neg_ds[:, b, :], a_turned[b][:], ACT.Silu, scale=-1.0)
+                sums_of[e, r] = y_sums
+                if e < E - 2:
+                    empty(e, r)
+        slope_first = keep.tile([P, H], F32, name="dy_s", align_bytes=64)
+        nc.vector.tensor_scalar(slope_first[:], half_tanh[2][:], 1.0, None, ALU.add)
+        nc.vector.scalar_tensor_tensor(neg_silu[2][:], neg_silu[2][:], 1.0, slope_first[:], ALU.subtract, ALU.mult)
+        for r in range(ROW_BLOCKS):
+            for e in (E - 2, E - 1):
+                empty(e, r)
 
         da_w = keep.tile([P, T], U32, name="da_w", align_bytes=64)
         da_s = keep.tile([P, T], U8, name="da_s", align_bytes=64)
         out_rows = out.rearrange("(kb p) t -> p kb t", p=P)
         chunks = (range(2, 4), range(4, 6), range(6, 8), range(0, 1), range(1, 2))
-        dh_bank = (6, 7, 4, 5, 0, 1, 2, 3)
-        back_bank = (4, 0, 2, 4, 6)
-        out_bank = (5, 1, 3, 5, 7)
+        dh_bank = (6, 7, 4, 5, 6, 7, 2, 3)
+        back_bank = (4, 5, 2, 4, 0)
+        out_bank = (4, 5, 3, 2, 1)
         gated = {}
         block = {}
         dh_t = {}
@@ -212,10 +214,9 @@ def tile_moe_sub_silu_kernel(
                         is_transpose=True,
                     )
 
-        def slope(first, stop):
-            nc.vector.scalar_tensor_tensor(
-                neg_ds[:, first:stop, :], neg_ds[:, first:stop, :], 1.0, sig[:, first:stop, :], ALU.subtract, ALU.mult
-            )
+        def first_factor(first, stop):
+            for b in range(first, stop):
+                nc.vector.scalar_tensor_tensor(neg_silu[b][:], neg_silu[b][:], 1.0, dh_t[b][:], ALU.subtract, ALU.mult)
 
         def turn_back(c):
             width = len(chunks[c])
@@ -223,7 +224,10 @@ def tile_moe_sub_silu_kernel(
             turned = bank(back_bank[c], [P, width, 2, P])
             for n, b in enumerate(chunks[c]):
                 da_t = keep.tile([P, H], BF16, name=f"da_t{b}")
-                nc.vector.scalar_tensor_tensor(da_t[:], dh_t[b][:], -1.0, neg_ds[:, b, :], ALU.mult, ALU.mult)
+                if b == 2:
+                    nc.vector.tensor_tensor(da_t[:], neg_silu[b][:], dh_t[b][:], ALU.mult)
+                else:
+                    nc.vector.scalar_tensor_tensor(da_t[:], half_tanh[b][:], 1.0, neg_silu[b][:], ALU.add, ALU.mult)
                 pairs = da_t[:].bitcast(F32)
                 for u in range(2):
                     nc.tensor.transpose(turned[:, n, u, :], pairs[:, u * P : (u + 1) * P], ident[:])
@@ -247,44 +251,48 @@ def tile_moe_sub_silu_kernel(
                     stop=True,
                 )
             res = keep.tile([P, K // P, width], F32, name=f"res{c}")
-            if c in (4,):
-                nc.vector.tensor_copy(res[:], sums[:])
+            if c in (2, 4):
+                nc.vector.tensor_scalar(res[:], sums[:], -0.5, None, ALU.mult)
             else:
-                nc.scalar.copy(res[:], sums[:])
+                nc.scalar.activation(res[:], sums[:], ACT.Copy, scale=-0.5)
             nc.sync.dma_start(out_rows[:, :, tokens(c)], res[:])
 
         gather_gated(1, 2, 4)
-        gather_gated(0, 0, 4)
-        gather_gated(0, 4, 6)
+        gather_gated(0, 0, 6, range(0, 3))
+        gather_gated(0, 0, 4, range(3, 4))
         turn(1, 2, 4)
         turn(0, 2, 4)
-        turn(0, 0, 2)
-        turn(0, 4, 6)
+        gather_plain(0, 4, 6, range(3, 4))
         gather_plain(1, 4, 6)
+        activate(4, 6)
         gather_plain(0, 6, 8)
         gather_plain(1, 6, 8)
-        slope(2, 6)
-        turn_back(0)
-        gather_plain(1, 0, 1)
-        gather_plain(1, 1, 2)
+        gather_plain(1, 0, 2)
+        activate(6, 8)
+        apply_gate(0, 4, 6)
+        turn(0, 4, 6)
         apply_gate(1, 4, 6)
         turn(1, 4, 6)
-        slope(6, 8)
+        first_factor(3, 4)
+        turn_back(0)
         apply_gate(0, 6, 8)
         turn(0, 6, 8)
-        slope(0, 2)
-        turn_back(1)
         apply_gate(1, 6, 8)
         turn(1, 6, 8)
-        apply_gate(1, 0, 1)
-        turn(1, 0, 1)
-        finish(0)
-        apply_gate(1, 1, 2)
-        turn(1, 1, 2)
+        activate(0, 2)
+        first_factor(4, 6)
+        turn_back(1)
+        apply_gate(1, 0, 2)
+        turn(0, 0, 2)
+        turn(1, 0, 2)
+        first_factor(6, 8)
         turn_back(2)
+        finish(0)
+        first_factor(0, 1)
         finish(1)
+        first_factor(1, 2)
+        finish(2)
         turn_back(3)
         turn_back(4)
-        finish(2)
         finish(3)
         finish(4)

@@ -49,7 +49,7 @@ def tile_moe_sub_silu_kernel(
         w1_s = keep.tile([P, K], U8, name="w1_s", align_bytes=64)
         w1_w = keep.tile([P, 2 * K], U8, name="w1_w", align_bytes=64)
         gates = [keep.tile([P, T], F32, name=f"gates{s}") for s in range(2)]
-        a_sb = [keep.tile([P, ROW_BLOCKS, 2 * P], F32, name=f"a_sb{c}") for c in range(TOKEN_TILES // 2)]
+        a_sb = {}
         ident = keep.tile([P, P], F32, name="ident")
 
         nc.vector.memset(w2_s[:].bitcast(I32), 0)
@@ -67,8 +67,11 @@ def tile_moe_sub_silu_kernel(
         w1_rows = w1t_scales[0].rearrange("(q j) k -> j q k", j=SCALE_ROWS)
         a_rows = a.rearrange("(r q) t -> q r t", q=P)
 
-        def load_a(pair):
-            nc.sync.dma_start(a_sb[pair][:], a_rows[:, :, pair * 2 * P : (pair + 1) * 2 * P])
+        def load_a(first, stop):
+            piece = keep.tile([P, ROW_BLOCKS, (stop - first) * P], F32, name=f"a_sb{first}")
+            nc.sync.dma_start(piece[:], a_rows[:, :, first * P : stop * P])
+            for b in range(first, stop):
+                a_sb[b] = piece[:, :, (b - first) * P : (b - first + 1) * P]
 
         def load_dy_words():
             nc.sync.dma_start(dy_w[:], dy_words[0].rearrange("p t d -> p (t d)").bitcast(I32))
@@ -86,13 +89,14 @@ def tile_moe_sub_silu_kernel(
         load_dy_scales(nc.sync, 1)
         load_dy_scales(nc.scalar, 2)
         load_dy_scales(nc.scalar, 3)
-        load_a(1)
+        load_a(2, 3)
+        load_a(3, 4)
         load_dy_words()
+        load_a(4, 5)
         load_w2_first()
         load_w2_rest()
-        load_a(2)
-        load_a(3)
-        load_a(0)
+        load_a(5, 8)
+        load_a(0, 2)
         for s, lst in enumerate((pos1, pos2)):
             nc.sync.dma_start(token_slots[s][:], lst)
         for s in range(2):
@@ -107,24 +111,32 @@ def tile_moe_sub_silu_kernel(
         def turn_a(b, place):
             a_turned = bank(place, [P, H])
             for r in range(ROW_BLOCKS):
-                nc.tensor.transpose(block_columns(a_turned, r), a_sb[b // 2][:, r, b % 2 * P : (b % 2 + 1) * P], ident[:])
+                nc.tensor.transpose(block_columns(a_turned, r), a_sb[b][:, r, :], ident[:])
             return a_turned
 
         half_tanh = {}
         neg_silu = {}
 
+        a_turned = {}
+
+        def silu(b):
+            a_turned[b] = turn_a(b, (3, 5, 0, 1, 6, 3, 3, 5)[b])
+            neg_silu[b] = keep.tile([P, H], F32, name=f"neg_silu{b}")
+            nc.scalar.activation(neg_silu[b][:], a_turned[b][:], ACT.Silu, scale=-1.0)
+
+        def tanh(b):
+            half_tanh[b] = keep.tile([P, H], F32, name=f"half_tanh{b}")
+            nc.scalar.activation(half_tanh[b][:], a_turned[b][:], ACT.Tanh, scale=0.5)
+
         def activate(first, stop):
             for b in range(first, stop):
-                a_turned = turn_a(b, (0, 1, 0, 1, 2, 3, 0, 1)[b])
-                half_tanh[b] = keep.tile([P, H], F32, name=f"half_tanh{b}")
-                neg_silu[b] = keep.tile([P, H], F32, name=f"neg_silu{b}")
-                nc.scalar.activation(neg_silu[b][:], a_turned[:], ACT.Silu, scale=-1.0)
-                nc.scalar.activation(half_tanh[b][:], a_turned[:], ACT.Tanh, scale=0.5)
+                silu(b)
+                tanh(b)
 
-        activate(2, 4)
+        activate(2, 5)
 
         y = [keep.tile([P, E * C], F32, name=f"y{r}") for r in range(ROW_BLOCKS)]
-        emptied_by_vector = ((3, 0),)
+        emptied_by_vector = ()
         sums_of = {}
 
         def empty(e, r):
@@ -154,20 +166,23 @@ def tile_moe_sub_silu_kernel(
                 sums_of[e, r] = y_sums
                 if e < E - 2:
                     empty(e, r)
-        slope_first = keep.tile([P, H], F32, name="dy_s", align_bytes=64)
-        nc.vector.tensor_scalar(slope_first[:], half_tanh[2][:], 1.0, None, ALU.add)
-        nc.vector.scalar_tensor_tensor(neg_silu[2][:], neg_silu[2][:], 1.0, slope_first[:], ALU.subtract, ALU.mult)
-        for r in range(ROW_BLOCKS):
+        slope_first = keep.tile([P, 2, H], F32, name="dy_s", align_bytes=64)
+        for b in (2, 3):
+            nc.vector.tensor_scalar(slope_first[:, b - 2, :], half_tanh[b][:], 1.0, None, ALU.add)
+        for b in (2, 3):
+            nc.vector.scalar_tensor_tensor(neg_silu[b][:], neg_silu[b][:], 1.0, slope_first[:, b - 2, :], ALU.subtract, ALU.mult)
+        for half in range(2):
             for e in (E - 2, E - 1):
-                empty(e, r)
+                for r in (2 * half, 2 * half + 1):
+                    empty(e, r)
 
         da_w = keep.tile([P, T], U32, name="da_w", align_bytes=64)
         da_s = keep.tile([P, T], U8, name="da_s", align_bytes=64)
         out_rows = out.rearrange("(kb p) t -> p kb t", p=P)
         chunks = (range(2, 4), range(4, 6), range(6, 8), range(0, 1), range(1, 2))
-        dh_bank = (6, 7, 4, 5, 6, 7, 2, 3)
-        back_bank = (4, 5, 2, 4, 0)
-        out_bank = (4, 5, 3, 2, 1)
+        dh_bank = (0, 1, 4, 5, 6, 7, 4, 2)
+        back_bank = (6, 7, 4, 0, 1)
+        out_bank = (6, 2, 3, 7, 4)
         gated = {}
         block = {}
         dh_t = {}
@@ -224,7 +239,7 @@ def tile_moe_sub_silu_kernel(
             turned = bank(back_bank[c], [P, width, 2, P])
             for n, b in enumerate(chunks[c]):
                 da_t = keep.tile([P, H], BF16, name=f"da_t{b}")
-                if b == 2:
+                if b in (2, 3):
                     nc.vector.tensor_tensor(da_t[:], neg_silu[b][:], dh_t[b][:], ALU.mult)
                 else:
                     nc.vector.scalar_tensor_tensor(da_t[:], half_tanh[b][:], 1.0, neg_silu[b][:], ALU.add, ALU.mult)
@@ -262,28 +277,30 @@ def tile_moe_sub_silu_kernel(
         gather_gated(0, 0, 4, range(3, 4))
         turn(1, 2, 4)
         turn(0, 2, 4)
+        turn(0, 0, 2)
         gather_plain(0, 4, 6, range(3, 4))
         gather_plain(1, 4, 6)
-        activate(4, 6)
         gather_plain(0, 6, 8)
         gather_plain(1, 6, 8)
+        activate(5, 6)
         gather_plain(1, 0, 2)
         activate(6, 8)
         apply_gate(0, 4, 6)
         turn(0, 4, 6)
         apply_gate(1, 4, 6)
         turn(1, 4, 6)
-        first_factor(3, 4)
-        turn_back(0)
         apply_gate(0, 6, 8)
         turn(0, 6, 8)
         apply_gate(1, 6, 8)
         turn(1, 6, 8)
-        activate(0, 2)
+        turn_back(0)
+        silu(0)
+        silu(1)
         first_factor(4, 6)
         turn_back(1)
+        tanh(0)
+        tanh(1)
         apply_gate(1, 0, 2)
-        turn(0, 0, 2)
         turn(1, 0, 2)
         first_factor(6, 8)
         turn_back(2)
@@ -291,8 +308,8 @@ def tile_moe_sub_silu_kernel(
         first_factor(0, 1)
         finish(1)
         first_factor(1, 2)
-        finish(2)
         turn_back(3)
+        finish(2)
         turn_back(4)
         finish(3)
         finish(4)

@@ -120,7 +120,7 @@ def tile_moe_sub_silu_kernel(
         a_turned = {}
 
         def silu(b):
-            a_turned[b] = turn_a(b, (3, 5, 0, 1, 6, 3, 3, 5)[b])
+            a_turned[b] = turn_a(b, (2, 3, 0, 1, 6, 3, 2, 3)[b])
             neg_silu[b] = keep.tile([P, H], F32, name=f"neg_silu{b}")
             nc.scalar.activation(neg_silu[b][:], a_turned[b][:], ACT.Silu, scale=-1.0)
 
@@ -180,9 +180,9 @@ def tile_moe_sub_silu_kernel(
         da_s = keep.tile([P, T], U8, name="da_s", align_bytes=64)
         out_rows = out.rearrange("(kb p) t -> p kb t", p=P)
         chunks = (range(2, 4), range(4, 6), range(6, 8), range(0, 1), range(1, 2))
-        dh_bank = (0, 1, 4, 5, 6, 7, 4, 2)
+        dh_bank = (0, 1, 4, 5, 6, 7, 4, 5)
         back_bank = (6, 7, 4, 0, 1)
-        out_bank = (6, 2, 3, 7, 4)
+        out_bank = (6, 5, 2, 7, 4)
         gated = {}
         block = {}
         dh_t = {}
@@ -289,11 +289,11 @@ def tile_moe_sub_silu_kernel(
         turn(0, 4, 6)
         apply_gate(1, 4, 6)
         turn(1, 4, 6)
+        turn_back(0)
         apply_gate(0, 6, 8)
         turn(0, 6, 8)
         apply_gate(1, 6, 8)
         turn(1, 6, 8)
-        turn_back(0)
         silu(0)
         silu(1)
         first_factor(4, 6)

@@ -3,9 +3,6 @@ from contextlib import ExitStack
 import concourse.mybir as mybir
 from concourse.masks import make_identity
 
-K, T, E, C, H, N = 256, 1024, 4, 512, 512, 512
-FLOPS = 2 * N * H * E * C + 2 * H * K * T
-
 F32 = mybir.dt.float32
 BF16 = mybir.dt.bfloat16
 I32 = mybir.dt.int32
@@ -17,14 +14,17 @@ E2M1 = mybir.dt.float4_e2m1fn_x4
 ACT = mybir.ActivationFunctionType
 ALU = mybir.AluOpType
 
+K, T, E, C, H, N = 256, 1024, 4, 512, 512, 512
+FLOPS = 2 * N * H * E * C + 2 * H * K * T
 P = 128
 PACK = 4
+PER_COL = 16
 QUADRANT = 32
 SCALE_ROWS = 4
-PER_COL = 16
 BANKS = 8
 ROW_BLOCKS = H // P
-TOKEN_TILES = T // P
+ALL_ROWS = range(ROW_BLOCKS)
+CHUNKS = (range(2, 4), range(4, 6), range(6, 8), range(0, 1), range(1, 2))
 
 
 def tile_moe_sub_silu_kernel(
@@ -36,8 +36,16 @@ def tile_moe_sub_silu_kernel(
         keep = ctx.enter_context(tc.tile_pool(name="keep", bufs=1))
         psum = ctx.enter_context(tc.psum_pool(name="psum", bufs=1))
 
-        def bank(place, shape):
-            return psum.tile(shape, F32, name=f"bank{place % BANKS}")
+        bank_of = {}
+        ring = []
+
+        def bank(tenant, shape, after=None):
+            if after is None:
+                bank_of[tenant] = len(ring) % BANKS
+                ring.append(tenant)
+            else:
+                bank_of[tenant] = bank_of[after]
+            return psum.tile(shape, F32, name=f"bank{bank_of[tenant]}")
 
         slot_tokens = keep.tile([P, E * C // PER_COL], U16, name="slot_tokens")
         token_slots = [keep.tile([P, T // PER_COL], U16, name=f"token_slots{s}") for s in range(2)]
@@ -49,23 +57,16 @@ def tile_moe_sub_silu_kernel(
         w1_s = keep.tile([P, K], U8, name="w1_s", align_bytes=64)
         w1_w = keep.tile([P, 2 * K], U8, name="w1_w", align_bytes=64)
         gates = [keep.tile([P, T], F32, name=f"gates{s}") for s in range(2)]
-        a_sb = {}
         ident = keep.tile([P, P], F32, name="ident")
 
         nc.vector.memset(w2_s[:].bitcast(I32), 0)
         nc.vector.memset(w1_s[:].bitcast(I32), 0)
         make_identity(nc, ident[:])
 
-        def load_dy_scales(queue, q):
-            rows = dy_scales[0, SCALE_ROWS * q : SCALE_ROWS * (q + 1), :].bitcast(I32)
-            queue.dma_start(
-                dy_s[QUADRANT * q : QUADRANT * (q + 1), :].bitcast(I32),
-                rows.unsqueeze(0).to_broadcast([QUADRANT // SCALE_ROWS, SCALE_ROWS, T // 4]),
-            )
-
         w2_rows = w2t_scales[:, 0].rearrange("e (q j) i -> j q e i", j=SCALE_ROWS)
         w1_rows = w1t_scales[0].rearrange("(q j) k -> j q k", j=SCALE_ROWS)
         a_rows = a.rearrange("(r q) t -> q r t", q=P)
+        a_sb = {}
 
         def load_a(first, stop):
             piece = keep.tile([P, ROW_BLOCKS, (stop - first) * P], F32, name=f"a_sb{first}")
@@ -73,28 +74,21 @@ def tile_moe_sub_silu_kernel(
             for b in range(first, stop):
                 a_sb[b] = piece[:, :, (b - first) * P : (b - first + 1) * P]
 
-        def load_dy_words():
-            nc.sync.dma_start(dy_w[:], dy_words[0].rearrange("p t d -> p (t d)").bitcast(I32))
-
-        def load_w2_first():
-            nc.sync.dma_start(w2_first[:].bitcast(I32), w2t_words[0:1, 0].rearrange("e p b -> p e b").bitcast(I32))
-            for j in range(SCALE_ROWS):
-                nc.sync.dma_start(w2_s[j:P:QUADRANT, :, :].bitcast(I32), w2_rows[j].bitcast(I32))
-
-        def load_w2_rest():
-            nc.sync.dma_start(w2_rest[:].bitcast(I32), w2t_words[1:E, 0].rearrange("e p b -> p e b").bitcast(I32))
-
         nc.sync.dma_start(slot_tokens[:], offs)
-        load_dy_scales(nc.sync, 0)
-        load_dy_scales(nc.sync, 1)
-        load_dy_scales(nc.scalar, 2)
-        load_dy_scales(nc.scalar, 3)
+        for q in range(P // QUADRANT):
+            rows = dy_scales[0, SCALE_ROWS * q : SCALE_ROWS * (q + 1), :].bitcast(I32)
+            (nc.sync if q < 2 else nc.scalar).dma_start(
+                dy_s[QUADRANT * q : QUADRANT * (q + 1), :].bitcast(I32),
+                rows.unsqueeze(0).to_broadcast([QUADRANT // SCALE_ROWS, SCALE_ROWS, T // 4]),
+            )
         load_a(2, 3)
         load_a(3, 4)
-        load_dy_words()
+        nc.sync.dma_start(dy_w[:], dy_words[0].rearrange("p t d -> p (t d)").bitcast(I32))
         load_a(4, 5)
-        load_w2_first()
-        load_w2_rest()
+        nc.sync.dma_start(w2_first[:].bitcast(I32), w2t_words[0:1, 0].rearrange("e p b -> p e b").bitcast(I32))
+        for j in range(SCALE_ROWS):
+            nc.sync.dma_start(w2_s[j:P:QUADRANT, :, :].bitcast(I32), w2_rows[j].bitcast(I32))
+        nc.sync.dma_start(w2_rest[:].bitcast(I32), w2t_words[1:E, 0].rearrange("e p b -> p e b").bitcast(I32))
         load_a(5, 8)
         load_a(0, 2)
         for s, lst in enumerate((pos1, pos2)):
@@ -108,19 +102,14 @@ def tile_moe_sub_silu_kernel(
         def block_columns(tile, r):
             return tile[:].rearrange("t (u r q d) -> t r q u d", u=2, r=ROW_BLOCKS, d=2)[:, r]
 
-        def turn_a(b, place):
-            a_turned = bank(place, [P, H])
-            for r in range(ROW_BLOCKS):
-                nc.tensor.transpose(block_columns(a_turned, r), a_sb[b][:, r, :], ident[:])
-            return a_turned
+        a_turned, neg_silu, half_tanh = {}, {}, {}
 
-        half_tanh = {}
-        neg_silu = {}
-
-        a_turned = {}
+        def turn_a(b, after=None):
+            a_turned[b] = bank(("a", b), [P, H], after)
+            for r in ALL_ROWS:
+                nc.tensor.transpose(block_columns(a_turned[b], r), a_sb[b][:, r, :], ident[:])
 
         def silu(b):
-            a_turned[b] = turn_a(b, (2, 3, 0, 1, 6, 3, 2, 3)[b])
             neg_silu[b] = keep.tile([P, H], F32, name=f"neg_silu{b}")
             nc.scalar.activation(neg_silu[b][:], a_turned[b][:], ACT.Silu, scale=-1.0)
 
@@ -128,118 +117,119 @@ def tile_moe_sub_silu_kernel(
             half_tanh[b] = keep.tile([P, H], F32, name=f"half_tanh{b}")
             nc.scalar.activation(half_tanh[b][:], a_turned[b][:], ACT.Tanh, scale=0.5)
 
-        def activate(first, stop):
-            for b in range(first, stop):
-                silu(b)
-                tanh(b)
+        def activate(b, after=None):
+            turn_a(b, after)
+            silu(b)
+            tanh(b)
 
-        activate(2, 5)
+        for b in (2, 3, 4):
+            activate(b)
 
-        y = [keep.tile([P, E * C], F32, name=f"y{r}") for r in range(ROW_BLOCKS)]
-        emptied_by_vector = ()
-        sums_of = {}
+        y = [keep.tile([P, E * C], F32, name=f"y{r}") for r in ALL_ROWS]
+        g_s, g_w = {}, {}
 
-        def empty(e, r):
-            if (e, r) in emptied_by_vector:
-                nc.vector.tensor_copy(y[r][:, e * C : (e + 1) * C], sums_of[e, r][:])
-            else:
-                nc.scalar.copy(y[r][:, e * C : (e + 1) * C], sums_of[e, r][:])
-
-        for e in range(E):
+        def gather_slots(e):
             entries = slot_tokens[:, e * C // PER_COL : (e + 1) * C // PER_COL]
-            g_s = keep.tile([P, C], U8, name=f"g_s{e % 2}", align_bytes=64)
-            g_w = keep.tile([P, C], U32, name=f"g_w{e}", align_bytes=64)
-            nc.vector.tensor_copy(g_s[:], dy_s[:].indirect(entries))
-            nc.vector.tensor_copy(g_w[:], dy_w[:].bitcast(U32).indirect(entries))
+            g_s[e] = keep.tile([P, C], U8, name=f"g_s{e % 2}", align_bytes=64)
+            g_w[e] = keep.tile([P, C], U32, name=f"g_w{e}", align_bytes=64)
+            nc.vector.tensor_copy(g_s[e][:], dy_s[:].indirect(entries))
+            nc.vector.tensor_copy(g_w[e][:], dy_w[:].bitcast(U32).indirect(entries))
+
+        def expert_pass(e, r):
             words = w2_first[:, 0, :] if e == 0 else w2_rest[:, e - 1, :]
-            for r in range(ROW_BLOCKS):
-                y_sums = bank(((2, 3, 4, 5), (6, 7, 0, 1), (2, 3, 4, 5), (6, 7, 0, 1))[e][r], [P, C])
-                nc.tensor.matmul_mx(
-                    y_sums[:],
-                    lhsT=words[:, 2 * P * r : 2 * P * (r + 1)].bitcast(E2M1),
-                    lhsT_scale=w2_s[:, e, P * r : P * (r + 1)],
-                    rhs=g_w[:].bitcast(E5M2),
-                    rhs_scale=g_s[:],
-                    start=True,
-                    stop=True,
-                )
-                sums_of[e, r] = y_sums
-                if e < E - 2:
-                    empty(e, r)
-        slope_first = keep.tile([P, 2, H], F32, name="dy_s", align_bytes=64)
-        for b in (2, 3):
-            nc.vector.tensor_scalar(slope_first[:, b - 2, :], half_tanh[b][:], 1.0, None, ALU.add)
-        for b in (2, 3):
-            nc.vector.scalar_tensor_tensor(neg_silu[b][:], neg_silu[b][:], 1.0, slope_first[:, b - 2, :], ALU.subtract, ALU.mult)
+            sums = bank(("y", e, r), [P, C])
+            nc.tensor.matmul_mx(
+                sums[:],
+                lhsT=words[:, 2 * P * r : 2 * P * (r + 1)].bitcast(E2M1),
+                lhsT_scale=w2_s[:, e, P * r : P * (r + 1)],
+                rhs=g_w[e][:].bitcast(E5M2),
+                rhs_scale=g_s[e][:],
+                start=True,
+                stop=True,
+            )
+            nc.scalar.copy(y[r][:, e * C : (e + 1) * C], sums[:])
+
+        for e in range(E - 2):
+            gather_slots(e)
+            for r in ALL_ROWS:
+                expert_pass(e, r)
+        for e in range(E - 2, E):
+            gather_slots(e)
+
+        tanh_plus_one = keep.tile([P, len(CHUNKS[0]), H], F32, name="dy_s", align_bytes=64)
+        for n, b in enumerate(CHUNKS[0]):
+            nc.vector.tensor_scalar(tanh_plus_one[:, n, :], half_tanh[b][:], 1.0, None, ALU.add)
+        for n, b in enumerate(CHUNKS[0]):
+            nc.vector.scalar_tensor_tensor(
+                neg_silu[b][:], neg_silu[b][:], 1.0, tanh_plus_one[:, n, :], ALU.subtract, ALU.mult
+            )
+
         for half in range(2):
-            for e in (E - 2, E - 1):
+            for e in range(E - 2, E):
                 for r in (2 * half, 2 * half + 1):
-                    empty(e, r)
+                    expert_pass(e, r)
 
         da_w = keep.tile([P, T], U32, name="da_w", align_bytes=64)
         da_s = keep.tile([P, T], U8, name="da_s", align_bytes=64)
         out_rows = out.rearrange("(kb p) t -> p kb t", p=P)
-        chunks = (range(2, 4), range(4, 6), range(6, 8), range(0, 1), range(1, 2))
-        dh_bank = (0, 1, 4, 5, 6, 7, 4, 5)
-        back_bank = (6, 7, 4, 0, 1)
-        out_bank = (6, 5, 2, 7, 4)
-        gated = {}
-        block = {}
-        dh_t = {}
-        da = {}
+        picked, block, dh_t, da = {}, {}, {}, {}
 
-        def tokens(c):
-            return slice(chunks[c].start * P, chunks[c].stop * P)
-
-        def new_gated(s, first, stop, rows):
-            name = f"gated{s}_{first}_{rows.start}"
-            gated[s, first] = keep.tile([P, len(rows), (stop - first) * P], F32, name=name)
+        def new_picked(s, first, stop, rows):
+            tile = keep.tile([P, len(rows), (stop - first) * P], F32, name=f"picked{s}_{first}_{rows.start}")
+            picked[s, first] = tile
             for b in range(first, stop):
                 for n, r in enumerate(rows):
-                    block[s, b, r] = gated[s, first][:, n, (b - first) * P : (b - first + 1) * P]
-            return gated[s, first], token_slots[s][:, first * P // PER_COL : stop * P // PER_COL]
+                    block[s, b, r] = tile[:, n, (b - first) * P : (b - first + 1) * P]
+            return tile, token_slots[s][:, first * P // PER_COL : stop * P // PER_COL]
 
-        def gather_gated(s, first, stop, rows=range(ROW_BLOCKS)):
-            tile, entries = new_gated(s, first, stop, rows)
+        def gather_gated(s, first, stop, rows=ALL_ROWS):
+            tile, entries = new_picked(s, first, stop, rows)
             for n, r in enumerate(rows):
-                nc.vector.tensor_tensor(tile[:, n, :], y[r][:].indirect(entries), gates[s][:, first * P : stop * P], ALU.mult)
+                nc.vector.tensor_tensor(
+                    tile[:, n, :], y[r][:].indirect(entries), gates[s][:, first * P : stop * P], ALU.mult
+                )
 
-        def gather_plain(s, first, stop, rows=range(ROW_BLOCKS)):
-            tile, entries = new_gated(s, first, stop, rows)
+        def gather_plain(s, first, stop, rows=ALL_ROWS):
+            tile, entries = new_picked(s, first, stop, rows)
             for n, r in enumerate(rows):
                 nc.scalar.activation(tile[:, n, :], y[r][:].indirect(entries), ACT.Copy)
 
         def apply_gate(s, first, stop):
-            tile = gated[s, first]
+            tile = picked[s, first]
             wide = gates[s][:, first * P : stop * P].unsqueeze(1).to_broadcast(tile.shape)
             nc.vector.tensor_tensor(tile[:], tile[:], wide, ALU.mult)
 
+        def open_dh(b, after=None):
+            dh_t[b] = bank(("dh", b), [P, H], after)
+
+        opened = set()
+
         def turn(s, first, stop):
             for b in range(first, stop):
-                opens = b not in dh_t
-                if opens:
-                    dh_t[b] = bank(dh_bank[b], [P, H])
-                for r in range(ROW_BLOCKS):
+                for r in ALL_ROWS:
                     nc.tensor.matmul(
                         block_columns(dh_t[b], r),
                         lhsT=block[s, b, r],
                         rhs=ident[:],
-                        start=(opens and r == 0),
-                        stop=(not opens and r == ROW_BLOCKS - 1),
+                        start=(b not in opened and r == 0),
+                        stop=(b in opened and r == ROW_BLOCKS - 1),
                         is_transpose=True,
                     )
+                opened.add(b)
 
         def first_factor(first, stop):
             for b in range(first, stop):
-                nc.vector.scalar_tensor_tensor(neg_silu[b][:], neg_silu[b][:], 1.0, dh_t[b][:], ALU.subtract, ALU.mult)
+                nc.vector.scalar_tensor_tensor(
+                    neg_silu[b][:], neg_silu[b][:], 1.0, dh_t[b][:], ALU.subtract, ALU.mult
+                )
 
-        def turn_back(c):
-            width = len(chunks[c])
+        def turn_back(c, after):
+            width = len(CHUNKS[c])
             da[c] = keep.tile([P, width * P * PACK], BF16, name=f"da{c}", align_bytes=64)
-            turned = bank(back_bank[c], [P, width, 2, P])
-            for n, b in enumerate(chunks[c]):
+            turned = bank(("back", c), [P, width, 2, P], after)
+            for n, b in enumerate(CHUNKS[c]):
                 da_t = keep.tile([P, H], BF16, name=f"da_t{b}")
-                if b in (2, 3):
+                if c == 0:
                     nc.vector.tensor_tensor(da_t[:], neg_silu[b][:], dh_t[b][:], ALU.mult)
                 else:
                     nc.vector.scalar_tensor_tensor(da_t[:], half_tanh[b][:], 1.0, neg_silu[b][:], ALU.add, ALU.mult)
@@ -251,65 +241,80 @@ def tile_moe_sub_silu_kernel(
                 turned[:].rearrange("p b u t -> p b t u"),
             )
 
-        def finish(c):
-            width = len(chunks[c]) * P
-            nc.vector.quantize_mx(da_w[:, tokens(c)].bitcast(E5M2), da_s[:, tokens(c)], da[c][:])
-            sums = bank(out_bank[c], [P, K // P, width])
+        def finish(c, after, on_vector=False):
+            tokens = slice(CHUNKS[c].start * P, CHUNKS[c].stop * P)
+            width = len(CHUNKS[c]) * P
+            nc.vector.quantize_mx(da_w[:, tokens].bitcast(E5M2), da_s[:, tokens], da[c][:])
+            sums = bank(("out", c), [P, K // P, width], after)
             for kb in range(K // P):
                 nc.tensor.matmul_mx(
                     sums[:, kb, :],
                     lhsT=w1_w[:, 2 * P * kb : 2 * P * (kb + 1)].bitcast(E2M1),
                     lhsT_scale=w1_s[:, P * kb : P * (kb + 1)],
-                    rhs=da_w[:, tokens(c)].bitcast(E5M2),
-                    rhs_scale=da_s[:, tokens(c)],
+                    rhs=da_w[:, tokens].bitcast(E5M2),
+                    rhs_scale=da_s[:, tokens],
                     start=True,
                     stop=True,
                 )
             res = keep.tile([P, K // P, width], F32, name=f"res{c}")
-            if c in (2, 4):
+            if on_vector:
                 nc.vector.tensor_scalar(res[:], sums[:], -0.5, None, ALU.mult)
             else:
                 nc.scalar.activation(res[:], sums[:], ACT.Copy, scale=-0.5)
-            nc.sync.dma_start(out_rows[:, :, tokens(c)], res[:])
+            nc.sync.dma_start(out_rows[:, :, tokens], res[:])
 
+        turn_a(5)
+        turn_a(6)
+        for b in (2, 3, 4, 5, 0, 1):
+            open_dh(b)
+
+        last_row = range(ROW_BLOCKS - 1, ROW_BLOCKS)
         gather_gated(1, 2, 4)
-        gather_gated(0, 0, 6, range(0, 3))
-        gather_gated(0, 0, 4, range(3, 4))
+        gather_gated(0, 0, 6, range(ROW_BLOCKS - 1))
+        gather_gated(0, 0, 4, last_row)
         turn(1, 2, 4)
         turn(0, 2, 4)
         turn(0, 0, 2)
-        gather_plain(0, 4, 6, range(3, 4))
+
+        gather_plain(0, 4, 6, last_row)
         gather_plain(1, 4, 6)
         gather_plain(0, 6, 8)
         gather_plain(1, 6, 8)
-        activate(5, 6)
+        silu(5)
+        tanh(5)
         gather_plain(1, 0, 2)
-        activate(6, 8)
+        silu(6)
+        tanh(6)
+        activate(7, after=("a", 5))
+
         apply_gate(0, 4, 6)
         turn(0, 4, 6)
         apply_gate(1, 4, 6)
         turn(1, 4, 6)
-        turn_back(0)
-        apply_gate(0, 6, 8)
-        turn(0, 6, 8)
-        apply_gate(1, 6, 8)
-        turn(1, 6, 8)
-        silu(0)
-        silu(1)
+        turn_back(0, after=("dh", 4))
+        open_dh(6, after=("dh", 2))
+        open_dh(7, after=("dh", 3))
+        for s in range(2):
+            apply_gate(s, 6, 8)
+            turn(s, 6, 8)
+        for b in (0, 1):
+            turn_a(b, after=("a", 6 + b))
+            silu(b)
         first_factor(4, 6)
-        turn_back(1)
+        turn_back(1, after=("dh", 5))
         tanh(0)
         tanh(1)
         apply_gate(1, 0, 2)
         turn(1, 0, 2)
         first_factor(6, 8)
-        turn_back(2)
-        finish(0)
+        turn_back(2, after=("dh", 6))
+
+        finish(0, after=("back", 0))
         first_factor(0, 1)
-        finish(1)
+        finish(1, after=("dh", 7))
         first_factor(1, 2)
-        turn_back(3)
-        finish(2)
-        turn_back(4)
-        finish(3)
-        finish(4)
+        turn_back(3, after=("dh", 0))
+        finish(2, after=("a", 0), on_vector=True)
+        turn_back(4, after=("dh", 1))
+        finish(3, after=("back", 1))
+        finish(4, after=("back", 2), on_vector=True)

@@ -117,13 +117,20 @@ def tile_moe_sub_silu_kernel(
             half_tanh[b] = keep.tile([P, H], F32, name=f"half_tanh{b}")
             nc.scalar.activation(half_tanh[b][:], a_turned[b][:], ACT.Tanh, scale=0.5)
 
+        def slope_on_gpsimd(b):
+            nc.gpsimd.tensor_scalar(neg_silu[b][:], neg_silu[b][:], 1.0, -1.0, ALU.mult, ALU.add)
+            nc.gpsimd.tensor_scalar(half_tanh[b][:], half_tanh[b][:], 1.0, 1.0, ALU.mult, ALU.add)
+            nc.gpsimd.tensor_tensor(neg_silu[b][:], neg_silu[b][:], half_tanh[b][:], ALU.mult)
+
         def activate(b, after=None):
             turn_a(b, after)
             silu(b)
             tanh(b)
 
-        for b in (2, 3, 4):
+        EARLY = (2, 3, 4)
+        for b in EARLY:
             activate(b)
+            slope_on_gpsimd(b)
 
         y = [keep.tile([P, E * C], F32, name=f"y{r}") for r in ALL_ROWS]
         g_s, g_w = {}, {}
@@ -147,7 +154,10 @@ def tile_moe_sub_silu_kernel(
                 start=True,
                 stop=True,
             )
-            nc.scalar.copy(y[r][:, e * C : (e + 1) * C], sums[:])
+            if e == E - 1 and r < 2:
+                nc.vector.tensor_copy(y[r][:, e * C : (e + 1) * C], sums[:])
+            else:
+                nc.scalar.copy(y[r][:, e * C : (e + 1) * C], sums[:])
 
         for e in range(E - 2):
             gather_slots(e)
@@ -156,13 +166,6 @@ def tile_moe_sub_silu_kernel(
         for e in range(E - 2, E):
             gather_slots(e)
 
-        tanh_plus_one = keep.tile([P, len(CHUNKS[0]), H], F32, name="dy_s", align_bytes=64)
-        for n, b in enumerate(CHUNKS[0]):
-            nc.vector.tensor_scalar(tanh_plus_one[:, n, :], half_tanh[b][:], 1.0, None, ALU.add)
-        for n, b in enumerate(CHUNKS[0]):
-            nc.vector.scalar_tensor_tensor(
-                neg_silu[b][:], neg_silu[b][:], 1.0, tanh_plus_one[:, n, :], ALU.subtract, ALU.mult
-            )
 
         for half in range(2):
             for e in range(E - 2, E):
@@ -229,7 +232,7 @@ def tile_moe_sub_silu_kernel(
             turned = bank(("back", c), [P, width, 2, P], after)
             for n, b in enumerate(CHUNKS[c]):
                 da_t = keep.tile([P, H], BF16, name=f"da_t{b}")
-                if c == 0:
+                if b in EARLY:
                     nc.vector.tensor_tensor(da_t[:], neg_silu[b][:], dh_t[b][:], ALU.mult)
                 else:
                     nc.vector.scalar_tensor_tensor(da_t[:], half_tanh[b][:], 1.0, neg_silu[b][:], ALU.add, ALU.mult)
@@ -300,7 +303,7 @@ def tile_moe_sub_silu_kernel(
         for b in (0, 1):
             turn_a(b, after=("a", 6 + b))
             silu(b)
-        first_factor(4, 6)
+        first_factor(5, 6)
         turn_back(1, after=("dh", 5))
         tanh(0)
         tanh(1)

@@ -24,7 +24,10 @@ SCALE_ROWS = 4
 BANKS = 8
 ROW_BLOCKS = H // P
 ALL_ROWS = range(ROW_BLOCKS)
-CHUNKS = (range(2, 4), range(4, 6), range(6, 8), range(0, 1), range(1, 2))
+CHUNKS = (range(0, 2), range(2, 4), range(4, 6), range(6, 7), range(7, 8))
+BOTH = range(2)
+FIRST, SECOND = BOTH
+EARLY = range(0, 3)
 
 
 def tile_moe_sub_silu_kernel(
@@ -56,8 +59,15 @@ def tile_moe_sub_silu_kernel(
         w2_s = keep.tile([P, E, H], U8, name="w2_s", align_bytes=64)
         w1_s = keep.tile([P, K], U8, name="w1_s", align_bytes=64)
         w1_w = keep.tile([P, 2 * K], U8, name="w1_w", align_bytes=64)
-        gates = [keep.tile([P, T], F32, name=f"gates{s}") for s in range(2)]
+        gate1 = [keep.tile([P, 2 * P], F32, name=f"gate1_{n}", align_bytes=64) for n in range(4)]
+        gate0 = keep.tile([P, T], F32, name="gate0")
         ident = keep.tile([P, P], F32, name="ident")
+
+        def gate_of(s, first, stop):
+            if s == 1:
+                base = first // 2 * 2
+                return gate1[first // 2][:, (first - base) * P : (stop - base) * P]
+            return gate0[:, first * P : stop * P]
 
         nc.vector.memset(w2_s[:].bitcast(I32), 0)
         nc.vector.memset(w1_s[:].bitcast(I32), 0)
@@ -81,20 +91,21 @@ def tile_moe_sub_silu_kernel(
                 dy_s[QUADRANT * q : QUADRANT * (q + 1), :].bitcast(I32),
                 rows.unsqueeze(0).to_broadcast([QUADRANT // SCALE_ROWS, SCALE_ROWS, T // 4]),
             )
-        load_a(2, 3)
-        load_a(3, 4)
+        load_a(0, 1)
+        load_a(1, 2)
         nc.sync.dma_start(dy_w[:], dy_words[0].rearrange("p t d -> p (t d)").bitcast(I32))
-        load_a(4, 5)
+        load_a(2, 3)
         nc.sync.dma_start(w2_first[:].bitcast(I32), w2t_words[0:1, 0].rearrange("e p b -> p e b").bitcast(I32))
         for j in range(SCALE_ROWS):
             nc.sync.dma_start(w2_s[j:P:QUADRANT, :, :].bitcast(I32), w2_rows[j].bitcast(I32))
         nc.sync.dma_start(w2_rest[:].bitcast(I32), w2t_words[1:E, 0].rearrange("e p b -> p e b").bitcast(I32))
-        load_a(5, 8)
-        load_a(0, 2)
+        load_a(3, 6)
+        load_a(6, 8)
         for s, lst in enumerate((pos1, pos2)):
             nc.sync.dma_start(token_slots[s][:], lst)
-        for s in range(2):
-            nc.sync.dma_start(gates[s][:], gate[s])
+        nc.sync.dma_start(gate0[:], gate[0])
+        for n in range(4):
+            nc.sync.dma_start(gate1[n][:], gate[1, :, 2 * n * P : 2 * (n + 1) * P])
         nc.sync.dma_start(w1_w[:].bitcast(I32), w1t_words[0].bitcast(I32))
         for j in range(SCALE_ROWS):
             nc.sync.dma_start(w1_s[j:P:QUADRANT, :].bitcast(I32), w1_rows[j].bitcast(I32))
@@ -102,35 +113,26 @@ def tile_moe_sub_silu_kernel(
         def block_columns(tile, r):
             return tile[:].rearrange("t (u r q d) -> t r q u d", u=2, r=ROW_BLOCKS, d=2)[:, r]
 
-        a_turned, neg_silu, half_tanh = {}, {}, {}
+        a_turned, factors = {}, {}
 
         def turn_a(b, after=None):
             a_turned[b] = bank(("a", b), [P, H], after)
             for r in ALL_ROWS:
                 nc.tensor.transpose(block_columns(a_turned[b], r), a_sb[b][:, r, :], ident[:])
 
-        def silu(b):
-            neg_silu[b] = keep.tile([P, H], F32, name=f"neg_silu{b}")
-            nc.scalar.activation(neg_silu[b][:], a_turned[b][:], ACT.Silu, scale=-1.0)
+        def activate(b):
+            factors[b] = keep.tile([P, 2, H], F32, name=f"factors{b}", align_bytes=64)
+            nc.scalar.activation(factors[b][:, 0, :], a_turned[b][:], ACT.Silu, scale=-1.0)
+            nc.scalar.activation(factors[b][:, 1, :], a_turned[b][:], ACT.Tanh, scale=-0.5)
 
-        def tanh(b):
-            half_tanh[b] = keep.tile([P, H], F32, name=f"half_tanh{b}")
-            nc.scalar.activation(half_tanh[b][:], a_turned[b][:], ACT.Tanh, scale=0.5)
-
-        def slope_on_gpsimd(b):
-            nc.gpsimd.tensor_scalar(neg_silu[b][:], neg_silu[b][:], 1.0, -1.0, ALU.mult, ALU.add)
-            nc.gpsimd.tensor_scalar(half_tanh[b][:], half_tanh[b][:], 1.0, 1.0, ALU.mult, ALU.add)
-            nc.gpsimd.tensor_tensor(neg_silu[b][:], neg_silu[b][:], half_tanh[b][:], ALU.mult)
-
-        def activate(b, after=None):
-            turn_a(b, after)
-            silu(b)
-            tanh(b)
-
-        EARLY = (2, 3, 4)
-        for b in EARLY:
+        def early_slope(b):
+            turn_a(b)
             activate(b)
-            slope_on_gpsimd(b)
+            nc.gpsimd.tensor_scalar(factors[b][:], factors[b][:], 1.0, -1.0, ALU.mult, ALU.add)
+            nc.gpsimd.tensor_tensor(factors[b][:, 0, :], factors[b][:, 0, :], factors[b][:, 1, :], ALU.mult)
+
+        for b in EARLY:
+            early_slope(b)
 
         y = [keep.tile([P, E * C], F32, name=f"y{r}") for r in ALL_ROWS]
         g_s, g_w = {}, {}
@@ -154,53 +156,46 @@ def tile_moe_sub_silu_kernel(
                 start=True,
                 stop=True,
             )
-            if e == E - 1 and r < 2:
+            if (e, r) in ON_VECTOR:
                 nc.vector.tensor_copy(y[r][:, e * C : (e + 1) * C], sums[:])
             else:
                 nc.scalar.copy(y[r][:, e * C : (e + 1) * C], sums[:])
 
-        for e in range(E - 2):
+        ON_VECTOR = ((2, 0), (2, 1), (3, 0), (3, 1))
+        for e in range(E):
             gather_slots(e)
             for r in ALL_ROWS:
                 expert_pass(e, r)
-        for e in range(E - 2, E):
-            gather_slots(e)
-
-
-        for half in range(2):
-            for e in range(E - 2, E):
-                for r in (2 * half, 2 * half + 1):
-                    expert_pass(e, r)
 
         da_w = keep.tile([P, T], U32, name="da_w", align_bytes=64)
         da_s = keep.tile([P, T], U8, name="da_s", align_bytes=64)
         out_rows = out.rearrange("(kb p) t -> p kb t", p=P)
-        picked, block, dh_t, da = {}, {}, {}, {}
+        picked, block, dh_t, da, da_t, back = {}, {}, {}, {}, {}, {}
 
-        def new_picked(s, first, stop, rows):
-            tile = keep.tile([P, len(rows), (stop - first) * P], F32, name=f"picked{s}_{first}_{rows.start}")
-            picked[s, first] = tile
+        def new_picked(s, first, stop, place=None):
+            tile = keep.tile(
+                [P, ROW_BLOCKS, (stop - first) * P], F32, name=place or f"picked{s}_{first}", align_bytes=64
+            )
             for b in range(first, stop):
-                for n, r in enumerate(rows):
-                    block[s, b, r] = tile[:, n, (b - first) * P : (b - first + 1) * P]
-            return tile, token_slots[s][:, first * P // PER_COL : stop * P // PER_COL]
+                picked[s, b] = (tile, first)
+                for r in ALL_ROWS:
+                    block[s, b, r] = tile[:, r, (b - first) * P : (b - first + 1) * P]
+            return tile
 
-        def gather_gated(s, first, stop, rows=ALL_ROWS):
-            tile, entries = new_picked(s, first, stop, rows)
-            for n, r in enumerate(rows):
-                nc.vector.tensor_tensor(
-                    tile[:, n, :], y[r][:].indirect(entries), gates[s][:, first * P : stop * P], ALU.mult
-                )
+        def entries(s, first, stop):
+            return token_slots[s][:, first * P // PER_COL : stop * P // PER_COL]
 
-        def gather_plain(s, first, stop, rows=ALL_ROWS):
-            tile, entries = new_picked(s, first, stop, rows)
-            for n, r in enumerate(rows):
-                nc.scalar.activation(tile[:, n, :], y[r][:].indirect(entries), ACT.Copy)
+        def gather_plain(s, first, stop):
+            tile = new_picked(s, first, stop)
+            for r in ALL_ROWS:
+                nc.scalar.activation(tile[:, r, :], y[r][:].indirect(entries(s, first, stop)), ACT.Copy)
 
-        def apply_gate(s, first, stop):
-            tile = picked[s, first]
-            wide = gates[s][:, first * P : stop * P].unsqueeze(1).to_broadcast(tile.shape)
-            nc.vector.tensor_tensor(tile[:], tile[:], wide, ALU.mult)
+        def apply_gate(s, first, stop, engine=nc.vector, place=None):
+            tile, base = picked[s, first]
+            part = tile[:, :, (first - base) * P : (stop - base) * P]
+            wide = gate_of(s, first, stop).unsqueeze(1).to_broadcast(part.shape)
+            gated = part if place is None else new_picked(s, first, stop, place)[:]
+            engine.tensor_tensor(gated, part, wide, ALU.mult)
 
         def open_dh(b, after=None):
             dh_t[b] = bank(("dh", b), [P, H], after)
@@ -220,34 +215,41 @@ def tile_moe_sub_silu_kernel(
                     )
                 opened.add(b)
 
-        def first_factor(first, stop):
-            for b in range(first, stop):
+        def first_factor(b):
+            nc.vector.scalar_tensor_tensor(
+                factors[b][:, 0, :], factors[b][:, 0, :], 1.0, dh_t[b][:], ALU.subtract, ALU.mult
+            )
+
+        def product(b, place=None):
+            da_t[b] = keep.tile([P, H], BF16, name=place or f"da_t{b}", align_bytes=64)
+            if b in EARLY:
+                nc.vector.tensor_tensor(da_t[b][:], factors[b][:, 0, :], dh_t[b][:], ALU.mult)
+            else:
                 nc.vector.scalar_tensor_tensor(
-                    neg_silu[b][:], neg_silu[b][:], 1.0, dh_t[b][:], ALU.subtract, ALU.mult
+                    da_t[b][:], factors[b][:, 1, :], 1.0, factors[b][:, 0, :], ALU.subtract, ALU.mult
                 )
 
         def turn_back(c, after):
-            width = len(CHUNKS[c])
-            da[c] = keep.tile([P, width * P * PACK], BF16, name=f"da{c}", align_bytes=64)
-            turned = bank(("back", c), [P, width, 2, P], after)
+            back[c] = bank(("back", c), [P, len(CHUNKS[c]), 2, P], after)
             for n, b in enumerate(CHUNKS[c]):
-                da_t = keep.tile([P, H], BF16, name=f"da_t{b}")
-                if b in EARLY:
-                    nc.vector.tensor_tensor(da_t[:], neg_silu[b][:], dh_t[b][:], ALU.mult)
-                else:
-                    nc.vector.scalar_tensor_tensor(da_t[:], half_tanh[b][:], 1.0, neg_silu[b][:], ALU.add, ALU.mult)
-                pairs = da_t[:].bitcast(F32)
+                pairs = da_t[b][:].bitcast(F32)
                 for u in range(2):
-                    nc.tensor.transpose(turned[:, n, u, :], pairs[:, u * P : (u + 1) * P], ident[:])
-            nc.scalar.copy(
+                    nc.tensor.transpose(back[c][:, n, u, :], pairs[:, u * P : (u + 1) * P], ident[:])
+
+        def weave(c, on_vector=False):
+            da[c] = keep.tile([P, len(CHUNKS[c]) * P * PACK], BF16, name=f"da{c}", align_bytes=64)
+            (nc.vector.tensor_copy if on_vector else nc.scalar.copy)(
                 da[c][:].bitcast(F32).rearrange("p (b t u) -> p b t u", t=P, u=2),
-                turned[:].rearrange("p b u t -> p b t u"),
+                back[c][:].rearrange("p b u t -> p b t u"),
             )
+
+        def quantise(c):
+            tokens = slice(CHUNKS[c].start * P, CHUNKS[c].stop * P)
+            nc.vector.quantize_mx(da_w[:, tokens].bitcast(E5M2), da_s[:, tokens], da[c][:])
 
         def finish(c, after, on_vector=False):
             tokens = slice(CHUNKS[c].start * P, CHUNKS[c].stop * P)
             width = len(CHUNKS[c]) * P
-            nc.vector.quantize_mx(da_w[:, tokens].bitcast(E5M2), da_s[:, tokens], da[c][:])
             sums = bank(("out", c), [P, K // P, width], after)
             for kb in range(K // P):
                 nc.tensor.matmul_mx(
@@ -261,63 +263,83 @@ def tile_moe_sub_silu_kernel(
                 )
             res = keep.tile([P, K // P, width], F32, name=f"res{c}")
             if on_vector:
-                nc.vector.tensor_scalar(res[:], sums[:], -0.5, None, ALU.mult)
+                nc.vector.tensor_scalar(res[:], sums[:], 0.5, None, ALU.mult)
             else:
-                nc.scalar.activation(res[:], sums[:], ACT.Copy, scale=-0.5)
+                nc.scalar.activation(res[:], sums[:], ACT.Copy, scale=0.5)
             nc.sync.dma_start(out_rows[:, :, tokens], res[:])
 
-        turn_a(5)
-        turn_a(6)
-        for b in (2, 3, 4, 5, 0, 1):
-            open_dh(b)
+        turn_a(3, after=("y", 2, 2))
+        turn_a(4, after=("y", 2, 3))
+        turn_a(5, after=("y", 3, 2))
+        turn_a(6, after=("y", 3, 3))
+        for b, tenant in enumerate(ON_VECTOR):
+            open_dh(b, after=("y",) + tenant)
 
-        last_row = range(ROW_BLOCKS - 1, ROW_BLOCKS)
-        gather_gated(1, 2, 4)
-        gather_gated(0, 0, 6, range(ROW_BLOCKS - 1))
-        gather_gated(0, 0, 4, last_row)
-        turn(1, 2, 4)
-        turn(0, 2, 4)
-        turn(0, 0, 2)
-
-        gather_plain(0, 4, 6, last_row)
-        gather_plain(1, 4, 6)
-        gather_plain(0, 6, 8)
-        gather_plain(1, 6, 8)
-        silu(5)
-        tanh(5)
-        gather_plain(1, 0, 2)
-        silu(6)
-        tanh(6)
-        activate(7, after=("a", 5))
-
-        apply_gate(0, 4, 6)
-        turn(0, 4, 6)
-        apply_gate(1, 4, 6)
-        turn(1, 4, 6)
-        turn_back(0, after=("dh", 4))
-        open_dh(6, after=("dh", 2))
-        open_dh(7, after=("dh", 3))
-        for s in range(2):
-            apply_gate(s, 6, 8)
-            turn(s, 6, 8)
-        for b in (0, 1):
-            turn_a(b, after=("a", 6 + b))
-            silu(b)
-        first_factor(5, 6)
-        turn_back(1, after=("dh", 5))
-        tanh(0)
-        tanh(1)
-        apply_gate(1, 0, 2)
+        stops = (4, 2)
+        fused = [new_picked(FIRST, 0, stops[0], place="g_w2"), new_picked(SECOND, 0, stops[1], place="g_w3")]
+        for r in ALL_ROWS:
+            for s in (SECOND, FIRST):
+                nc.vector.tensor_tensor(
+                    fused[s][:, r, :], y[r][:].indirect(entries(s, 0, stops[s])), gate_of(s, 0, stops[s]), ALU.mult
+                )
         turn(1, 0, 2)
-        first_factor(6, 8)
-        turn_back(2, after=("dh", 6))
+        turn(0, 0, 4)
 
-        finish(0, after=("back", 0))
-        first_factor(0, 1)
-        finish(1, after=("dh", 7))
-        first_factor(1, 2)
-        turn_back(3, after=("dh", 0))
-        finish(2, after=("a", 0), on_vector=True)
-        turn_back(4, after=("dh", 1))
+        gather_plain(SECOND, 2, 6)
+        gather_plain(FIRST, 4, 6)
+        activate(3)
+        gather_plain(FIRST, 6, 8)
+        activate(4)
+        gather_plain(SECOND, 6, 8)
+        activate(5)
+
+        apply_gate(SECOND, 2, 4)
+        turn(1, 2, 4)
+        apply_gate(SECOND, 4, 6)
+        apply_gate(FIRST, 4, 6, engine=nc.gpsimd, place="gate1_2")
+        product(0, place="gate1_1")
+        product(1)
+        turn_back(0, after=("dh", 0))
+        product(2)
+        first_factor(3)
+        weave(0, on_vector=True)
+        open_dh(4, after=("dh", 1))
+        open_dh(5, after=("dh", 2))
+        open_dh(6, after=("dh", 3))
+        open_dh(7, after=("a", 3))
+        turn(1, 4, 6)
+        turn(0, 4, 6)
+        apply_gate(FIRST, 6, 8, place="da_t1")
+        turn(0, 6, 8)
+        product(3)
+        turn_back(1, after=("back", 0))
+        quantise(0)
+        turn_a(7, after=("a", 4))
+        first_factor(4)
+        activate(6)
+        activate(7)
+        weave(1)
+        finish(0, after=("dh", 4))
+        apply_gate(SECOND, 6, 8)
+        turn(1, 6, 8)
+        first_factor(5)
+        product(4)
+        product(5)
+        turn_back(2, after=("a", 5))
+        weave(2)
+        first_factor(6)
+        first_factor(7)
+        quantise(1)
+        product(6)
+        turn_back(3, after=("dh", 5))
+        product(7)
+        turn_back(4, after=("dh", 6))
+        weave(3)
+        weave(4)
+        quantise(2)
+        finish(1, after=("a", 6), on_vector=True)
+        quantise(3)
+        quantise(4)
+        finish(2, after=("a", 7))
         finish(3, after=("back", 1))
-        finish(4, after=("back", 2), on_vector=True)
+        finish(4, after=("dh", 7), on_vector=True)

@@ -27,6 +27,7 @@ ALL_ROWS = range(ROW_BLOCKS)
 CHUNKS = (range(0, 2), range(2, 4), range(4, 6), range(6, 7), range(7, 8))
 BOTH = range(2)
 FIRST, SECOND = BOTH
+GATE1_PIECES = (range(0, 3), range(3, 4), range(4, 6), range(6, 8))
 EARLY = range(0, 3)
 
 
@@ -59,14 +60,18 @@ def tile_moe_sub_silu_kernel(
         w2_s = keep.tile([P, E, H], U8, name="w2_s", align_bytes=64)
         w1_s = keep.tile([P, K], U8, name="w1_s", align_bytes=64)
         w1_w = keep.tile([P, 2 * K], U8, name="w1_w", align_bytes=64)
-        gate1 = [keep.tile([P, 2 * P], F32, name=f"gate1_{n}", align_bytes=64) for n in range(4)]
+        gate1 = {}
+        for piece in GATE1_PIECES:
+            tile = keep.tile([P, len(piece) * P], F32, name=f"gate1_{piece.start}", align_bytes=64)
+            for b in piece:
+                gate1[b] = (tile, piece.start)
         gate0 = keep.tile([P, T], F32, name="gate0")
         ident = keep.tile([P, P], F32, name="ident")
 
         def gate_of(s, first, stop):
             if s == 1:
-                base = first // 2 * 2
-                return gate1[first // 2][:, (first - base) * P : (stop - base) * P]
+                tile, base = gate1[first]
+                return tile[:, (first - base) * P : (stop - base) * P]
             return gate0[:, first * P : stop * P]
 
         nc.vector.memset(w2_s[:].bitcast(I32), 0)
@@ -104,8 +109,8 @@ def tile_moe_sub_silu_kernel(
         for s, lst in enumerate((pos1, pos2)):
             nc.sync.dma_start(token_slots[s][:], lst)
         nc.sync.dma_start(gate0[:], gate[0])
-        for n in range(4):
-            nc.sync.dma_start(gate1[n][:], gate[1, :, 2 * n * P : 2 * (n + 1) * P])
+        for piece in GATE1_PIECES:
+            nc.sync.dma_start(gate1[piece.start][0][:], gate[1, :, piece.start * P : piece.stop * P])
         nc.sync.dma_start(w1_w[:].bitcast(I32), w1t_words[0].bitcast(I32))
         for j in range(SCALE_ROWS):
             nc.sync.dma_start(w1_s[j:P:QUADRANT, :].bitcast(I32), w1_rows[j].bitcast(I32))
@@ -275,17 +280,17 @@ def tile_moe_sub_silu_kernel(
         for b, tenant in enumerate(ON_VECTOR):
             open_dh(b, after=("y",) + tenant)
 
-        stops = (4, 2)
+        stops = (4, 3)
         fused = [new_picked(FIRST, 0, stops[0], place="g_w2"), new_picked(SECOND, 0, stops[1], place="g_w3")]
         for r in ALL_ROWS:
             for s in (SECOND, FIRST):
                 nc.vector.tensor_tensor(
                     fused[s][:, r, :], y[r][:].indirect(entries(s, 0, stops[s])), gate_of(s, 0, stops[s]), ALU.mult
                 )
-        turn(1, 0, 2)
+        turn(1, 0, 3)
         turn(0, 0, 4)
 
-        gather_plain(SECOND, 2, 6)
+        gather_plain(SECOND, 3, 6)
         gather_plain(FIRST, 4, 6)
         activate(3)
         gather_plain(FIRST, 6, 8)
@@ -293,11 +298,11 @@ def tile_moe_sub_silu_kernel(
         gather_plain(SECOND, 6, 8)
         activate(5)
 
-        apply_gate(SECOND, 2, 4)
-        turn(1, 2, 4)
+        apply_gate(SECOND, 3, 4)
+        turn(1, 3, 4)
         apply_gate(SECOND, 4, 6)
-        apply_gate(FIRST, 4, 6, engine=nc.gpsimd, place="gate1_2")
-        product(0, place="gate1_1")
+        apply_gate(FIRST, 4, 6, engine=nc.gpsimd, place="gate1_4")
+        product(0, place="gate1_3")
         product(1)
         turn_back(0, after=("dh", 0))
         product(2)

@@ -27,7 +27,7 @@ ALL_ROWS = range(ROW_BLOCKS)
 CHUNKS = (range(0, 2), range(2, 4), range(4, 6), range(6, 7), range(7, 8))
 BOTH = range(2)
 FIRST, SECOND = BOTH
-GATE1_PIECES = (range(0, 3), range(3, 4), range(4, 6), range(6, 8))
+GATE_PIECES = ((range(0, 4), range(4, 6), range(6, 8)), (range(0, 3), range(3, 4), range(4, 6), range(6, 8)))
 EARLY = range(0, 3)
 
 
@@ -60,19 +60,17 @@ def tile_moe_sub_silu_kernel(
         w2_s = keep.tile([P, E, H], U8, name="w2_s", align_bytes=64)
         w1_s = keep.tile([P, K], U8, name="w1_s", align_bytes=64)
         w1_w = keep.tile([P, 2 * K], U8, name="w1_w", align_bytes=64)
-        gate1 = {}
-        for piece in GATE1_PIECES:
-            tile = keep.tile([P, len(piece) * P], F32, name=f"gate1_{piece.start}", align_bytes=64)
-            for b in piece:
-                gate1[b] = (tile, piece.start)
-        gate0 = keep.tile([P, T], F32, name="gate0")
+        gates = {}
+        for s, pieces in enumerate(GATE_PIECES):
+            for piece in pieces:
+                tile = keep.tile([P, len(piece) * P], F32, name=f"gate{s}_{piece.start}", align_bytes=64)
+                for b in piece:
+                    gates[s, b] = (tile, piece.start)
         ident = keep.tile([P, P], F32, name="ident")
 
         def gate_of(s, first, stop):
-            if s == 1:
-                tile, base = gate1[first]
-                return tile[:, (first - base) * P : (stop - base) * P]
-            return gate0[:, first * P : stop * P]
+            tile, base = gates[s, first]
+            return tile[:, (first - base) * P : (stop - base) * P]
 
         nc.vector.memset(w2_s[:].bitcast(I32), 0)
         nc.vector.memset(w1_s[:].bitcast(I32), 0)
@@ -108,9 +106,10 @@ def tile_moe_sub_silu_kernel(
         load_a(6, 8)
         for s, lst in enumerate((pos1, pos2)):
             nc.sync.dma_start(token_slots[s][:], lst)
-        nc.sync.dma_start(gate0[:], gate[0])
-        for piece in GATE1_PIECES:
-            nc.sync.dma_start(gate1[piece.start][0][:], gate[1, :, piece.start * P : piece.stop * P])
+        for n in range(4):
+            for s, pieces in enumerate(GATE_PIECES):
+                for piece in pieces[n : n + 1]:
+                    nc.sync.dma_start(gates[s, piece.start][0][:], gate[s, :, piece.start * P : piece.stop * P])
         nc.sync.dma_start(w1_w[:].bitcast(I32), w1t_words[0].bitcast(I32))
         for j in range(SCALE_ROWS):
             nc.sync.dma_start(w1_s[j:P:QUADRANT, :].bitcast(I32), w1_rows[j].bitcast(I32))
@@ -177,29 +176,31 @@ def tile_moe_sub_silu_kernel(
         out_rows = out.rearrange("(kb p) t -> p kb t", p=P)
         picked, block, dh_t, da, da_t, back = {}, {}, {}, {}, {}, {}
 
-        def new_picked(s, first, stop, place=None):
-            tile = keep.tile(
-                [P, ROW_BLOCKS, (stop - first) * P], F32, name=place or f"picked{s}_{first}", align_bytes=64
-            )
+        def new_picked(s, first, stop, place=None, rows=ALL_ROWS):
+            name = place or f"picked{s}_{first}_{rows.start}"
+            tile = keep.tile([P, len(rows), (stop - first) * P], F32, name=name, align_bytes=64)
             for b in range(first, stop):
-                picked[s, b] = (tile, first)
-                for r in ALL_ROWS:
-                    block[s, b, r] = tile[:, r, (b - first) * P : (b - first + 1) * P]
+                picked[s, b] = (tile, first, rows)
+                for n, r in enumerate(rows):
+                    block[s, b, r] = tile[:, n, (b - first) * P : (b - first + 1) * P]
             return tile
 
         def entries(s, first, stop):
             return token_slots[s][:, first * P // PER_COL : stop * P // PER_COL]
 
-        def gather_plain(s, first, stop):
-            tile = new_picked(s, first, stop)
-            for r in ALL_ROWS:
-                nc.scalar.activation(tile[:, r, :], y[r][:].indirect(entries(s, first, stop)), ACT.Copy)
+        def gather_gated(s, first, stop, r, tile):
+            nc.vector.tensor_tensor(tile, y[r][:].indirect(entries(s, first, stop)), gate_of(s, first, stop), ALU.mult)
+
+        def gather_plain(s, first, stop, rows=ALL_ROWS):
+            tile = new_picked(s, first, stop, rows=rows)
+            for n, r in enumerate(rows):
+                nc.scalar.activation(tile[:, n, :], y[r][:].indirect(entries(s, first, stop)), ACT.Copy)
 
         def apply_gate(s, first, stop, engine=nc.vector, place=None):
-            tile, base = picked[s, first]
+            tile, base, rows = picked[s, first]
             part = tile[:, :, (first - base) * P : (stop - base) * P]
             wide = gate_of(s, first, stop).unsqueeze(1).to_broadcast(part.shape)
-            gated = part if place is None else new_picked(s, first, stop, place)[:]
+            gated = part if place is None else new_picked(s, first, stop, place, rows)[:]
             engine.tensor_tensor(gated, part, wide, ALU.mult)
 
         def open_dh(b, after=None):
@@ -276,62 +277,65 @@ def tile_moe_sub_silu_kernel(
         turn_a(3, after=("y", 2, 2))
         turn_a(4, after=("y", 2, 3))
         turn_a(5, after=("y", 3, 2))
-        turn_a(6, after=("y", 3, 3))
-        for b, tenant in enumerate(ON_VECTOR):
+        for b, tenant in enumerate(ON_VECTOR + ((3, 3),)):
             open_dh(b, after=("y",) + tenant)
 
-        stops = (4, 3)
-        fused = [new_picked(FIRST, 0, stops[0], place="g_w2"), new_picked(SECOND, 0, stops[1], place="g_w3")]
+        firsts = new_picked(FIRST, 0, 4, place="g_w2")
+        seconds = new_picked(SECOND, 0, 3, place="g_w3")
         for r in ALL_ROWS:
-            for s in (SECOND, FIRST):
-                nc.vector.tensor_tensor(
-                    fused[s][:, r, :], y[r][:].indirect(entries(s, 0, stops[s])), gate_of(s, 0, stops[s]), ALU.mult
-                )
+            gather_gated(SECOND, 0, 3, r, seconds[:, r, :])
+            gather_gated(FIRST, 0, 4, r, firsts[:, r, :])
         turn(1, 0, 3)
         turn(0, 0, 4)
 
         gather_plain(SECOND, 3, 6)
-        gather_plain(FIRST, 4, 6)
+        gather_plain(FIRST, 4, 6, ALL_ROWS[:3])
+        middle_rows = picked[FIRST, 4]
+        gather_plain(FIRST, 4, 6, ALL_ROWS[3:])
+        last_row = picked[FIRST, 4]
         activate(3)
         gather_plain(FIRST, 6, 8)
         activate(4)
-        gather_plain(SECOND, 6, 8)
         activate(5)
+        gather_plain(SECOND, 6, 8)
 
         apply_gate(SECOND, 3, 4)
         turn(1, 3, 4)
+        picked[FIRST, 4] = middle_rows
+        apply_gate(FIRST, 4, 6)
         apply_gate(SECOND, 4, 6)
+        open_dh(5, after=("a", 3))
+        turn(1, 4, 6)
+        picked[FIRST, 4] = last_row
         apply_gate(FIRST, 4, 6, engine=nc.gpsimd, place="gate1_4")
+        turn(0, 4, 6)
+        apply_gate(FIRST, 6, 8, engine=nc.gpsimd, place="gate0_4")
         product(0, place="gate1_3")
         product(1)
         turn_back(0, after=("dh", 0))
         product(2)
         first_factor(3)
-        weave(0, on_vector=True)
-        open_dh(4, after=("dh", 1))
-        open_dh(5, after=("dh", 2))
-        open_dh(6, after=("dh", 3))
-        open_dh(7, after=("a", 3))
-        turn(1, 4, 6)
-        turn(0, 4, 6)
-        apply_gate(FIRST, 6, 8, place="da_t1")
+        first_factor(4)
+        first_factor(5)
+        weave(0)
+        turn_a(6, after=("a", 4))
+        turn_a(7, after=("a", 5))
+        open_dh(6, after=("dh", 1))
+        open_dh(7, after=("dh", 2))
         turn(0, 6, 8)
         product(3)
-        turn_back(1, after=("back", 0))
-        quantise(0)
-        turn_a(7, after=("a", 4))
-        first_factor(4)
+        turn_back(1, after=("dh", 3))
+        product(4)
         activate(6)
         activate(7)
         weave(1)
-        finish(0, after=("dh", 4))
         apply_gate(SECOND, 6, 8)
         turn(1, 6, 8)
-        first_factor(5)
-        product(4)
         product(5)
-        turn_back(2, after=("a", 5))
+        turn_back(2, after=("dh", 4))
         weave(2)
+        quantise(0)
+        finish(0, after=("back", 0))
         first_factor(6)
         first_factor(7)
         quantise(1)

@@ -27,7 +27,7 @@ ALL_ROWS = range(ROW_BLOCKS)
 CHUNKS = (range(0, 2), range(2, 4), range(4, 6), range(6, 7), range(7, 8))
 BOTH = range(2)
 FIRST, SECOND = BOTH
-GATE_PIECES = ((range(0, 4), range(4, 6), range(6, 8)), (range(0, 3), range(3, 4), range(4, 6), range(6, 8)))
+GATE_PIECES = ((range(0, 4), range(4, 5), range(5, 6), range(6, 8)), (range(0, 3), range(3, 4), range(4, 6), range(6, 8)))
 EARLY = range(0, 3)
 
 
@@ -68,9 +68,9 @@ def tile_moe_sub_silu_kernel(
                     gates[s, b] = (tile, piece.start)
         ident = keep.tile([P, P], F32, name="ident")
 
-        def gate_of(s, first, stop):
-            tile, base = gates[s, first]
-            return tile[:, (first - base) * P : (stop - base) * P]
+        def gate_of(s, tiles):
+            tile, base = gates[s, tiles.start]
+            return tile[:, (tiles.start - base) * P : (tiles.stop - base) * P]
 
         nc.vector.memset(w2_s[:].bitcast(I32), 0)
         nc.vector.memset(w1_s[:].bitcast(I32), 0)
@@ -124,10 +124,16 @@ def tile_moe_sub_silu_kernel(
             for r in ALL_ROWS:
                 nc.tensor.transpose(block_columns(a_turned[b], r), a_sb[b][:, r, :], ident[:])
 
-        def activate(b):
+        def silu(b):
             factors[b] = keep.tile([P, 2, H], F32, name=f"factors{b}", align_bytes=64)
             nc.scalar.activation(factors[b][:, 0, :], a_turned[b][:], ACT.Silu, scale=-1.0)
+
+        def tanh(b):
             nc.scalar.activation(factors[b][:, 1, :], a_turned[b][:], ACT.Tanh, scale=-0.5)
+
+        def activate(b):
+            silu(b)
+            tanh(b)
 
         def early_slope(b):
             turn_a(b)
@@ -176,50 +182,55 @@ def tile_moe_sub_silu_kernel(
         out_rows = out.rearrange("(kb p) t -> p kb t", p=P)
         picked, block, dh_t, da, da_t, back = {}, {}, {}, {}, {}, {}
 
-        def new_picked(s, first, stop, place=None, rows=ALL_ROWS):
-            name = place or f"picked{s}_{first}_{rows.start}"
-            tile = keep.tile([P, len(rows), (stop - first) * P], F32, name=name, align_bytes=64)
-            for b in range(first, stop):
-                picked[s, b] = (tile, first, rows)
-                for n, r in enumerate(rows):
-                    block[s, b, r] = tile[:, n, (b - first) * P : (b - first + 1) * P]
-            return tile
+        def entries(s, tiles):
+            return token_slots[s][:, tiles.start * P // PER_COL : tiles.stop * P // PER_COL]
 
-        def entries(s, first, stop):
-            return token_slots[s][:, first * P // PER_COL : stop * P // PER_COL]
-
-        def gather_gated(s, first, stop, r, tile):
-            nc.vector.tensor_tensor(tile, y[r][:].indirect(entries(s, first, stop)), gate_of(s, first, stop), ALU.mult)
-
-        def gather_plain(s, first, stop, rows=ALL_ROWS):
-            tile = new_picked(s, first, stop, rows=rows)
+        def note_blocks(s, tiles, rows, columns):
             for n, r in enumerate(rows):
-                nc.scalar.activation(tile[:, n, :], y[r][:].indirect(entries(s, first, stop)), ACT.Copy)
+                for b in tiles:
+                    block[s, b, r] = columns[:, n, (b - tiles.start) * P : (b - tiles.start + 1) * P]
 
-        def apply_gate(s, first, stop, engine=nc.vector, place=None):
-            tile, base, rows = picked[s, first]
-            part = tile[:, :, (first - base) * P : (stop - base) * P]
-            wide = gate_of(s, first, stop).unsqueeze(1).to_broadcast(part.shape)
-            gated = part if place is None else new_picked(s, first, stop, place, rows)[:]
-            engine.tensor_tensor(gated, part, wide, ALU.mult)
+        def room(place, tiles, rows):
+            return keep.tile([P, len(rows), len(tiles) * P], F32, name=place, align_bytes=64)
+
+        def gather_gated(s, tiles, r, columns):
+            nc.vector.tensor_tensor(columns, y[r][:].indirect(entries(s, tiles)), gate_of(s, tiles), ALU.mult)
+            note_blocks(s, tiles, ALL_ROWS[r : r + 1], columns.unsqueeze(1))
+            turn(s, tiles, ALL_ROWS[r : r + 1])
+
+        def gather_plain(s, tiles, rows=ALL_ROWS):
+            tile = room(f"picked{s}_{tiles.start}_{rows.start}", tiles, rows)
+            for n, r in enumerate(rows):
+                nc.scalar.activation(tile[:, n, :], y[r][:].indirect(entries(s, tiles)), ACT.Copy)
+                for b in tiles:
+                    picked[s, b, r] = (tile, tiles.start, rows.start)
+
+        def apply_gate(s, tiles, rows=ALL_ROWS, engine=nc.vector, place=None):
+            tile, first, top = picked[s, tiles.start, rows.start]
+            plain = tile[:, rows.start - top : rows.stop - top, (tiles.start - first) * P : (tiles.stop - first) * P]
+            wide = gate_of(s, tiles).unsqueeze(1).to_broadcast(plain.shape)
+            gated = plain if place is None else place
+            engine.tensor_tensor(gated, plain, wide, ALU.mult)
+            note_blocks(s, tiles, rows, gated)
 
         def open_dh(b, after=None):
             dh_t[b] = bank(("dh", b), [P, H], after)
 
-        opened = set()
+        turned = {}
 
-        def turn(s, first, stop):
-            for b in range(first, stop):
-                for r in ALL_ROWS:
+        def turn(s, tiles, rows=ALL_ROWS):
+            for b in tiles:
+                for r in rows:
+                    done = turned.get(b, 0)
                     nc.tensor.matmul(
                         block_columns(dh_t[b], r),
                         lhsT=block[s, b, r],
                         rhs=ident[:],
-                        start=(b not in opened and r == 0),
-                        stop=(b in opened and r == ROW_BLOCKS - 1),
+                        start=(done == 0),
+                        stop=(done == 2 * ROW_BLOCKS - 1),
                         is_transpose=True,
                     )
-                opened.add(b)
+                    turned[b] = done + 1
 
         def first_factor(b):
             nc.vector.scalar_tensor_tensor(
@@ -274,81 +285,83 @@ def tile_moe_sub_silu_kernel(
                 nc.scalar.activation(res[:], sums[:], ACT.Copy, scale=0.5)
             nc.sync.dma_start(out_rows[:, :, tokens], res[:])
 
-        turn_a(3, after=("y", 2, 2))
-        turn_a(4, after=("y", 2, 3))
-        turn_a(5, after=("y", 3, 2))
-        for b, tenant in enumerate(ON_VECTOR + ((3, 3),)):
+        for b, tenant in zip(range(3, 7), ((2, 2), (2, 3), (3, 2), (3, 3))):
+            turn_a(b, after=("y",) + tenant)
+        for b, tenant in enumerate(ON_VECTOR):
             open_dh(b, after=("y",) + tenant)
 
-        firsts = new_picked(FIRST, 0, 4, place="g_w2")
-        seconds = new_picked(SECOND, 0, 3, place="g_w3")
-        for r in ALL_ROWS:
-            gather_gated(SECOND, 0, 3, r, seconds[:, r, :])
-            gather_gated(FIRST, 0, 4, r, firsts[:, r, :])
-        turn(1, 0, 3)
-        turn(0, 0, 4)
-
-        gather_plain(SECOND, 3, 6)
-        gather_plain(FIRST, 4, 6, ALL_ROWS[:3])
-        middle_rows = picked[FIRST, 4]
-        gather_plain(FIRST, 4, 6, ALL_ROWS[3:])
-        last_row = picked[FIRST, 4]
+        FIRSTS, SECONDS = range(0, 4), range(0, 3)
+        ONE = range(1)
+        gather_plain(SECOND, range(3, 6))
         activate(3)
-        gather_plain(FIRST, 6, 8)
+        open_dh(4, after=("a", 3))
+        gather_plain(FIRST, range(4, 6))
         activate(4)
+        open_dh(5, after=("a", 4))
+        gather_plain(FIRST, range(6, 8), ALL_ROWS[:2])
+        gather_plain(FIRST, range(6, 8), ALL_ROWS[2:])
         activate(5)
-        gather_plain(SECOND, 6, 8)
-
-        apply_gate(SECOND, 3, 4)
-        turn(1, 3, 4)
-        picked[FIRST, 4] = middle_rows
-        apply_gate(FIRST, 4, 6)
-        apply_gate(SECOND, 4, 6)
-        open_dh(5, after=("a", 3))
-        turn(1, 4, 6)
-        picked[FIRST, 4] = last_row
-        apply_gate(FIRST, 4, 6, engine=nc.gpsimd, place="gate1_4")
-        turn(0, 4, 6)
-        apply_gate(FIRST, 6, 8, engine=nc.gpsimd, place="gate0_4")
-        product(0, place="gate1_3")
+        gather_plain(SECOND, range(6, 8))
+        gather_gated(SECOND, SECONDS, 0, room("g_w3", SECONDS, ONE)[:, 0, :])
+        gather_gated(FIRST, FIRSTS, 0, room("g_w2", FIRSTS, ONE)[:, 0, :])
+        gather_gated(SECOND, SECONDS, 1, room("g_w0", SECONDS, ONE)[:, 0, :])
+        gather_gated(FIRST, FIRSTS, 1, room("g_w1", FIRSTS, ONE)[:, 0, :])
+        gather_gated(SECOND, SECONDS, 2, room("seconds2", SECONDS, ONE)[:, 0, :])
+        apply_gate(SECOND, range(3, 4))
+        turn(SECOND, range(3, 4))
+        apply_gate(SECOND, range(4, 6))
+        turn(SECOND, range(4, 5))
+        gather_gated(FIRST, FIRSTS, 2, room("gate1_3", FIRSTS, ONE)[:, 0, :])
+        gather_gated(SECOND, SECONDS, 3, room("gate1_4", SECONDS, ONE)[:, 0, :])
+        apply_gate(FIRST, range(4, 5))
+        turn(FIRST, range(4, 5))
+        turn(SECOND, range(5, 6))
+        gather_gated(FIRST, FIRSTS, 3, room("gate1_0", FIRSTS, ONE)[:, 0, :])
+        apply_gate(FIRST, range(5, 6), place=room("gate0_4", ONE, ALL_ROWS)[:])
+        turn(FIRST, range(5, 6))
+        late = room("gate0_0", range(6, 8), ALL_ROWS)
+        apply_gate(FIRST, range(6, 8), ALL_ROWS[:2], engine=nc.gpsimd, place=late[:, :2, :])
+        apply_gate(FIRST, range(6, 8), ALL_ROWS[2:], engine=nc.gpsimd, place=late[:, 2:, :])
+        first_factor(4)
+        product(0)
         product(1)
-        turn_back(0, after=("dh", 0))
+        turn_back(0, after=("dh", 4))
         product(2)
         first_factor(3)
-        first_factor(4)
         first_factor(5)
-        weave(0)
-        turn_a(6, after=("a", 4))
-        turn_a(7, after=("a", 5))
-        open_dh(6, after=("dh", 1))
-        open_dh(7, after=("dh", 2))
-        turn(0, 6, 8)
-        product(3)
-        turn_back(1, after=("dh", 3))
-        product(4)
         activate(6)
-        activate(7)
+        weave(0)
+        open_dh(6, after=("dh", 0))
+        open_dh(7, after=("dh", 1))
+        turn(FIRST, range(6, 8))
+        product(3)
+        turn_back(1, after=("dh", 2))
+        turn_a(7, after=("dh", 5))
+        product(4)
+        apply_gate(SECOND, range(6, 7))
+        turn(SECOND, range(6, 7))
+        apply_gate(SECOND, range(7, 8))
+        turn(SECOND, range(7, 8))
         weave(1)
-        apply_gate(SECOND, 6, 8)
-        turn(1, 6, 8)
+        activate(7)
         product(5)
-        turn_back(2, after=("dh", 4))
-        weave(2)
+        turn_back(2, after=("a", 5))
         quantise(0)
         finish(0, after=("back", 0))
         first_factor(6)
-        first_factor(7)
         quantise(1)
+        finish(1, after=("dh", 3))
+        first_factor(7)
+        weave(2)
         product(6)
-        turn_back(3, after=("dh", 5))
+        turn_back(3, after=("back", 1))
         product(7)
         turn_back(4, after=("dh", 6))
+        quantise(2)
         weave(3)
         weave(4)
-        quantise(2)
-        finish(1, after=("a", 6), on_vector=True)
+        finish(2, after=("a", 6))
         quantise(3)
         quantise(4)
-        finish(2, after=("a", 7))
-        finish(3, after=("back", 1))
-        finish(4, after=("dh", 7), on_vector=True)
+        finish(3, after=("a", 7), on_vector=True)
+        finish(4, after=("dh", 7))

@@ -27,7 +27,7 @@ ALL_ROWS = range(ROW_BLOCKS)
 CHUNKS = (range(0, 2), range(2, 4), range(4, 6), range(6, 7), range(7, 8))
 BOTH = range(2)
 FIRST, SECOND = BOTH
-GATE_PIECES = ((range(0, 4), range(4, 5), range(5, 6), range(6, 8)), (range(0, 3), range(3, 4), range(4, 6), range(6, 8)))
+GATE_PIECES = ((range(0, 4), range(4, 5), range(5, 6), range(6, 8)), (range(0, 3), range(3, 4), range(4, 5), range(5, 6), range(6, 8)))
 EARLY = range(0, 3)
 
 
@@ -106,7 +106,7 @@ def tile_moe_sub_silu_kernel(
         load_a(6, 8)
         for s, lst in enumerate((pos1, pos2)):
             nc.sync.dma_start(token_slots[s][:], lst)
-        for n in range(4):
+        for n in range(5):
             for s, pieces in enumerate(GATE_PIECES):
                 for piece in pieces[n : n + 1]:
                     nc.sync.dma_start(gates[s, piece.start][0][:], gate[s, :, piece.start * P : piece.stop * P])
@@ -117,19 +117,20 @@ def tile_moe_sub_silu_kernel(
         def block_columns(tile, r):
             return tile[:].rearrange("t (u r q d) -> t r q u d", u=2, r=ROW_BLOCKS, d=2)[:, r]
 
-        a_turned, factors = {}, {}
+        a_turned, silus, tanhs, slopes = {}, {}, {}, {}
 
         def turn_a(b, after=None):
             a_turned[b] = bank(("a", b), [P, H], after)
             for r in ALL_ROWS:
                 nc.tensor.transpose(block_columns(a_turned[b], r), a_sb[b][:, r, :], ident[:])
 
-        def silu(b):
-            factors[b] = keep.tile([P, 2, H], F32, name=f"factors{b}", align_bytes=64)
-            nc.scalar.activation(factors[b][:, 0, :], a_turned[b][:], ACT.Silu, scale=-1.0)
+        def silu(b, place=None):
+            silus[b] = keep.tile([P, H], F32, name=place or f"silu{b}", align_bytes=64)
+            nc.scalar.activation(silus[b][:], a_turned[b][:], ACT.Silu, scale=-1.0)
 
-        def tanh(b):
-            nc.scalar.activation(factors[b][:, 1, :], a_turned[b][:], ACT.Tanh, scale=-0.5)
+        def tanh(b, place=None):
+            tanhs[b] = keep.tile([P, H], F32, name=place or f"tanh{b}", align_bytes=64)
+            nc.scalar.activation(tanhs[b][:], a_turned[b][:], ACT.Tanh, scale=-0.5)
 
         def activate(b):
             silu(b)
@@ -137,9 +138,12 @@ def tile_moe_sub_silu_kernel(
 
         def early_slope(b):
             turn_a(b)
-            activate(b)
-            nc.gpsimd.tensor_scalar(factors[b][:], factors[b][:], 1.0, -1.0, ALU.mult, ALU.add)
-            nc.gpsimd.tensor_tensor(factors[b][:, 0, :], factors[b][:, 0, :], factors[b][:, 1, :], ALU.mult)
+            both = keep.tile([P, 2, H], F32, name=f"factors{b}", align_bytes=64)
+            nc.scalar.activation(both[:, 0, :], a_turned[b][:], ACT.Silu, scale=-1.0)
+            nc.scalar.activation(both[:, 1, :], a_turned[b][:], ACT.Tanh, scale=-0.5)
+            nc.gpsimd.tensor_scalar(both[:], both[:], 1.0, -1.0, ALU.mult, ALU.add)
+            nc.gpsimd.tensor_tensor(both[:, 0, :], both[:, 0, :], both[:, 1, :], ALU.mult)
+            slopes[b] = both[:, 0, :]
 
         for b in EARLY:
             early_slope(b)
@@ -177,7 +181,6 @@ def tile_moe_sub_silu_kernel(
             for r in ALL_ROWS:
                 expert_pass(e, r)
 
-        da_w = keep.tile([P, T], U32, name="da_w", align_bytes=64)
         da_s = keep.tile([P, T], U8, name="da_s", align_bytes=64)
         out_rows = out.rearrange("(kb p) t -> p kb t", p=P)
         picked, block, dh_t, da, da_t, back = {}, {}, {}, {}, {}, {}
@@ -232,18 +235,19 @@ def tile_moe_sub_silu_kernel(
                     )
                     turned[b] = done + 1
 
-        def first_factor(b):
-            nc.vector.scalar_tensor_tensor(
-                factors[b][:, 0, :], factors[b][:, 0, :], 1.0, dh_t[b][:], ALU.subtract, ALU.mult
-            )
+        def first_factor(b, in_place=True):
+            plain = silus[b]
+            if not in_place:
+                silus[b] = keep.tile([P, H], F32, name=f"scaled{b}", align_bytes=64)
+            nc.vector.scalar_tensor_tensor(silus[b][:], plain[:], 1.0, dh_t[b][:], ALU.subtract, ALU.mult)
 
         def product(b, place=None):
             da_t[b] = keep.tile([P, H], BF16, name=place or f"da_t{b}", align_bytes=64)
             if b in EARLY:
-                nc.vector.tensor_tensor(da_t[b][:], factors[b][:, 0, :], dh_t[b][:], ALU.mult)
+                nc.vector.tensor_tensor(da_t[b][:], slopes[b], dh_t[b][:], ALU.mult)
             else:
                 nc.vector.scalar_tensor_tensor(
-                    da_t[b][:], factors[b][:, 1, :], 1.0, factors[b][:, 0, :], ALU.subtract, ALU.mult
+                    da_t[b][:], tanhs[b][:], 1.0, silus[b][:], ALU.subtract, ALU.mult
                 )
 
         def turn_back(c, after):
@@ -264,7 +268,7 @@ def tile_moe_sub_silu_kernel(
             tokens = slice(CHUNKS[c].start * P, CHUNKS[c].stop * P)
             nc.vector.quantize_mx(da_w[:, tokens].bitcast(E5M2), da_s[:, tokens], da[c][:])
 
-        def finish(c, after, on_vector=False):
+        def finish(c, after, on_vector=False, place=None):
             tokens = slice(CHUNKS[c].start * P, CHUNKS[c].stop * P)
             width = len(CHUNKS[c]) * P
             sums = bank(("out", c), [P, K // P, width], after)
@@ -278,7 +282,7 @@ def tile_moe_sub_silu_kernel(
                     start=True,
                     stop=True,
                 )
-            res = keep.tile([P, K // P, width], F32, name=f"res{c}")
+            res = keep.tile([P, K // P, width], F32, name=place or f"res{c}", align_bytes=64)
             if on_vector:
                 nc.vector.tensor_scalar(res[:], sums[:], 0.5, None, ALU.mult)
             else:
@@ -309,12 +313,13 @@ def tile_moe_sub_silu_kernel(
         gather_gated(SECOND, SECONDS, 2, room("seconds2", SECONDS, ONE)[:, 0, :])
         apply_gate(SECOND, range(3, 4))
         turn(SECOND, range(3, 4))
-        apply_gate(SECOND, range(4, 6))
+        apply_gate(SECOND, range(4, 5))
         turn(SECOND, range(4, 5))
         gather_gated(FIRST, FIRSTS, 2, room("gate1_3", FIRSTS, ONE)[:, 0, :])
         gather_gated(SECOND, SECONDS, 3, room("gate1_4", SECONDS, ONE)[:, 0, :])
         apply_gate(FIRST, range(4, 5))
         turn(FIRST, range(4, 5))
+        apply_gate(SECOND, range(5, 6))
         turn(SECOND, range(5, 6))
         gather_gated(FIRST, FIRSTS, 3, room("gate1_0", FIRSTS, ONE)[:, 0, :])
         apply_gate(FIRST, range(5, 6), place=room("gate0_4", ONE, ALL_ROWS)[:])
@@ -323,45 +328,48 @@ def tile_moe_sub_silu_kernel(
         apply_gate(FIRST, range(6, 8), ALL_ROWS[:2], engine=nc.gpsimd, place=late[:, :2, :])
         apply_gate(FIRST, range(6, 8), ALL_ROWS[2:], engine=nc.gpsimd, place=late[:, 2:, :])
         first_factor(4)
+        turn_a(7, after=("dh", 4))
         product(0)
         product(1)
-        turn_back(0, after=("dh", 4))
+        turn_back(0, after=("a", 5))
         product(2)
         first_factor(3)
         first_factor(5)
-        activate(6)
+        silu(6)
         weave(0)
         open_dh(6, after=("dh", 0))
         open_dh(7, after=("dh", 1))
         turn(FIRST, range(6, 8))
         product(3)
         turn_back(1, after=("dh", 2))
-        turn_a(7, after=("dh", 5))
         product(4)
-        apply_gate(SECOND, range(6, 7))
+        apply_gate(SECOND, range(6, 7), place=room("tanh3", ONE, ALL_ROWS)[:])
         turn(SECOND, range(6, 7))
-        apply_gate(SECOND, range(7, 8))
+        product(5)
+        turn_back(2, after=("dh", 5))
+        apply_gate(SECOND, range(7, 8), place=room("tanh4", ONE, ALL_ROWS)[:])
         turn(SECOND, range(7, 8))
         weave(1)
-        activate(7)
-        product(5)
-        turn_back(2, after=("a", 5))
+        silu(7, place="da_t3")
+        tanh(6, place="da_t4")
+        weave(2)
+        tanh(7, place="da_t5")
+        da_w = keep.tile([P, T], U32, name="tanh5", align_bytes=64)
         quantise(0)
         finish(0, after=("back", 0))
         first_factor(6)
         quantise(1)
         finish(1, after=("dh", 3))
-        first_factor(7)
-        weave(2)
-        product(6)
+        first_factor(7, in_place=False)
+        quantise(2)
+        product(6, place="da_t3")
         turn_back(3, after=("back", 1))
         product(7)
         turn_back(4, after=("dh", 6))
-        quantise(2)
+        finish(2, after=("a", 6), on_vector=True, place="da_t4")
         weave(3)
         weave(4)
-        finish(2, after=("a", 6))
         quantise(3)
         quantise(4)
-        finish(3, after=("a", 7), on_vector=True)
+        finish(3, after=("a", 7), on_vector=True, place="da4")
         finish(4, after=("dh", 7))

@@ -27,7 +27,7 @@ ALL_ROWS = range(ROW_BLOCKS)
 CHUNKS = (range(0, 2), range(2, 4), range(4, 6), range(6, 7), range(7, 8))
 BOTH = range(2)
 FIRST, SECOND = BOTH
-GATE_PIECES = ((range(0, 4), range(4, 5), range(5, 6), range(6, 8)), (range(0, 3), range(3, 4), range(4, 5), range(5, 6), range(6, 8)))
+GATE_PIECES = ((range(0, 4), range(4, 6)), (range(0, 3), range(3, 4), range(4, 5), range(5, 6), range(6, 8)))
 EARLY = range(0, 3)
 
 
@@ -66,6 +66,7 @@ def tile_moe_sub_silu_kernel(
                 tile = keep.tile([P, len(piece) * P], F32, name=f"gate{s}_{piece.start}", align_bytes=64)
                 for b in piece:
                     gates[s, b] = (tile, piece.start)
+        late_gate = keep.tile([P, 2, 2 * P], F32, name="late_gate", align_bytes=64)
         ident = keep.tile([P, P], F32, name="ident")
 
         def gate_of(s, tiles):
@@ -110,6 +111,7 @@ def tile_moe_sub_silu_kernel(
             for s, pieces in enumerate(GATE_PIECES):
                 for piece in pieces[n : n + 1]:
                     nc.sync.dma_start(gates[s, piece.start][0][:], gate[s, :, piece.start * P : piece.stop * P])
+        nc.sync.dma_start(late_gate[:], gate[FIRST, :, 6 * P :].unsqueeze(1).to_broadcast([P, 2, 2 * P]))
         nc.sync.dma_start(w1_w[:].bitcast(I32), w1t_words[0].bitcast(I32))
         for j in range(SCALE_ROWS):
             nc.sync.dma_start(w1_s[j:P:QUADRANT, :].bitcast(I32), w1_rows[j].bitcast(I32))
@@ -181,7 +183,7 @@ def tile_moe_sub_silu_kernel(
             for r in ALL_ROWS:
                 expert_pass(e, r)
 
-        da_s = keep.tile([P, T], U8, name="da_s", align_bytes=64)
+        codes, scales = {}, {}
         out_rows = out.rearrange("(kb p) t -> p kb t", p=P)
         picked, block, dh_t, da, da_t, back = {}, {}, {}, {}, {}, {}
 
@@ -208,10 +210,11 @@ def tile_moe_sub_silu_kernel(
                 for b in tiles:
                     picked[s, b, r] = (tile, tiles.start, rows.start)
 
-        def apply_gate(s, tiles, rows=ALL_ROWS, engine=nc.vector, place=None):
+        def apply_gate(s, tiles, rows=ALL_ROWS, engine=nc.vector, place=None, wide=None):
             tile, first, top = picked[s, tiles.start, rows.start]
             plain = tile[:, rows.start - top : rows.stop - top, (tiles.start - first) * P : (tiles.stop - first) * P]
-            wide = gate_of(s, tiles).unsqueeze(1).to_broadcast(plain.shape)
+            if wide is None:
+                wide = gate_of(s, tiles).unsqueeze(1).to_broadcast(plain.shape)
             gated = plain if place is None else place
             engine.tensor_tensor(gated, plain, wide, ALU.mult)
             note_blocks(s, tiles, rows, gated)
@@ -264,9 +267,11 @@ def tile_moe_sub_silu_kernel(
                 back[c][:].rearrange("p b u t -> p b t u"),
             )
 
-        def quantise(c):
-            tokens = slice(CHUNKS[c].start * P, CHUNKS[c].stop * P)
-            nc.vector.quantize_mx(da_w[:, tokens].bitcast(E5M2), da_s[:, tokens], da[c][:])
+        def quantise(c, place=None):
+            width = len(CHUNKS[c]) * P
+            codes[c] = keep.tile([P, width], U32, name=place or f"codes{c}", align_bytes=64)
+            scales[c] = keep.tile([P, width], U8, name=f"scales{c}", align_bytes=64)
+            nc.vector.quantize_mx(codes[c][:].bitcast(E5M2), scales[c][:], da[c][:])
 
         def finish(c, after, on_vector=False, place=None):
             tokens = slice(CHUNKS[c].start * P, CHUNKS[c].stop * P)
@@ -277,8 +282,8 @@ def tile_moe_sub_silu_kernel(
                     sums[:, kb, :],
                     lhsT=w1_w[:, 2 * P * kb : 2 * P * (kb + 1)].bitcast(E2M1),
                     lhsT_scale=w1_s[:, P * kb : P * (kb + 1)],
-                    rhs=da_w[:, tokens].bitcast(E5M2),
-                    rhs_scale=da_s[:, tokens],
+                    rhs=codes[c][:].bitcast(E5M2),
+                    rhs_scale=scales[c][:],
                     start=True,
                     stop=True,
                 )
@@ -304,8 +309,9 @@ def tile_moe_sub_silu_kernel(
         open_dh(5, after=("a", 4))
         gather_plain(FIRST, range(6, 8), ALL_ROWS[:2])
         gather_plain(FIRST, range(6, 8), ALL_ROWS[2:])
-        activate(5)
+        silu(5)
         gather_plain(SECOND, range(6, 8))
+        tanh(5)
         gather_gated(SECOND, SECONDS, 0, room("g_w3", SECONDS, ONE)[:, 0, :])
         gather_gated(FIRST, FIRSTS, 0, room("g_w2", FIRSTS, ONE)[:, 0, :])
         gather_gated(SECOND, SECONDS, 1, room("g_w0", SECONDS, ONE)[:, 0, :])
@@ -317,59 +323,59 @@ def tile_moe_sub_silu_kernel(
         turn(SECOND, range(4, 5))
         gather_gated(FIRST, FIRSTS, 2, room("gate1_3", FIRSTS, ONE)[:, 0, :])
         gather_gated(SECOND, SECONDS, 3, room("gate1_4", SECONDS, ONE)[:, 0, :])
-        apply_gate(FIRST, range(4, 5))
-        turn(FIRST, range(4, 5))
         apply_gate(SECOND, range(5, 6))
         turn(SECOND, range(5, 6))
         gather_gated(FIRST, FIRSTS, 3, room("gate1_0", FIRSTS, ONE)[:, 0, :])
-        apply_gate(FIRST, range(5, 6), place=room("gate0_4", ONE, ALL_ROWS)[:])
-        turn(FIRST, range(5, 6))
-        late = room("gate0_0", range(6, 8), ALL_ROWS)
-        apply_gate(FIRST, range(6, 8), ALL_ROWS[:2], engine=nc.gpsimd, place=late[:, :2, :])
-        apply_gate(FIRST, range(6, 8), ALL_ROWS[2:], engine=nc.gpsimd, place=late[:, 2:, :])
-        first_factor(4)
-        turn_a(7, after=("dh", 4))
+        apply_gate(FIRST, range(4, 6), ALL_ROWS[:3], place=room("gate1_5", range(2), ALL_ROWS[:3])[:])
+        turn(FIRST, range(4, 6), ALL_ROWS[:3])
+        late = room("gate0_0", range(10), ONE)
+        apply_gate(FIRST, range(4, 6), ALL_ROWS[3:], engine=nc.gpsimd, place=late[:, :, : 2 * P])
+        turn(FIRST, range(4, 6), ALL_ROWS[3:])
+        for n, rows in enumerate((ALL_ROWS[:2], ALL_ROWS[2:])):
+            part = late[:, 0, (2 + 4 * n) * P : (6 + 4 * n) * P].rearrange("p (r t) -> p r t", r=2)
+            apply_gate(FIRST, range(6, 8), rows, engine=nc.gpsimd, place=part, wide=late_gate[:])
         product(0)
+        turn_a(7, after=("dh", 0))
         product(1)
-        turn_back(0, after=("a", 5))
         product(2)
         first_factor(3)
+        turn_back(0, after=("dh", 3))
+        first_factor(4)
         first_factor(5)
         silu(6)
         weave(0)
-        open_dh(6, after=("dh", 0))
-        open_dh(7, after=("dh", 1))
+        silu(7, place="da_t1")
+        open_dh(6, after=("dh", 1))
+        open_dh(7, after=("dh", 2))
         turn(FIRST, range(6, 8))
         product(3)
-        turn_back(1, after=("dh", 2))
+        turn_back(1, after=("dh", 4))
         product(4)
-        apply_gate(SECOND, range(6, 7), place=room("tanh3", ONE, ALL_ROWS)[:])
+        apply_gate(SECOND, range(6, 7))
         turn(SECOND, range(6, 7))
-        product(5)
-        turn_back(2, after=("dh", 5))
-        apply_gate(SECOND, range(7, 8), place=room("tanh4", ONE, ALL_ROWS)[:])
+        apply_gate(SECOND, range(7, 8))
         turn(SECOND, range(7, 8))
         weave(1)
-        silu(7, place="da_t3")
-        tanh(6, place="da_t4")
-        weave(2)
-        tanh(7, place="da_t5")
-        da_w = keep.tile([P, T], U32, name="tanh5", align_bytes=64)
-        quantise(0)
+        tanh(6, place="da_t3")
+        tanh(7, place="da_t4")
+        product(5)
+        turn_back(2, after=("dh", 5))
+        quantise(0, place="tanh4")
         finish(0, after=("back", 0))
         first_factor(6)
         quantise(1)
-        finish(1, after=("dh", 3))
-        first_factor(7, in_place=False)
-        quantise(2)
-        product(6, place="da_t3")
+        finish(1, after=("a", 5))
+        first_factor(7)
+        weave(2)
+        product(6)
         turn_back(3, after=("back", 1))
         product(7)
         turn_back(4, after=("dh", 6))
-        finish(2, after=("a", 6), on_vector=True, place="da_t4")
+        quantise(2, place="da_t3")
         weave(3)
         weave(4)
         quantise(3)
         quantise(4)
+        finish(2, after=("a", 6))
         finish(3, after=("a", 7), on_vector=True, place="da4")
         finish(4, after=("dh", 7))

@@ -24,11 +24,14 @@ SCALE_ROWS = 4
 BANKS = 8
 ROW_BLOCKS = H // P
 ALL_ROWS = range(ROW_BLOCKS)
+ONE_ROW = range(1)
+FIRST, SECOND = 0, 1
 CHUNKS = (range(0, 2), range(2, 4), range(4, 6), range(6, 7), range(7, 8))
-BOTH = range(2)
-FIRST, SECOND = BOTH
-GATE_PIECES = ((range(0, 4), range(4, 6)), (range(0, 3), range(3, 4), range(4, 5), range(5, 6), range(6, 8)))
-EARLY = range(0, 3)
+EARLY = (1, 2, 0)
+VECTOR_TILES = (range(0, 4), range(0, 3))
+MIDDLE, LAST = range(4, 6), range(6, 8)
+ON_VECTOR = ((2, 0), (2, 1), (3, 0), (3, 1))
+GATE_PIECES = ((range(0, 4), MIDDLE), (range(0, 3), range(3, 4), range(4, 5), range(5, 6), LAST))
 
 
 def tile_moe_sub_silu_kernel(
@@ -52,7 +55,7 @@ def tile_moe_sub_silu_kernel(
             return psum.tile(shape, F32, name=f"bank{bank_of[tenant]}")
 
         slot_tokens = keep.tile([P, E * C // PER_COL], U16, name="slot_tokens")
-        token_slots = [keep.tile([P, T // PER_COL], U16, name=f"token_slots{s}") for s in range(2)]
+        token_slots = [keep.tile([P, T // PER_COL], U16, name=f"token_slots{s}") for s in (FIRST, SECOND)]
         dy_w = keep.tile([P, T], I32, name="dy_w", align_bytes=64)
         dy_s = keep.tile([P, T], U8, name="dy_s", align_bytes=64)
         w2_first = keep.tile([P, 1, 2 * H], U8, name="w2_first", align_bytes=64)
@@ -66,7 +69,7 @@ def tile_moe_sub_silu_kernel(
                 tile = keep.tile([P, len(piece) * P], F32, name=f"gate{s}_{piece.start}", align_bytes=64)
                 for b in piece:
                     gates[s, b] = (tile, piece.start)
-        late_gate = keep.tile([P, 2, 2 * P], F32, name="late_gate", align_bytes=64)
+        last_gate = keep.tile([P, 2, len(LAST) * P], F32, name="last_gate", align_bytes=64)
         ident = keep.tile([P, P], F32, name="ident")
 
         def gate_of(s, tiles):
@@ -95,26 +98,34 @@ def tile_moe_sub_silu_kernel(
                 dy_s[QUADRANT * q : QUADRANT * (q + 1), :].bitcast(I32),
                 rows.unsqueeze(0).to_broadcast([QUADRANT // SCALE_ROWS, SCALE_ROWS, T // 4]),
             )
-        load_a(0, 1)
-        load_a(1, 2)
+        for b in EARLY[:2]:
+            load_a(b, b + 1)
         nc.sync.dma_start(dy_w[:], dy_words[0].rearrange("p t d -> p (t d)").bitcast(I32))
-        load_a(2, 3)
+        load_a(EARLY[2], EARLY[2] + 1)
         nc.sync.dma_start(w2_first[:].bitcast(I32), w2t_words[0:1, 0].rearrange("e p b -> p e b").bitcast(I32))
         for j in range(SCALE_ROWS):
             nc.sync.dma_start(w2_s[j:P:QUADRANT, :, :].bitcast(I32), w2_rows[j].bitcast(I32))
         nc.sync.dma_start(w2_rest[:].bitcast(I32), w2t_words[1:E, 0].rearrange("e p b -> p e b").bitcast(I32))
-        load_a(3, 6)
-        load_a(6, 8)
+        load_a(3, LAST.start)
+        load_a(LAST.start, LAST.stop)
+
+        def load_gate(s, first):
+            tile = gates[s, first][0]
+            nc.sync.dma_start(tile[:], gate[s, :, first * P : first * P + tile.shape[1]])
+
         for s, lst in enumerate((pos1, pos2)):
             nc.sync.dma_start(token_slots[s][:], lst)
-        for n in range(5):
-            for s, pieces in enumerate(GATE_PIECES):
-                for piece in pieces[n : n + 1]:
-                    nc.sync.dma_start(gates[s, piece.start][0][:], gate[s, :, piece.start * P : piece.stop * P])
-        nc.sync.dma_start(late_gate[:], gate[FIRST, :, 6 * P :].unsqueeze(1).to_broadcast([P, 2, 2 * P]))
-        nc.sync.dma_start(w1_w[:].bitcast(I32), w1t_words[0].bitcast(I32))
+        load_gate(FIRST, 0)
+        load_gate(SECOND, 0)
+        load_gate(FIRST, MIDDLE.start)
+        load_gate(SECOND, LAST.start)
+        load_gate(SECOND, 3)
+        nc.sync.dma_start(last_gate[:], gate[FIRST, :, LAST.start * P :].unsqueeze(1).to_broadcast(last_gate.shape))
         for j in range(SCALE_ROWS):
             nc.sync.dma_start(w1_s[j:P:QUADRANT, :].bitcast(I32), w1_rows[j].bitcast(I32))
+        for b in MIDDLE:
+            load_gate(SECOND, b)
+        nc.sync.dma_start(w1_w[:].bitcast(I32), w1t_words[0].bitcast(I32))
 
         def block_columns(tile, r):
             return tile[:].rearrange("t (u r q d) -> t r q u d", u=2, r=ROW_BLOCKS, d=2)[:, r]
@@ -130,35 +141,32 @@ def tile_moe_sub_silu_kernel(
             silus[b] = keep.tile([P, H], F32, name=place or f"silu{b}", align_bytes=64)
             nc.scalar.activation(silus[b][:], a_turned[b][:], ACT.Silu, scale=-1.0)
 
-        def tanh(b, place=None):
-            tanhs[b] = keep.tile([P, H], F32, name=place or f"tanh{b}", align_bytes=64)
-            nc.scalar.activation(tanhs[b][:], a_turned[b][:], ACT.Tanh, scale=-0.5)
+        def tanh(b, into=None):
+            tanhs[b] = keep.tile([P, H], F32, name=f"tanh{b}", align_bytes=64)[:] if into is None else into
+            nc.scalar.activation(tanhs[b], a_turned[b][:], ACT.Tanh, scale=-0.5)
 
         def activate(b):
             silu(b)
             tanh(b)
 
-        def early_slope(b):
+        for b in EARLY:
             turn_a(b)
             both = keep.tile([P, 2, H], F32, name=f"factors{b}", align_bytes=64)
             nc.scalar.activation(both[:, 0, :], a_turned[b][:], ACT.Silu, scale=-1.0)
             nc.scalar.activation(both[:, 1, :], a_turned[b][:], ACT.Tanh, scale=-0.5)
             nc.gpsimd.tensor_scalar(both[:], both[:], 1.0, -1.0, ALU.mult, ALU.add)
-            nc.gpsimd.tensor_tensor(both[:, 0, :], both[:, 0, :], both[:, 1, :], ALU.mult)
-            slopes[b] = both[:, 0, :]
-
-        for b in EARLY:
-            early_slope(b)
+            slopes[b] = keep.tile([P, H], F32, name=f"slope{b}", align_bytes=64)
+            nc.gpsimd.tensor_tensor(slopes[b][:], both[:, 0, :], both[:, 1, :], ALU.mult)
 
         y = [keep.tile([P, E * C], F32, name=f"y{r}") for r in ALL_ROWS]
         g_s, g_w = {}, {}
 
         def gather_slots(e):
-            entries = slot_tokens[:, e * C // PER_COL : (e + 1) * C // PER_COL]
+            slots = slot_tokens[:, e * C // PER_COL : (e + 1) * C // PER_COL]
             g_s[e] = keep.tile([P, C], U8, name=f"g_s{e % 2}", align_bytes=64)
             g_w[e] = keep.tile([P, C], U32, name=f"g_w{e}", align_bytes=64)
-            nc.vector.tensor_copy(g_s[e][:], dy_s[:].indirect(entries))
-            nc.vector.tensor_copy(g_w[e][:], dy_w[:].bitcast(U32).indirect(entries))
+            nc.vector.tensor_copy(g_s[e][:], dy_s[:].indirect(slots))
+            nc.vector.tensor_copy(g_w[e][:], dy_w[:].bitcast(U32).indirect(slots))
 
         def expert_pass(e, r):
             words = w2_first[:, 0, :] if e == 0 else w2_rest[:, e - 1, :]
@@ -177,15 +185,17 @@ def tile_moe_sub_silu_kernel(
             else:
                 nc.scalar.copy(y[r][:, e * C : (e + 1) * C], sums[:])
 
-        ON_VECTOR = ((2, 0), (2, 1), (3, 0), (3, 1))
         for e in range(E):
             gather_slots(e)
             for r in ALL_ROWS:
                 expert_pass(e, r)
 
-        codes, scales = {}, {}
         out_rows = out.rearrange("(kb p) t -> p kb t", p=P)
-        picked, block, dh_t, da, da_t, back = {}, {}, {}, {}, {}, {}
+        picked = {}
+        block = {}
+        dh_t, da_t = {}, {}
+        turned = {}
+        back, da, codes, scales = {}, {}, {}, {}
 
         def entries(s, tiles):
             return token_slots[s][:, tiles.start * P // PER_COL : tiles.stop * P // PER_COL]
@@ -198,10 +208,12 @@ def tile_moe_sub_silu_kernel(
         def room(place, tiles, rows):
             return keep.tile([P, len(rows), len(tiles) * P], F32, name=place, align_bytes=64)
 
-        def gather_gated(s, tiles, r, columns):
-            nc.vector.tensor_tensor(columns, y[r][:].indirect(entries(s, tiles)), gate_of(s, tiles), ALU.mult)
-            note_blocks(s, tiles, ALL_ROWS[r : r + 1], columns.unsqueeze(1))
-            turn(s, tiles, ALL_ROWS[r : r + 1])
+        def gather_gated(s, r, place):
+            tiles, rows = VECTOR_TILES[s], ALL_ROWS[r : r + 1]
+            columns = room(place, tiles, rows)
+            nc.vector.tensor_tensor(columns[:, 0, :], y[r][:].indirect(entries(s, tiles)), gate_of(s, tiles), ALU.mult)
+            note_blocks(s, tiles, rows, columns)
+            turn(s, tiles, rows)
 
         def gather_plain(s, tiles, rows=ALL_ROWS):
             tile = room(f"picked{s}_{tiles.start}_{rows.start}", tiles, rows)
@@ -210,19 +222,21 @@ def tile_moe_sub_silu_kernel(
                 for b in tiles:
                     picked[s, b, r] = (tile, tiles.start, rows.start)
 
-        def apply_gate(s, tiles, rows=ALL_ROWS, engine=nc.vector, place=None, wide=None):
+        def apply_gate(s, tiles, rows=ALL_ROWS, engine=nc.vector, into=None, wide=None):
             tile, first, top = picked[s, tiles.start, rows.start]
             plain = tile[:, rows.start - top : rows.stop - top, (tiles.start - first) * P : (tiles.stop - first) * P]
             if wide is None:
                 wide = gate_of(s, tiles).unsqueeze(1).to_broadcast(plain.shape)
-            gated = plain if place is None else place
+            gated = plain if into is None else into
             engine.tensor_tensor(gated, plain, wide, ALU.mult)
             note_blocks(s, tiles, rows, gated)
 
-        def open_dh(b, after=None):
-            dh_t[b] = bank(("dh", b), [P, H], after)
+        def gate_and_turn(s, b):
+            apply_gate(s, range(b, b + 1))
+            turn(s, range(b, b + 1))
 
-        turned = {}
+        def open_dh(b, after):
+            dh_t[b] = bank(("dh", b), [P, H], after)
 
         def turn(s, tiles, rows=ALL_ROWS):
             for b in tiles:
@@ -238,20 +252,15 @@ def tile_moe_sub_silu_kernel(
                     )
                     turned[b] = done + 1
 
-        def first_factor(b, in_place=True):
-            plain = silus[b]
-            if not in_place:
-                silus[b] = keep.tile([P, H], F32, name=f"scaled{b}", align_bytes=64)
-            nc.vector.scalar_tensor_tensor(silus[b][:], plain[:], 1.0, dh_t[b][:], ALU.subtract, ALU.mult)
+        def first_factor(b):
+            nc.vector.scalar_tensor_tensor(silus[b][:], silus[b][:], 1.0, dh_t[b][:], ALU.subtract, ALU.mult)
 
-        def product(b, place=None):
-            da_t[b] = keep.tile([P, H], BF16, name=place or f"da_t{b}", align_bytes=64)
+        def product(b):
+            da_t[b] = keep.tile([P, H], BF16, name=f"da_t{b}", align_bytes=64)
             if b in EARLY:
-                nc.vector.tensor_tensor(da_t[b][:], slopes[b], dh_t[b][:], ALU.mult)
+                nc.vector.tensor_tensor(da_t[b][:], slopes[b][:], dh_t[b][:], ALU.mult)
             else:
-                nc.vector.scalar_tensor_tensor(
-                    da_t[b][:], tanhs[b][:], 1.0, silus[b][:], ALU.subtract, ALU.mult
-                )
+                nc.vector.scalar_tensor_tensor(da_t[b][:], tanhs[b], 1.0, silus[b][:], ALU.subtract, ALU.mult)
 
         def turn_back(c, after):
             back[c] = bank(("back", c), [P, len(CHUNKS[c]), 2, P], after)
@@ -260,20 +269,20 @@ def tile_moe_sub_silu_kernel(
                 for u in range(2):
                     nc.tensor.transpose(back[c][:, n, u, :], pairs[:, u * P : (u + 1) * P], ident[:])
 
-        def weave(c, on_vector=False):
+        def weave(c):
             da[c] = keep.tile([P, len(CHUNKS[c]) * P * PACK], BF16, name=f"da{c}", align_bytes=64)
-            (nc.vector.tensor_copy if on_vector else nc.scalar.copy)(
+            nc.scalar.copy(
                 da[c][:].bitcast(F32).rearrange("p (b t u) -> p b t u", t=P, u=2),
                 back[c][:].rearrange("p b u t -> p b t u"),
             )
 
-        def quantise(c, place=None):
+        def quantise(c):
             width = len(CHUNKS[c]) * P
-            codes[c] = keep.tile([P, width], U32, name=place or f"codes{c}", align_bytes=64)
+            codes[c] = keep.tile([P, width], U32, name=f"codes{c}", align_bytes=64)
             scales[c] = keep.tile([P, width], U8, name=f"scales{c}", align_bytes=64)
             nc.vector.quantize_mx(codes[c][:].bitcast(E5M2), scales[c][:], da[c][:])
 
-        def finish(c, after, on_vector=False, place=None):
+        def finish(c, after, on_vector=False):
             tokens = slice(CHUNKS[c].start * P, CHUNKS[c].stop * P)
             width = len(CHUNKS[c]) * P
             sums = bank(("out", c), [P, K // P, width], after)
@@ -287,7 +296,7 @@ def tile_moe_sub_silu_kernel(
                     start=True,
                     stop=True,
                 )
-            res = keep.tile([P, K // P, width], F32, name=place or f"res{c}", align_bytes=64)
+            res = keep.tile([P, K // P, width], F32, name=f"res{c}", align_bytes=64)
             if on_vector:
                 nc.vector.tensor_scalar(res[:], sums[:], 0.5, None, ALU.mult)
             else:
@@ -299,68 +308,68 @@ def tile_moe_sub_silu_kernel(
         for b, tenant in enumerate(ON_VECTOR):
             open_dh(b, after=("y",) + tenant)
 
-        FIRSTS, SECONDS = range(0, 4), range(0, 3)
-        ONE = range(1)
-        gather_plain(SECOND, range(3, 6))
+        gather_plain(SECOND, range(3, LAST.start))
         activate(3)
         open_dh(4, after=("a", 3))
-        gather_plain(FIRST, range(4, 6))
+        gather_plain(FIRST, MIDDLE)
         activate(4)
         open_dh(5, after=("a", 4))
-        gather_plain(FIRST, range(6, 8), ALL_ROWS[:2])
-        gather_plain(FIRST, range(6, 8), ALL_ROWS[2:])
+        gather_plain(FIRST, LAST, ALL_ROWS[:2])
+        gather_plain(FIRST, LAST, ALL_ROWS[2:])
         silu(5)
-        gather_plain(SECOND, range(6, 8))
+        gather_plain(SECOND, LAST)
         tanh(5)
-        gather_gated(SECOND, SECONDS, 0, room("g_w3", SECONDS, ONE)[:, 0, :])
-        gather_gated(FIRST, FIRSTS, 0, room("g_w2", FIRSTS, ONE)[:, 0, :])
-        gather_gated(SECOND, SECONDS, 1, room("g_w0", SECONDS, ONE)[:, 0, :])
-        gather_gated(FIRST, FIRSTS, 1, room("g_w1", FIRSTS, ONE)[:, 0, :])
-        gather_gated(SECOND, SECONDS, 2, room("seconds2", SECONDS, ONE)[:, 0, :])
-        apply_gate(SECOND, range(3, 4))
-        turn(SECOND, range(3, 4))
-        apply_gate(SECOND, range(4, 5))
-        turn(SECOND, range(4, 5))
-        gather_gated(FIRST, FIRSTS, 2, room("gate1_3", FIRSTS, ONE)[:, 0, :])
-        gather_gated(SECOND, SECONDS, 3, room("gate1_4", SECONDS, ONE)[:, 0, :])
-        apply_gate(SECOND, range(5, 6))
-        turn(SECOND, range(5, 6))
-        gather_gated(FIRST, FIRSTS, 3, room("gate1_0", FIRSTS, ONE)[:, 0, :])
-        apply_gate(FIRST, range(4, 6), ALL_ROWS[:3], place=room("gate1_5", range(2), ALL_ROWS[:3])[:])
-        turn(FIRST, range(4, 6), ALL_ROWS[:3])
-        late = room("gate0_0", range(10), ONE)
-        apply_gate(FIRST, range(4, 6), ALL_ROWS[3:], engine=nc.gpsimd, place=late[:, :, : 2 * P])
-        turn(FIRST, range(4, 6), ALL_ROWS[3:])
+
+        gather_gated(SECOND, 0, "g_w3")
+        gather_gated(FIRST, 0, "g_w2")
+        gather_gated(SECOND, 1, "g_w0")
+        gather_gated(FIRST, 1, f"factors{EARLY[-1]}")
+        gather_gated(SECOND, 2, "seconds2")
+        gate_and_turn(SECOND, 3)
+        gate_and_turn(SECOND, 4)
+        gather_gated(FIRST, 2, "gate1_3")
+        gather_gated(SECOND, 3, "gate1_4")
+        gate_and_turn(SECOND, 5)
+        gather_gated(FIRST, 3, "gate1_0")
+        apply_gate(FIRST, MIDDLE, ALL_ROWS[:3])
+        turn(FIRST, MIDDLE[::-1], ALL_ROWS[:3])
+
+        width = len(LAST) * P
+        late = room("gate0_0", range(5 * len(LAST)), ONE_ROW)
+        apply_gate(FIRST, MIDDLE, ALL_ROWS[3:], engine=nc.gpsimd, into=late[:, :, :width])
+        turn(FIRST, MIDDLE[::-1], ALL_ROWS[3:])
         for n, rows in enumerate((ALL_ROWS[:2], ALL_ROWS[2:])):
-            part = late[:, 0, (2 + 4 * n) * P : (6 + 4 * n) * P].rearrange("p (r t) -> p r t", r=2)
-            apply_gate(FIRST, range(6, 8), rows, engine=nc.gpsimd, place=part, wide=late_gate[:])
+            part = late[:, 0, (1 + 2 * n) * width : (3 + 2 * n) * width].rearrange("p (r t) -> p r t", r=2)
+            apply_gate(FIRST, LAST, rows, engine=nc.gpsimd, into=part, wide=last_gate[:])
+
         product(0)
         turn_a(7, after=("dh", 0))
         product(1)
         product(2)
         first_factor(3)
         turn_back(0, after=("dh", 3))
-        first_factor(4)
         first_factor(5)
+        first_factor(4)
+
         silu(6)
         weave(0)
         silu(7, place="da_t1")
         open_dh(6, after=("dh", 1))
         open_dh(7, after=("dh", 2))
-        turn(FIRST, range(6, 8))
+        turn(FIRST, LAST)
         product(3)
-        turn_back(1, after=("dh", 4))
+        turn_back(1, after=("dh", 5))
         product(4)
-        apply_gate(SECOND, range(6, 7))
-        turn(SECOND, range(6, 7))
-        apply_gate(SECOND, range(7, 8))
-        turn(SECOND, range(7, 8))
+        for b in LAST:
+            gate_and_turn(SECOND, b)
         weave(1)
-        tanh(6, place="da_t3")
-        tanh(7, place="da_t4")
+        last_tanhs = keep.tile([P, len(LAST), H], F32, name="da_t3", align_bytes=64)
+        for n, b in enumerate(LAST):
+            tanh(b, into=last_tanhs[:, n, :])
+
         product(5)
-        turn_back(2, after=("dh", 5))
-        quantise(0, place="tanh4")
+        turn_back(2, after=("dh", 4))
+        quantise(0)
         finish(0, after=("back", 0))
         first_factor(6)
         quantise(1)
@@ -371,11 +380,11 @@ def tile_moe_sub_silu_kernel(
         turn_back(3, after=("back", 1))
         product(7)
         turn_back(4, after=("dh", 6))
-        quantise(2, place="da_t3")
+        quantise(2)
         weave(3)
         weave(4)
         quantise(3)
         quantise(4)
         finish(2, after=("a", 6))
-        finish(3, after=("a", 7), on_vector=True, place="da4")
+        finish(3, after=("a", 7), on_vector=True)
         finish(4, after=("dh", 7))

from contextlib import ExitStack

import concourse.mybir as mybir
from concourse.masks import make_identity

F32 = mybir.dt.float32
BF16 = mybir.dt.bfloat16
I32 = mybir.dt.int32
U32 = mybir.dt.uint32
U16 = mybir.dt.uint16
U8 = mybir.dt.uint8
E5M2 = mybir.dt.float8_e5m2_x4
E2M1 = mybir.dt.float4_e2m1fn_x4
ACT = mybir.ActivationFunctionType
ALU = mybir.AluOpType

K, T, E, C, H, N = 256, 1024, 4, 512, 512, 512
FLOPS = 2 * N * H * E * C + 2 * H * K * T
P = 128
PACK = 4
PER_COL = 16
QUADRANT = 32
SCALE_ROWS = 4
BANKS = 8
ROW_BLOCKS = H // P
ALL_ROWS = range(ROW_BLOCKS)
ONE_ROW = range(1)
FIRST, SECOND = 0, 1
CHUNKS = (range(0, 2), range(2, 4), range(4, 6), range(6, 7), range(7, 8))
EARLY = (1, 2, 0)
VECTOR_TILES = (range(0, 4), range(0, 3))
MIDDLE, LAST = range(4, 6), range(6, 8)
ON_VECTOR = ((2, 0), (2, 1), (3, 0), (3, 1))
GATE_PIECES = ((range(0, 4), MIDDLE), (range(0, 3), range(3, 4), range(4, 5), range(5, 6), LAST))


def tile_moe_sub_silu_kernel(
    tc, dy_words, dy_scales, w2t_words, w2t_scales, w1t_words, w1t_scales, a, gate, offs, pos1, pos2, out
):
    nc = tc.nc

    with ExitStack() as ctx:
        keep = ctx.enter_context(tc.tile_pool(name="keep", bufs=1))
        psum = ctx.enter_context(tc.psum_pool(name="psum", bufs=1))

        bank_of = {}
        ring = []

        def bank(tenant, shape, after=None):
            if after is None:
                bank_of[tenant] = len(ring) % BANKS
                ring.append(tenant)
            else:
                bank_of[tenant] = bank_of[after]
            return psum.tile(shape, F32, name=f"bank{bank_of[tenant]}")

        slot_tokens = keep.tile([P, E * C // PER_COL], U16, name="slot_tokens")
        token_slots = [keep.tile([P, T // PER_COL], U16, name=f"token_slots{s}") for s in (FIRST, SECOND)]
        dy_w = keep.tile([P, T], I32, name="dy_w", align_bytes=64)
        dy_s = keep.tile([P, T], U8, name="dy_s", align_bytes=64)
        w2_first = keep.tile([P, 1, 2 * H], U8, name="w2_first", align_bytes=64)
        w2_rest = keep.tile([P, E - 1, 2 * H], U8, name="w2_rest", align_bytes=64)
        w2_s = keep.tile([P, E, H], U8, name="w2_s", align_bytes=64)
        w1_s = keep.tile([P, K], U8, name="w1_s", align_bytes=64)
        w1_w = keep.tile([P, 2 * K], U8, name="w1_w", align_bytes=64)
        gates = {}
        for s, pieces in enumerate(GATE_PIECES):
            for piece in pieces:
                tile = keep.tile([P, len(piece) * P], F32, name=f"gate{s}_{piece.start}", align_bytes=64)
                for b in piece:
                    gates[s, b] = (tile, piece.start)
        last_gate = keep.tile([P, 2, len(LAST) * P], F32, name="last_gate", align_bytes=64)
        ident = keep.tile([P, P], F32, name="ident")

        def gate_of(s, tiles):
            tile, base = gates[s, tiles.start]
            return tile[:, (tiles.start - base) * P : (tiles.stop - base) * P]

        nc.vector.memset(w2_s[:].bitcast(I32), 0)
        nc.vector.memset(w1_s[:].bitcast(I32), 0)
        make_identity(nc, ident[:])

        w2_rows = w2t_scales[:, 0].rearrange("e (q j) i -> j q e i", j=SCALE_ROWS)
        w1_rows = w1t_scales[0].rearrange("(q j) k -> j q k", j=SCALE_ROWS)
        a_rows = a.rearrange("(r q) t -> q r t", q=P)
        a_sb = {}

        def load_a(first, stop):
            piece = keep.tile([P, ROW_BLOCKS, (stop - first) * P], F32, name=f"a_sb{first}")
            nc.sync.dma_start(piece[:], a_rows[:, :, first * P : stop * P])
            for b in range(first, stop):
                a_sb[b] = piece[:, :, (b - first) * P : (b - first + 1) * P]

        nc.sync.dma_start(slot_tokens[:], offs)
        for q in range(P // QUADRANT):
            rows = dy_scales[0, SCALE_ROWS * q : SCALE_ROWS * (q + 1), :].bitcast(I32)
            (nc.sync if q < 2 else nc.scalar).dma_start(
                dy_s[QUADRANT * q : QUADRANT * (q + 1), :].bitcast(I32),
                rows.unsqueeze(0).to_broadcast([QUADRANT // SCALE_ROWS, SCALE_ROWS, T // 4]),
            )
        for b in EARLY[:2]:
            load_a(b, b + 1)
        nc.sync.dma_start(dy_w[:], dy_words[0].rearrange("p t d -> p (t d)").bitcast(I32))
        load_a(EARLY[2], EARLY[2] + 1)
        nc.sync.dma_start(w2_first[:].bitcast(I32), w2t_words[0:1, 0].rearrange("e p b -> p e b").bitcast(I32))
        for j in range(SCALE_ROWS):
            nc.sync.dma_start(w2_s[j:P:QUADRANT, :, :].bitcast(I32), w2_rows[j].bitcast(I32))
        nc.sync.dma_start(w2_rest[:].bitcast(I32), w2t_words[1:E, 0].rearrange("e p b -> p e b").bitcast(I32))
        load_a(3, LAST.start)
        load_a(LAST.start, LAST.stop)

        def load_gate(s, first):
            tile = gates[s, first][0]
            nc.sync.dma_start(tile[:], gate[s, :, first * P : first * P + tile.shape[1]])

        for s, lst in enumerate((pos1, pos2)):
            nc.sync.dma_start(token_slots[s][:], lst)
        load_gate(FIRST, 0)
        load_gate(SECOND, 0)
        load_gate(FIRST, MIDDLE.start)
        load_gate(SECOND, LAST.start)
        load_gate(SECOND, 3)
        nc.sync.dma_start(last_gate[:], gate[FIRST, :, LAST.start * P :].unsqueeze(1).to_broadcast(last_gate.shape))
        for j in range(SCALE_ROWS):
            nc.sync.dma_start(w1_s[j:P:QUADRANT, :].bitcast(I32), w1_rows[j].bitcast(I32))
        for b in MIDDLE:
            load_gate(SECOND, b)
        nc.sync.dma_start(w1_w[:].bitcast(I32), w1t_words[0].bitcast(I32))

        def block_columns(tile, r):
            return tile[:].rearrange("t (u r q d) -> t r q u d", u=2, r=ROW_BLOCKS, d=2)[:, r]

        a_turned, silus, tanhs, slopes = {}, {}, {}, {}

        def turn_a(b, after=None):
            a_turned[b] = bank(("a", b), [P, H], after)
            for r in ALL_ROWS:
                nc.tensor.transpose(block_columns(a_turned[b], r), a_sb[b][:, r, :], ident[:])

        def silu(b, place=None):
            silus[b] = keep.tile([P, H], F32, name=place or f"silu{b}", align_bytes=64)
            nc.scalar.activation(silus[b][:], a_turned[b][:], ACT.Silu, scale=-1.0)

        def tanh(b, into=None):
            tanhs[b] = keep.tile([P, H], F32, name=f"tanh{b}", align_bytes=64)[:] if into is None else into
            nc.scalar.activation(tanhs[b], a_turned[b][:], ACT.Tanh, scale=-0.5)

        def activate(b):
            silu(b)
            tanh(b)

        for b in EARLY:
            turn_a(b)
            both = keep.tile([P, 2, H], F32, name=f"factors{b}", align_bytes=64)
            nc.scalar.activation(both[:, 0, :], a_turned[b][:], ACT.Silu, scale=-1.0)
            nc.scalar.activation(both[:, 1, :], a_turned[b][:], ACT.Tanh, scale=-0.5)
            nc.gpsimd.tensor_scalar(both[:], both[:], 1.0, -1.0, ALU.mult, ALU.add)
            slopes[b] = keep.tile([P, H], F32, name=f"slope{b}", align_bytes=64)
            nc.gpsimd.tensor_tensor(slopes[b][:], both[:, 0, :], both[:, 1, :], ALU.mult)

        y = [keep.tile([P, E * C], F32, name=f"y{r}") for r in ALL_ROWS]
        g_s, g_w = {}, {}

        def gather_slots(e):
            slots = slot_tokens[:, e * C // PER_COL : (e + 1) * C // PER_COL]
            g_s[e] = keep.tile([P, C], U8, name=f"g_s{e % 2}", align_bytes=64)
            g_w[e] = keep.tile([P, C], U32, name=f"g_w{e}", align_bytes=64)
            nc.vector.tensor_copy(g_s[e][:], dy_s[:].indirect(slots))
            nc.vector.tensor_copy(g_w[e][:], dy_w[:].bitcast(U32).indirect(slots))

        def expert_pass(e, r):
            words = w2_first[:, 0, :] if e == 0 else w2_rest[:, e - 1, :]
            sums = bank(("y", e, r), [P, C])
            nc.tensor.matmul_mx(
                sums[:],
                lhsT=words[:, 2 * P * r : 2 * P * (r + 1)].bitcast(E2M1),
                lhsT_scale=w2_s[:, e, P * r : P * (r + 1)],
                rhs=g_w[e][:].bitcast(E5M2),
                rhs_scale=g_s[e][:],
                start=True,
                stop=True,
            )
            if (e, r) in ON_VECTOR:
                nc.vector.tensor_copy(y[r][:, e * C : (e + 1) * C], sums[:])
            else:
                nc.scalar.copy(y[r][:, e * C : (e + 1) * C], sums[:])

        for e in range(E):
            gather_slots(e)
            for r in ALL_ROWS:
                expert_pass(e, r)

        out_rows = out.rearrange("(kb p) t -> p kb t", p=P)
        picked = {}
        block = {}
        dh_t, da_t = {}, {}
        turned = {}
        back, da, codes, scales = {}, {}, {}, {}

        def entries(s, tiles):
            return token_slots[s][:, tiles.start * P // PER_COL : tiles.stop * P // PER_COL]

        def note_blocks(s, tiles, rows, columns):
            for n, r in enumerate(rows):
                for b in tiles:
                    block[s, b, r] = columns[:, n, (b - tiles.start) * P : (b - tiles.start + 1) * P]

        def room(place, tiles, rows):
            return keep.tile([P, len(rows), len(tiles) * P], F32, name=place, align_bytes=64)

        def gather_gated(s, r, place):
            tiles, rows = VECTOR_TILES[s], ALL_ROWS[r : r + 1]
            columns = room(place, tiles, rows)
            nc.vector.tensor_tensor(columns[:, 0, :], y[r][:].indirect(entries(s, tiles)), gate_of(s, tiles), ALU.mult)
            note_blocks(s, tiles, rows, columns)
            turn(s, tiles, rows)

        def gather_plain(s, tiles, rows=ALL_ROWS):
            tile = room(f"picked{s}_{tiles.start}_{rows.start}", tiles, rows)
            for n, r in enumerate(rows):
                nc.scalar.activation(tile[:, n, :], y[r][:].indirect(entries(s, tiles)), ACT.Copy)
                for b in tiles:
                    picked[s, b, r] = (tile, tiles.start, rows.start)

        def apply_gate(s, tiles, rows=ALL_ROWS, engine=nc.vector, into=None, wide=None):
            tile, first, top = picked[s, tiles.start, rows.start]
            plain = tile[:, rows.start - top : rows.stop - top, (tiles.start - first) * P : (tiles.stop - first) * P]
            if wide is None:
                wide = gate_of(s, tiles).unsqueeze(1).to_broadcast(plain.shape)
            gated = plain if into is None else into
            engine.tensor_tensor(gated, plain, wide, ALU.mult)
            note_blocks(s, tiles, rows, gated)

        def gate_and_turn(s, b):
            apply_gate(s, range(b, b + 1))
            turn(s, range(b, b + 1))

        def open_dh(b, after):
            dh_t[b] = bank(("dh", b), [P, H], after)

        def turn(s, tiles, rows=ALL_ROWS):
            for b in tiles:
                for r in rows:
                    done = turned.get(b, 0)
                    nc.tensor.matmul(
                        block_columns(dh_t[b], r),
                        lhsT=block[s, b, r],
                        rhs=ident[:],
                        start=(done == 0),
                        stop=(done == 2 * ROW_BLOCKS - 1),
                        is_transpose=True,
                    )
                    turned[b] = done + 1

        def first_factor(b):
            nc.vector.scalar_tensor_tensor(silus[b][:], silus[b][:], 1.0, dh_t[b][:], ALU.subtract, ALU.mult)

        def product(b):
            da_t[b] = keep.tile([P, H], BF16, name=f"da_t{b}", align_bytes=64)
            if b in EARLY:
                nc.vector.tensor_tensor(da_t[b][:], slopes[b][:], dh_t[b][:], ALU.mult)
            else:
                nc.vector.scalar_tensor_tensor(da_t[b][:], tanhs[b], 1.0, silus[b][:], ALU.subtract, ALU.mult)

        def turn_back(c, after):
            back[c] = bank(("back", c), [P, len(CHUNKS[c]), 2, P], after)
            for n, b in enumerate(CHUNKS[c]):
                pairs = da_t[b][:].bitcast(F32)
                for u in range(2):
                    nc.tensor.transpose(back[c][:, n, u, :], pairs[:, u * P : (u + 1) * P], ident[:])

        def weave(c):
            da[c] = keep.tile([P, len(CHUNKS[c]) * P * PACK], BF16, name=f"da{c}", align_bytes=64)
            nc.scalar.copy(
                da[c][:].bitcast(F32).rearrange("p (b t u) -> p b t u", t=P, u=2),
                back[c][:].rearrange("p b u t -> p b t u"),
            )

        def quantise(c):
            width = len(CHUNKS[c]) * P
            codes[c] = keep.tile([P, width], U32, name=f"codes{c}", align_bytes=64)
            scales[c] = keep.tile([P, width], U8, name=f"scales{c}", align_bytes=64)
            nc.vector.quantize_mx(codes[c][:].bitcast(E5M2), scales[c][:], da[c][:])

        def finish(c, after, on_vector=False):
            tokens = slice(CHUNKS[c].start * P, CHUNKS[c].stop * P)
            width = len(CHUNKS[c]) * P
            sums = bank(("out", c), [P, K // P, width], after)
            for kb in range(K // P):
                nc.tensor.matmul_mx(
                    sums[:, kb, :],
                    lhsT=w1_w[:, 2 * P * kb : 2 * P * (kb + 1)].bitcast(E2M1),
                    lhsT_scale=w1_s[:, P * kb : P * (kb + 1)],
                    rhs=codes[c][:].bitcast(E5M2),
                    rhs_scale=scales[c][:],
                    start=True,
                    stop=True,
                )
            res = keep.tile([P, K // P, width], F32, name=f"res{c}", align_bytes=64)
            if on_vector:
                nc.vector.tensor_scalar(res[:], sums[:], 0.5, None, ALU.mult)
            else:
                nc.scalar.activation(res[:], sums[:], ACT.Copy, scale=0.5)
            nc.sync.dma_start(out_rows[:, :, tokens], res[:])

        for b, tenant in zip(range(3, 7), ((2, 2), (2, 3), (3, 2), (3, 3))):
            turn_a(b, after=("y",) + tenant)
        for b, tenant in enumerate(ON_VECTOR):
            open_dh(b, after=("y",) + tenant)

        gather_plain(SECOND, range(3, LAST.start))
        activate(3)
        open_dh(4, after=("a", 3))
        gather_plain(FIRST, MIDDLE)
        activate(4)
        open_dh(5, after=("a", 4))
        gather_plain(FIRST, LAST, ALL_ROWS[:2])
        gather_plain(FIRST, LAST, ALL_ROWS[2:])
        silu(5)
        gather_plain(SECOND, LAST)
        tanh(5)

        gather_gated(SECOND, 0, "g_w3")
        gather_gated(FIRST, 0, "g_w2")
        gather_gated(SECOND, 1, "g_w0")
        gather_gated(FIRST, 1, f"factors{EARLY[-1]}")
        gather_gated(SECOND, 2, "seconds2")
        gate_and_turn(SECOND, 3)
        gate_and_turn(SECOND, 4)
        gather_gated(FIRST, 2, "gate1_3")
        gather_gated(SECOND, 3, "gate1_4")
        gate_and_turn(SECOND, 5)
        gather_gated(FIRST, 3, "gate1_0")
        apply_gate(FIRST, MIDDLE, ALL_ROWS[:3])
        turn(FIRST, MIDDLE[::-1], ALL_ROWS[:3])

        width = len(LAST) * P
        late = room("gate0_0", range(5 * len(LAST)), ONE_ROW)
        apply_gate(FIRST, MIDDLE, ALL_ROWS[3:], engine=nc.gpsimd, into=late[:, :, :width])
        turn(FIRST, MIDDLE[::-1], ALL_ROWS[3:])
        for n, rows in enumerate((ALL_ROWS[:2], ALL_ROWS[2:])):
            part = late[:, 0, (1 + 2 * n) * width : (3 + 2 * n) * width].rearrange("p (r t) -> p r t", r=2)
            apply_gate(FIRST, LAST, rows, engine=nc.gpsimd, into=part, wide=last_gate[:])

        product(0)
        turn_a(7, after=("dh", 0))
        product(1)
        product(2)
        first_factor(3)
        turn_back(0, after=("dh", 3))
        first_factor(5)
        first_factor(4)

        silu(6)
        weave(0)
        silu(7, place="da_t1")
        open_dh(6, after=("dh", 1))
        open_dh(7, after=("dh", 2))
        turn(FIRST, LAST)
        product(3)
        turn_back(1, after=("dh", 5))
        product(4)
        for b in LAST:
            gate_and_turn(SECOND, b)
        weave(1)
        last_tanhs = keep.tile([P, len(LAST), H], F32, name="da_t3", align_bytes=64)
        for n, b in enumerate(LAST):
            tanh(b, into=last_tanhs[:, n, :])

        product(5)
        turn_back(2, after=("dh", 4))
        quantise(0)
        finish(0, after=("back", 0))
        first_factor(6)
        quantise(1)
        finish(1, after=("a", 5))
        first_factor(7)
        weave(2)
        product(6)
        turn_back(3, after=("back", 1))
        product(7)
        turn_back(4, after=("dh", 6))
        quantise(2)
        weave(3)
        weave(4)
        quantise(3)
        quantise(4)
        finish(2, after=("a", 6))
        finish(3, after=("a", 7), on_vector=True)
        finish(4, after=("dh", 7))
